import numpy as np
import ml_dtypes


def mxq(x, axis, fmt="e4m3"):
    dtype, down = {"e4m3": (ml_dtypes.float8_e4m3fn, 7), "e5m2": (ml_dtypes.float8_e5m2, 14)}[fmt]
    v = np.moveaxis(np.asarray(x, np.float32).astype(ml_dtypes.bfloat16).astype(np.float64), axis, -1)
    blocks = v.reshape(v.shape[:-1] + (-1, 32))
    amax = np.abs(blocks).max(-1, keepdims=True)
    byte = np.maximum(np.where(amax > 0, np.frexp(amax)[1] - 1 + 127, 0) - down, 1)
    scale = np.exp2(byte - 127.0)
    codes = (blocks / scale).astype(np.float32).astype(dtype).astype(np.float64)
    return np.moveaxis((codes * scale).reshape(v.shape), -1, axis)


WIDE = False


def mx_kscale(k):
    if not WIDE:
        return np.ones(k)
    levels = np.array([18, -18])
    if k % 512:
        return np.exp2(np.random.permutation(np.resize(levels, k // 32))).repeat(32)
    a = np.empty((k // 512, 16))
    for p in range(k // 512):
        a[p, :8] = np.random.permutation(np.resize(levels, 8))
        for g in range(8):
            far = levels[np.abs(levels - a[p, g]) >= 10]
            a[p, g + 8] = far[np.random.randint(len(far))]
    return np.exp2(a.ravel()).repeat(32)


def f64(x):
    return np.asarray(x).astype(np.float64)


def striped(idx):
    return np.tile(np.asarray(idx).reshape(-1, 16).T, (8, 1)).astype(np.uint16)


def unstriped(offs):
    return offs[:16].T.reshape(-1).astype(np.int64)


B, N, T, D, R = 2, 512, 2048, 512, 512


def setup_inputs():
    n = np.random.standard_normal
    idx = np.random.permutation(T)[:B * N]
    s = mx_kscale(D)[:, None]
    z = mx_kscale(R)[:, None]
    x = n((B, D, R))
    return {
        "xT": (x * s).astype(np.float32),
        "wT": (n((D, T)) * (1.00 / np.sqrt(D)) / s).astype(np.float32),
        "vT": (n((D, T)) / np.sqrt(D) / s).astype(np.float32),
        "y": n((B, R, N)).astype(np.float32),
        "wt": (np.random.uniform(0.5, 1.5, (B, R, 1)) * 1.0 / np.sqrt(R) * z).astype(np.float32),
        "xm": (x.transpose(0, 2, 1) / z).astype(np.float32),
        "offs": striped(idx),
    }


def reference(xT, wT, vT, y, wt, xm, offs):
    idx = unstriped(offs)
    pick = lambda x: x[:, idx].reshape(x.shape[0], B, N).transpose(1, 0, 2)
    xq = mxq(f64(xT), 1, "e4m3").transpose(0, 2, 1)
    a = xq @ mxq(pick(f64(wT)), 1, "e4m3")
    av = xq @ mxq(pick(f64(vT)), 1, "e4m3")
    q = a - f64(y)
    g = f64(wt) * av / (1.0 + q * q)
    dw = mxq(f64(xm), 1, "e4m3").transpose(0, 2, 1) @ mxq(g, 1, "e5m2")
    gw = np.zeros((D, T))
    gw[:, idx] = dw.transpose(1, 0, 2).reshape(D, B * N)
    return gw

@@ -1,0 +1,299 @@
+from contextlib import ExitStack
+
+import concourse.mybir as mybir
+
+B, N, T, D, R = 2, 512, 2048, 512, 512
+P = 128
+FLOPS = 3 * 2 * B * N * D * R
+
+F32 = mybir.dt.float32
+BF16 = mybir.dt.bfloat16
+U32 = mybir.dt.uint32
+U16 = mybir.dt.uint16
+U8 = mybir.dt.uint8
+E4M3 = mybir.dt.float8_e4m3fn_x4
+E5M2 = mybir.dt.float8_e5m2_x4
+ACT = mybir.ActivationFunctionType
+ALU = mybir.AluOpType
+COLS = N // 16
+
+
+def tile_attend_ghv_cau_kernel(tc, xT, wT, vT, y, wt, xm, offs, out):
+    nc = tc.nc
+    with ExitStack() as ctx:
+        held = ctx.enter_context(tc.tile_pool(name="held", bufs=1))
+        keep = ctx.enter_context(tc.tile_pool(name="keep", bufs=1))
+        stage = ctx.enter_context(tc.tile_pool(name="stage", bufs=5))
+        rawp = ctx.enter_context(tc.tile_pool(name="rawp", bufs=6))
+        dwp = ctx.enter_context(tc.tile_pool(name="dwp", bufs=4))
+        ps_a = ctx.enter_context(tc.psum_pool(name="ps_a", bufs=3))
+        ps_av = ctx.enter_context(tc.psum_pool(name="ps_av", bufs=3))
+        ps_dw = ctx.enter_context(tc.psum_pool(name="ps_dw", bufs=2))
+
+        offsets = held.tile([P, B * COLS], U16, name="offsets")
+        nc.sync.dma_start(offsets[:], offs)
+
+        def listed(b):
+            return offsets[:, b * COLS:(b + 1) * COLS]
+
+        def move(eng, dst, src):
+            if eng == "s":
+                nc.scalar.activation(dst, src, ACT.Copy)
+            elif eng == "g":
+                nc.gpsimd.tensor_scalar(dst, src, 1.0, 0.0, ALU.mult, ALU.add)
+            else:
+                nc.vector.tensor_copy(dst, src)
+
+        def quantise(name, src, fmt):
+            codes = keep.tile([P, 512], U32, name=name + "_codes", align_bytes=64)
+            scales = keep.tile([P, 512], U8, name=name + "_scales", align_bytes=64)
+            nc.vector.quantize_mx(out=codes[:].bitcast(fmt), scales=scales[:], in_=src[:])
+            return codes, scales
+
+        warm = keep.tile([P, 1], F32, name="warm")
+        nc.vector.memset(warm[:], 1.0)
+        nc.scalar.activation(warm[:], warm[:], ACT.Abs_reciprocal_sqrt)
+
+        windows = [keep.tile([P, T], F32, name=f"window{j}") for j in range(4)]
+
+        def zero(j, eng):
+            (nc.vector if eng == "v" else nc.gpsimd).memset(windows[j][:], 0.0)
+
+        tables = {"w": wT.rearrange("(p t) n -> p t n", t=4), "v": vT.rearrange("(p t) n -> p t n", t=4)}
+        raw, pairs, gath, staged, y_sb = {}, {}, {}, {}, {}
+        wq, vq, xq, xmq, gq, g_bf = {}, {}, {}, {}, {}, {}
+        quantised = {"w": wq, "v": vq, "x": xq, "xm": xmq, "g": gq}
+        wt_sb = keep.tile([P, B, 4], F32, name="wt_sb")
+
+        def load_chunk(tab, u, h):
+            raw[tab, u, h] = rawp.tile([P, 2, 512], F32, name="chunk")
+            nc.sync.dma_start(raw[tab, u, h][:], tables[tab][:, 2 * u:2 * u + 2, h * 512:(h + 1) * 512])
+
+        def load_plane(tab, t):
+            raw[tab, t] = keep.tile([P, T], F32, name=f"plane_{tab}{t}")
+            nc.sync.dma_start(raw[tab, t][:], tables[tab][:, t, :])
+
+        def load_half(nm, b, h):
+            src = {"x": xT, "xm": xm}[nm][b].rearrange("(p j) r -> p j r", j=4)
+            raw[nm, b, h] = keep.tile([P, 4, 256], F32, name=f"raw_{nm}{b}{h}")
+            nc.sync.dma_start(raw[nm, b, h][:], src[:, :, h * 256:(h + 1) * 256])
+
+        def load_y(b, t):
+            if b not in y_sb:
+                y_sb[b] = keep.tile([P, 4, N], F32, name=f"y_sb{b}")
+            nc.sync.dma_start(y_sb[b][:, t:t + 2, :], y[b].rearrange("(p t) n -> p t n", t=4)[:, t:t + 2, :])
+
+        def load_wt():
+            nc.sync.dma_start(wt_sb[:], wt.rearrange("b (p t) o -> p b (t o)", t=4))
+
+        def cast(tab, u, h, eng):
+            if (tab, u) not in pairs:
+                pairs[tab, u] = keep.tile([P, 2 * T], BF16, name=f"pairs_{tab}{u}")
+            dst = pairs[tab, u][:, 1024 * h:1024 * (h + 1)].rearrange("p (c i e) -> p c e i", i=4, e=2)
+            move(eng, dst, raw[tab, u, h][:].rearrange("p e (c i) -> p c e i", i=4))
+
+        def gpair(tab, u, b):
+            if (tab, b) not in gath:
+                gath[tab, b] = keep.tile([P, 2, 2 * N], BF16, name=f"gath_{tab}{b}")
+            nc.vector.tensor_copy(gath[tab, b][:, u, :].bitcast(U32), pairs[tab, u][:].bitcast(U32).indirect(listed(b)))
+
+        def gplane(tab, t, b):
+            if (tab, b) not in gath:
+                gath[tab, b] = keep.tile([P, 4, N], F32, name=f"gath_{tab}{b}")
+            nc.vector.tensor_copy(gath[tab, b][:, t, :], raw[tab, t][:].indirect(listed(b)))
+
+        def stage_of(nm, b):
+            if (nm, b) not in staged:
+                staged[nm, b] = stage.tile([P, 4 * N], BF16, name="stage", align_bytes=64)
+                quantised[nm][b] = staged[nm, b]
+            return staged[nm, b]
+
+        def ppair(tab, b, eng):
+            dst = stage_of(tab, b)[:].rearrange("p (n u e) -> p n u e", u=2, e=2)
+            src = gath[tab, b][:].rearrange("p u (n e) -> p n u e", e=2)
+            if eng == "s":
+                nc.scalar.copy(dst, src)
+            else:
+                nc.vector.tensor_copy(dst, src)
+
+        def il(nm, b, h, eng):
+            st = stage_of(nm, b)
+            if nm == "x":
+                dst = st[:].rearrange("p (t m j) -> p m j t", t=4, j=4)[:, 64 * h:64 * (h + 1)]
+                move(eng, dst, raw[nm, b, h][:].rearrange("p j (m t) -> p m j t", t=4))
+            else:
+                src = raw[nm, b, h][:] if nm == "xm" else gath[nm, b][:, :, 256 * h:256 * (h + 1)]
+                dst = st[:, 1024 * h:1024 * (h + 1)].rearrange("p (c i t) -> p c t i", i=4, t=4)
+                move(eng, dst, src.rearrange("p t (c i) -> p c t i", i=4))
+
+        def quant(d, key, name, fmt=E4M3):
+            d[key] = quantise(name, d[key], fmt)
+
+        def residual(b, t):
+            bank = ps_a.tile([P, N], F32, name="a_bank")
+            cols = slice(t * P, (t + 1) * P)
+            nc.tensor.matmul_mx(out=bank[:], lhsT=xq[b][0][:, cols].bitcast(E4M3), lhsT_scale=xq[b][1][:, cols],
+                                rhs=wq[b][0][:].bitcast(E4M3), rhs_scale=wq[b][1][:], start=True, stop=True)
+            nc.vector.tensor_tensor(y_sb[b][:, t, :], bank[:], y_sb[b][:, t, :], ALU.subtract)
+
+        def weight(b, t, eng):
+            z = y_sb[b][:, t, :]
+            nc.scalar.activation(z, z, ACT.Square)
+            nc.scalar.activation(z, z, ACT.Abs_reciprocal_sqrt, bias=1.0)
+            if eng == "vv":
+                nc.vector.scalar_tensor_tensor(z, z, wt_sb[:, b, t:t + 1], z, ALU.mult, ALU.mult)
+                return
+            nc.scalar.activation(z, z, ACT.Square)
+            if eng == "s":
+                nc.scalar.activation(z, z, ACT.Copy, scale=wt_sb[:, b, t:t + 1])
+            elif eng == "g":
+                nc.gpsimd.tensor_scalar(z, z, wt_sb[:, b, t:t + 1], 0.0, ALU.mult, ALU.add)
+            else:
+                nc.vector.tensor_scalar(z, z, wt_sb[:, b, t:t + 1], None, ALU.mult)
+
+        def grad(b, c):
+            if b not in g_bf:
+                g_bf[b] = stage_of("g", b)
+            bank = ps_av.tile([P, 4, P], F32, name="av_bank")
+            items = slice(c * P, (c + 1) * P)
+            for t in range(4):
+                cols = slice(t * P, (t + 1) * P)
+                nc.tensor.matmul_mx(out=bank[:, t, :], lhsT=xq[b][0][:, cols].bitcast(E4M3), lhsT_scale=xq[b][1][:, cols],
+                                    rhs=vq[b][0][:, items].bitcast(E4M3), rhs_scale=vq[b][1][:, items], start=True, stop=True)
+            dst = g_bf[b][:, 4 * c * P:4 * (c + 1) * P].rearrange("p (c i t) -> p c t i", i=4, t=4)
+            nc.vector.tensor_tensor(dst, bank[:].rearrange("p t (c i) -> p c t i", i=4),
+                                    y_sb[b][:, :, items].rearrange("p t (c i) -> p c t i", i=4), ALU.mult)
+
+        dw = {}
+
+        def product(b, j):
+            bank = ps_dw.tile([P, N], F32, name="dw_bank")
+            cols = slice(j * P, (j + 1) * P)
+            nc.tensor.matmul_mx(out=bank[:], lhsT=xmq[b][0][:, cols].bitcast(E4M3), lhsT_scale=xmq[b][1][:, cols],
+                                rhs=gq[b][0][:].bitcast(E5M2), rhs_scale=gq[b][1][:], start=True, stop=True)
+            dw[b, j] = dwp.tile([P, N], F32, name="dw")
+            nc.scalar.activation(dw[b, j][:], bank[:], ACT.Copy)
+
+        def scatter(b, j):
+            nc.vector.tensor_copy(windows[j][:].indirect(listed(b)), dw[b, j][:])
+
+        def store(j):
+            nc.sync.dma_start(out[j * P:(j + 1) * P, :], windows[j][:])
+
+        zero(0, "v")
+        zero(1, "v")
+        zero(2, "g")
+        zero(3, "g")
+        load_chunk("w", 1, 3)
+        load_chunk("w", 1, 0)
+        load_chunk("w", 1, 2)
+        load_chunk("w", 1, 1)
+        load_chunk("w", 0, 2)
+        cast("w", 1, 3, "s")
+        load_chunk("w", 0, 0)
+        load_chunk("w", 0, 1)
+        load_chunk("w", 0, 3)
+        cast("w", 1, 1, "s")
+        cast("w", 1, 0, "v")
+        cast("w", 0, 2, "s")
+        load_half("x", 0, 0)
+        load_wt()
+        load_plane("v", 2)
+        il("x", 0, 0, "s")
+        cast("w", 0, 3, "v")
+        load_half("x", 0, 1)
+        cast("w", 1, 2, "v")
+        cast("w", 0, 1, "s")
+        gpair("w", 1, 0)
+        load_y(0, 0)
+        cast("w", 0, 0, "s")
+        load_half("x", 1, 0)
+        gpair("w", 0, 0)
+        load_half("x", 1, 1)
+        il("x", 1, 0, "s")
+        il("x", 0, 1, "s")
+        load_y(0, 2)
+        gpair("w", 1, 1)
+        quant(quantised["x"], 0, "x0")
+        load_plane("v", 3)
+        load_plane("v", 0)
+        ppair("w", 0, "s")
+        load_plane("v", 1)
+        load_half("xm", 1, 0)
+        gplane("v", 0, 0)
+        quant(quantised["w"], 0, "w0")
+        residual(0, 0)
+        gplane("v", 3, 0)
+        gplane("v", 2, 0)
+        gplane("v", 1, 0)
+        il("v", 0, 1, "s")
+        residual(0, 2)
+        il("x", 1, 1, "s")
+        gplane("v", 2, 1)
+        residual(0, 1)
+        weight(0, 1, "v")
+        load_half("xm", 0, 0)
+        load_y(1, 2)
+        residual(0, 3)
+        weight(0, 2, "v")
+        gpair("w", 0, 1)
+        load_half("xm", 1, 1)
+        load_half("xm", 0, 1)
+        weight(0, 0, "s")
+        ppair("w", 1, "s")
+        il("xm", 0, 1, "s")
+        il("v", 0, 0, "s")
+        quant(quantised["v"], 0, "v0")
+        weight(0, 3, "s")
+        gplane("v", 0, 1)
+        il("xm", 0, 0, "s")
+        grad(0, 1)
+        quant(quantised["x"], 1, "x1")
+        grad(0, 2)
+        load_y(1, 0)
+        quant(quantised["w"], 1, "w1")
+        residual(1, 2)
+        gplane("v", 1, 1)
+        grad(0, 3)
+        grad(0, 0)
+        quant(quantised["xm"], 0, "xm0")
+        quant(quantised["g"], 0, "g0", E5M2)
+        product(0, 1)
+        gplane("v", 3, 1)
+        il("v", 1, 1, "s")
+        residual(1, 1)
+        residual(1, 3)
+        product(0, 0)
+        il("v", 1, 0, "s")
+        weight(1, 2, "s")
+        quant(quantised["v"], 1, "v1")
+        scatter(0, 1)
+        weight(1, 3, "s")
+        product(0, 2)
+        residual(1, 0)
+        scatter(0, 0)
+        weight(1, 0, "s")
+        weight(1, 1, "s")
+        grad(1, 1)
+        il("xm", 1, 0, "s")
+        grad(1, 3)
+        grad(1, 2)
+        scatter(0, 2)
+        grad(1, 0)
+        quant(quantised["g"], 1, "g1", E5M2)
+        il("xm", 1, 1, "s")
+        quant(quantised["xm"], 1, "xm1")
+        product(1, 2)
+        product(0, 3)
+        scatter(0, 3)
+        scatter(1, 2)
+        store(2)
+        product(1, 0)
+        product(1, 1)
+        product(1, 3)
+        scatter(1, 0)
+        store(0)
+        scatter(1, 3)
+        store(3)
+        scatter(1, 1)
+        store(1)

@@ -24,11 +24,9 @@ def tile_attend_ghv_cau_kernel(tc, xT, wT, vT, y, wt, xm, offs, out):
         held = ctx.enter_context(tc.tile_pool(name="held", bufs=1))
         keep = ctx.enter_context(tc.tile_pool(name="keep", bufs=1))
         stage = ctx.enter_context(tc.tile_pool(name="stage", bufs=5))
-        rawp = ctx.enter_context(tc.tile_pool(name="rawp", bufs=6))
+        rawp = ctx.enter_context(tc.tile_pool(name="rawp", bufs=4))
         dwp = ctx.enter_context(tc.tile_pool(name="dwp", bufs=4))
-        ps_a = ctx.enter_context(tc.psum_pool(name="ps_a", bufs=3))
-        ps_av = ctx.enter_context(tc.psum_pool(name="ps_av", bufs=3))
-        ps_dw = ctx.enter_context(tc.psum_pool(name="ps_dw", bufs=2))
+        psum = ctx.enter_context(tc.psum_pool(name="psum", bufs=1))
 
         offsets = held.tile([P, B * COLS], U16, name="offsets")
         nc.sync.dma_start(offsets[:], offs)
@@ -66,8 +64,8 @@ def tile_attend_ghv_cau_kernel(tc, xT, wT, vT, y, wt, xm, offs, out):
         wt_sb = keep.tile([P, B, 4], F32, name="wt_sb")
 
         def load_chunk(tab, u, h):
-            raw[tab, u, h] = rawp.tile([P, 2, 512], F32, name="chunk")
-            nc.sync.dma_start(raw[tab, u, h][:], tables[tab][:, 2 * u:2 * u + 2, h * 512:(h + 1) * 512])
+            raw[tab, u, h] = rawp.tile([P, 2, 1024], F32, name="chunk")
+            nc.sync.dma_start(raw[tab, u, h][:], tables[tab][:, 2 * u:2 * u + 2, h * 1024:(h + 1) * 1024])
 
         def load_plane(tab, t):
             raw[tab, t] = keep.tile([P, T], F32, name=f"plane_{tab}{t}")
@@ -75,8 +73,8 @@ def tile_attend_ghv_cau_kernel(tc, xT, wT, vT, y, wt, xm, offs, out):
 
         def load_half(nm, b, h):
             src = {"x": xT, "xm": xm}[nm][b].rearrange("(p j) r -> p j r", j=4)
-            raw[nm, b, h] = keep.tile([P, 4, 256], F32, name=f"raw_{nm}{b}{h}")
-            nc.sync.dma_start(raw[nm, b, h][:], src[:, :, h * 256:(h + 1) * 256])
+            raw[nm, b, h] = keep.tile([P, 4, 512], F32, name=f"raw_{nm}{b}{h}")
+            nc.sync.dma_start(raw[nm, b, h][:], src)
 
         def load_y(b, t):
             if b not in y_sb:
@@ -86,11 +84,11 @@ def tile_attend_ghv_cau_kernel(tc, xT, wT, vT, y, wt, xm, offs, out):
         def load_wt():
             nc.sync.dma_start(wt_sb[:], wt.rearrange("b (p t) o -> p b (t o)", t=4))
 
-        def cast(tab, u, h, eng):
+        def cast(tab, u, h, eng, lo, w):
             if (tab, u) not in pairs:
                 pairs[tab, u] = keep.tile([P, 2 * T], BF16, name=f"pairs_{tab}{u}")
-            dst = pairs[tab, u][:, 1024 * h:1024 * (h + 1)].rearrange("p (c i e) -> p c e i", i=4, e=2)
-            move(eng, dst, raw[tab, u, h][:].rearrange("p e (c i) -> p c e i", i=4))
+            dst = pairs[tab, u][:, 2 * (1024 * h + lo):2 * (1024 * h + lo + w)].rearrange("p (c i e) -> p c e i", i=4, e=2)
+            move(eng, dst, raw[tab, u, h][:, :, lo:lo + w].rearrange("p e (c i) -> p c e i", i=4))
 
         def gpair(tab, u, b):
             if (tab, b) not in gath:
@@ -116,21 +114,24 @@ def tile_attend_ghv_cau_kernel(tc, xT, wT, vT, y, wt, xm, offs, out):
             else:
                 nc.vector.tensor_copy(dst, src)
 
-        def il(nm, b, h, eng):
+        def il(nm, b, eng, lo, w):
             st = stage_of(nm, b)
             if nm == "x":
-                dst = st[:].rearrange("p (t m j) -> p m j t", t=4, j=4)[:, 64 * h:64 * (h + 1)]
-                move(eng, dst, raw[nm, b, h][:].rearrange("p j (m t) -> p m j t", t=4))
+                dst = st[:].rearrange("p (t m j) -> p m j t", t=4, j=4)[:, lo // 4:(lo + w) // 4]
+                move(eng, dst, raw[nm, b, 0][:, :, lo:lo + w].rearrange("p j (m t) -> p m j t", t=4))
             else:
-                src = raw[nm, b, h][:] if nm == "xm" else gath[nm, b][:, :, 256 * h:256 * (h + 1)]
-                dst = st[:, 1024 * h:1024 * (h + 1)].rearrange("p (c i t) -> p c t i", i=4, t=4)
+                src = (raw[nm, b, 0] if nm == "xm" else gath[nm, b])[:, :, lo:lo + w]
+                if eng == "g":
+                    move(eng, st[:, 4 * lo:4 * (lo + w)].rearrange("p (n t) -> p n t", t=4), src.rearrange("p t n -> p n t"))
+                    return
+                dst = st[:, 4 * lo:4 * (lo + w)].rearrange("p (c i t) -> p c t i", i=4, t=4)
                 move(eng, dst, src.rearrange("p t (c i) -> p c t i", i=4))
 
         def quant(d, key, name, fmt=E4M3):
             d[key] = quantise(name, d[key], fmt)
 
-        def residual(b, t):
-            bank = ps_a.tile([P, N], F32, name="a_bank")
+        def residual(b, t, k):
+            bank = psum.tile([P, N], F32, name=f"bank{k}")
             cols = slice(t * P, (t + 1) * P)
             nc.tensor.matmul_mx(out=bank[:], lhsT=xq[b][0][:, cols].bitcast(E4M3), lhsT_scale=xq[b][1][:, cols],
                                 rhs=wq[b][0][:].bitcast(E4M3), rhs_scale=wq[b][1][:], start=True, stop=True)
@@ -151,10 +152,10 @@ def tile_attend_ghv_cau_kernel(tc, xT, wT, vT, y, wt, xm, offs, out):
             else:
                 nc.vector.tensor_scalar(z, z, wt_sb[:, b, t:t + 1], None, ALU.mult)
 
-        def grad(b, c):
+        def grad(b, c, k):
             if b not in g_bf:
                 g_bf[b] = stage_of("g", b)
-            bank = ps_av.tile([P, 4, P], F32, name="av_bank")
+            bank = psum.tile([P, 4, P], F32, name=f"bank{k}")
             items = slice(c * P, (c + 1) * P)
             for t in range(4):
                 cols = slice(t * P, (t + 1) * P)
@@ -166,8 +167,8 @@ def tile_attend_ghv_cau_kernel(tc, xT, wT, vT, y, wt, xm, offs, out):
 
         dw = {}
 
-        def product(b, j):
-            bank = ps_dw.tile([P, N], F32, name="dw_bank")
+        def product(b, j, k):
+            bank = psum.tile([P, N], F32, name=f"bank{k}")
             cols = slice(j * P, (j + 1) * P)
             nc.tensor.matmul_mx(out=bank[:], lhsT=xmq[b][0][:, cols].bitcast(E4M3), lhsT_scale=xmq[b][1][:, cols],
                                 rhs=gq[b][0][:].bitcast(E5M2), rhs_scale=gq[b][1][:], start=True, stop=True)
@@ -179,121 +180,111 @@ def tile_attend_ghv_cau_kernel(tc, xT, wT, vT, y, wt, xm, offs, out):
 
         def store(j):
             nc.sync.dma_start(out[j * P:(j + 1) * P, :], windows[j][:])
-
         zero(0, "v")
         zero(1, "v")
         zero(2, "g")
         zero(3, "g")
-        load_chunk("w", 1, 3)
-        load_chunk("w", 1, 0)
-        load_chunk("w", 1, 2)
-        load_chunk("w", 1, 1)
-        load_chunk("w", 0, 2)
-        cast("w", 1, 3, "s")
         load_chunk("w", 0, 0)
         load_chunk("w", 0, 1)
-        load_chunk("w", 0, 3)
-        cast("w", 1, 1, "s")
-        cast("w", 1, 0, "v")
-        cast("w", 0, 2, "s")
+        load_chunk("w", 1, 0)
+        load_chunk("w", 1, 1)
         load_half("x", 0, 0)
         load_wt()
-        load_plane("v", 2)
-        il("x", 0, 0, "s")
-        cast("w", 0, 3, "v")
-        load_half("x", 0, 1)
-        cast("w", 1, 2, "v")
-        cast("w", 0, 1, "s")
-        gpair("w", 1, 0)
         load_y(0, 0)
-        cast("w", 0, 0, "s")
-        load_half("x", 1, 0)
-        gpair("w", 0, 0)
-        load_half("x", 1, 1)
-        il("x", 1, 0, "s")
-        il("x", 0, 1, "s")
         load_y(0, 2)
-        gpair("w", 1, 1)
-        quant(quantised["x"], 0, "x0")
-        load_plane("v", 3)
         load_plane("v", 0)
-        ppair("w", 0, "s")
         load_plane("v", 1)
-        load_half("xm", 1, 0)
-        gplane("v", 0, 0)
-        quant(quantised["w"], 0, "w0")
-        residual(0, 0)
-        gplane("v", 3, 0)
-        gplane("v", 2, 0)
-        gplane("v", 1, 0)
-        il("v", 0, 1, "s")
-        residual(0, 2)
-        il("x", 1, 1, "s")
-        gplane("v", 2, 1)
-        residual(0, 1)
-        weight(0, 1, "v")
+        load_plane("v", 2)
+        load_plane("v", 3)
         load_half("xm", 0, 0)
-        load_y(1, 2)
-        residual(0, 3)
-        weight(0, 2, "v")
-        gpair("w", 0, 1)
-        load_half("xm", 1, 1)
-        load_half("xm", 0, 1)
-        weight(0, 0, "s")
-        ppair("w", 1, "s")
-        il("xm", 0, 1, "s")
-        il("v", 0, 0, "s")
-        quant(quantised["v"], 0, "v0")
-        weight(0, 3, "s")
-        gplane("v", 0, 1)
-        il("xm", 0, 0, "s")
-        grad(0, 1)
-        quant(quantised["x"], 1, "x1")
-        grad(0, 2)
+        load_half("x", 1, 0)
         load_y(1, 0)
-        quant(quantised["w"], 1, "w1")
-        residual(1, 2)
-        gplane("v", 1, 1)
-        grad(0, 3)
-        grad(0, 0)
+        load_y(1, 2)
+        load_half("xm", 1, 0)
+        cast("w", 0, 0, "s", 0, 1024)
+        cast("w", 0, 1, "s", 0, 384)
+        cast("w", 0, 1, "v", 384, 640)
+        cast("w", 1, 0, "s", 0, 1024)
+        cast("w", 1, 1, "s", 0, 384)
+        cast("w", 1, 1, "v", 384, 640)
+        gpair("w", 0, 0)
+        gpair("w", 1, 0)
+        il("x", 0, "s", 0, 512)
+        ppair("w", 0, "v")
+        gpair("w", 0, 1)
+        gpair("w", 1, 1)
+        quant(quantised["w"], 0, "w0")
+        quant(quantised["x"], 0, "x0")
+        residual(0, 0, 0)
+        residual(0, 1, 1)
+        residual(0, 2, 2)
+        residual(0, 3, 3)
+        ppair("w", 1, "s")
+        weight(0, 0, "g")
+        weight(0, 1, "g")
+        weight(0, 2, "g")
+        weight(0, 3, "g")
+        gplane("v", 0, 0)
+        gplane("v", 1, 0)
+        gplane("v", 2, 0)
+        gplane("v", 3, 0)
+        il("v", 0, "v", 0, 256)
+        il("v", 0, "s", 256, 256)
+        quant(quantised["v"], 0, "v0")
+        grad(0, 0, 4)
+        grad(0, 1, 5)
+        grad(0, 2, 6)
+        grad(0, 3, 7)
+        il("xm", 0, "g", 0, 128)
+        il("xm", 0, "g", 128, 128)
+        il("xm", 0, "g", 256, 128)
+        il("xm", 0, "g", 384, 128)
         quant(quantised["xm"], 0, "xm0")
         quant(quantised["g"], 0, "g0", E5M2)
-        product(0, 1)
+        product(0, 0, 0)
+        il("x", 1, "s", 0, 512)
+        quant(quantised["w"], 1, "w1")
+        quant(quantised["x"], 1, "x1")
+        residual(1, 0, 1)
+        residual(1, 1, 2)
+        residual(1, 2, 3)
+        residual(1, 3, 4)
+        product(0, 1, 4)
+        product(0, 2, 3)
+        weight(1, 0, "g")
+        weight(1, 1, "g")
+        weight(1, 2, "g")
+        weight(1, 3, "g")
+        gplane("v", 0, 1)
+        gplane("v", 1, 1)
+        gplane("v", 2, 1)
         gplane("v", 3, 1)
-        il("v", 1, 1, "s")
-        residual(1, 1)
-        residual(1, 3)
-        product(0, 0)
-        il("v", 1, 0, "s")
-        weight(1, 2, "s")
+        il("v", 1, "s", 0, 512)
         quant(quantised["v"], 1, "v1")
-        scatter(0, 1)
-        weight(1, 3, "s")
-        product(0, 2)
-        residual(1, 0)
-        scatter(0, 0)
-        weight(1, 0, "s")
-        weight(1, 1, "s")
-        grad(1, 1)
-        il("xm", 1, 0, "s")
-        grad(1, 3)
-        grad(1, 2)
-        scatter(0, 2)
-        grad(1, 0)
-        quant(quantised["g"], 1, "g1", E5M2)
-        il("xm", 1, 1, "s")
+        il("xm", 1, "g", 0, 128)
+        il("xm", 1, "g", 128, 128)
+        il("xm", 1, "g", 256, 128)
+        il("xm", 1, "g", 384, 128)
         quant(quantised["xm"], 1, "xm1")
-        product(1, 2)
-        product(0, 3)
+        grad(1, 0, 5)
+        grad(1, 1, 6)
+        grad(1, 2, 7)
+        grad(1, 3, 0)
+        quant(quantised["g"], 1, "g1", E5M2)
+        scatter(0, 0)
+        scatter(0, 1)
+        scatter(0, 2)
+        product(0, 3, 0)
         scatter(0, 3)
-        scatter(1, 2)
-        store(2)
-        product(1, 0)
-        product(1, 1)
-        product(1, 3)
+        product(1, 0, 1)
         scatter(1, 0)
         store(0)
-        scatter(1, 3)
-        store(3)
+        product(1, 1, 2)
         scatter(1, 1)
         store(1)
+        product(1, 2, 3)
+        scatter(1, 2)
+        store(2)
+        product(1, 3, 4)
+        scatter(1, 3)
+        store(3)

@@ -23,11 +23,12 @@ def tile_attend_ghv_cau_kernel(tc, xT, wT, vT, y, wt, xm, offs, out):
     with ExitStack() as ctx:
         held = ctx.enter_context(tc.tile_pool(name="held", bufs=1))
         keep = ctx.enter_context(tc.tile_pool(name="keep", bufs=1))
-        stage = ctx.enter_context(tc.tile_pool(name="stage", bufs=5))
-        rawp = ctx.enter_context(tc.tile_pool(name="rawp", bufs=4))
-        dwp = ctx.enter_context(tc.tile_pool(name="dwp", bufs=4))
+        stage = ctx.enter_context(tc.tile_pool(name="stage", bufs=1))
+        rawp = ctx.enter_context(tc.tile_pool(name="rawp", bufs=1))
+        dwp = ctx.enter_context(tc.tile_pool(name="dwp", bufs=1))
         psum = ctx.enter_context(tc.psum_pool(name="psum", bufs=1))
 
+        SLOT = {"xst0":"s1","wst0":"s4","wst1":"s2","vst0":"s3","xmst0":"s4","gst0":"s3","xst1":"s0","vst1":"s2","xmst1":"s2","gst1":"s2","wg0":"g1","wg1":"g2","vg0":"g1","vg1":"g2","dw00":"d0","dw01":"d2","dw02":"d1","dw03":"d1","dw10":"d0","dw11":"d1","dw12":"d1","dw13":"d0","w0_0":"r0","w0_1":"r3","w1_0":"r2","w1_1":"r1","ac0":"r3","ac1":"r1","avc1":"r2","gt1":"r0"}
         offsets = held.tile([P, B * COLS], U16, name="offsets")
         nc.sync.dma_start(offsets[:], offs)
 
@@ -64,7 +65,7 @@ def tile_attend_ghv_cau_kernel(tc, xT, wT, vT, y, wt, xm, offs, out):
         wt_sb = keep.tile([P, B, 4], F32, name="wt_sb")
 
         def load_chunk(tab, u, h):
-            raw[tab, u, h] = rawp.tile([P, 2, 1024], F32, name="chunk")
+            raw[tab, u, h] = rawp.tile([P, 2, 1024], F32, name=SLOT[f"{tab}{u}_{h}"])
             nc.sync.dma_start(raw[tab, u, h][:], tables[tab][:, 2 * u:2 * u + 2, h * 1024:(h + 1) * 1024])
 
         def load_plane(tab, t):
@@ -92,17 +93,17 @@ def tile_attend_ghv_cau_kernel(tc, xT, wT, vT, y, wt, xm, offs, out):
 
         def gpair(tab, u, b):
             if (tab, b) not in gath:
-                gath[tab, b] = keep.tile([P, 2, 2 * N], BF16, name=f"gath_{tab}{b}")
+                gath[tab, b] = keep.tile([P, 2, 2 * N], BF16, name=SLOT[f"{tab}g{b}"])
             nc.vector.tensor_copy(gath[tab, b][:, u, :].bitcast(U32), pairs[tab, u][:].bitcast(U32).indirect(listed(b)))
 
         def gplane(tab, t, b):
             if (tab, b) not in gath:
-                gath[tab, b] = keep.tile([P, 4, N], F32, name=f"gath_{tab}{b}")
+                gath[tab, b] = keep.tile([P, 4, N], F32, name=SLOT[f"{tab}g{b}"])
             nc.vector.tensor_copy(gath[tab, b][:, t, :], raw[tab, t][:].indirect(listed(b)))
 
         def stage_of(nm, b):
             if (nm, b) not in staged:
-                staged[nm, b] = stage.tile([P, 4 * N], BF16, name="stage", align_bytes=64)
+                staged[nm, b] = stage.tile([P, 4 * N], BF16, name=SLOT[f"{nm}st{b}"], align_bytes=64)
                 quantised[nm][b] = staged[nm, b]
             return staged[nm, b]
 
@@ -137,6 +138,43 @@ def tile_attend_ghv_cau_kernel(tc, xT, wT, vT, y, wt, xm, offs, out):
                                 rhs=wq[b][0][:].bitcast(E4M3), rhs_scale=wq[b][1][:], start=True, stop=True)
             nc.vector.tensor_tensor(y_sb[b][:, t, :], bank[:], y_sb[b][:, t, :], ALU.subtract)
 
+        spare = {}
+
+        def spare_tile(key):
+            if key not in spare:
+                spare[key] = rawp.tile([P, 4, N], F32, name=SLOT[f"{key[0]}{key[1]}"])
+            return spare[key]
+
+        def residual_g(b, t, k):
+            bank = psum.tile([P, N], F32, name=f"bank{k}")
+            cols = slice(t * P, (t + 1) * P)
+            nc.tensor.matmul_mx(out=bank[:], lhsT=xq[b][0][:, cols].bitcast(E4M3), lhsT_scale=xq[b][1][:, cols],
+                                rhs=wq[b][0][:].bitcast(E4M3), rhs_scale=wq[b][1][:], start=True, stop=True)
+            a_sb = spare_tile(("ac", b))
+            nc.scalar.activation(a_sb[:, t, :], bank[:], ACT.Copy)
+            nc.gpsimd.tensor_tensor(y_sb[b][:, t, :], a_sb[:, t, :], y_sb[b][:, t, :], ALU.subtract)
+
+        g_rows = {}
+
+        def gradp(b, t, k):
+            bank = psum.tile([P, N], F32, name=f"bank{k}")
+            cols = slice(t * P, (t + 1) * P)
+            nc.tensor.matmul_mx(out=bank[:], lhsT=xq[b][0][:, cols].bitcast(E4M3), lhsT_scale=xq[b][1][:, cols],
+                                rhs=vq[b][0][:].bitcast(E4M3), rhs_scale=vq[b][1][:], start=True, stop=True)
+            avw = spare_tile(("avc", b))
+            if b not in g_rows:
+                g_rows[b] = rawp.tile([P, 4, N], BF16, name=SLOT[f"gt{b}"])
+            nc.scalar.activation(avw[:, t, :], bank[:], ACT.Copy, scale=wt_sb[:, b, t:t + 1])
+            nc.gpsimd.tensor_tensor(g_rows[b][:, t, :], avw[:, t, :], y_sb[b][:, t, :], ALU.mult)
+
+        def ilg(b, lo, eng, w):
+            dst = stage_of("g", b)[:, 4 * lo:4 * (lo + w)].rearrange("p (c i t) -> p c t i", i=4, t=4)
+            src = g_rows[b][:, :, lo:lo + w].rearrange("p t (c i) -> p c t i", i=4)
+            if eng == "s":
+                nc.scalar.copy(dst, src)
+            else:
+                nc.vector.tensor_copy(dst, src)
+
         def weight(b, t, eng):
             z = y_sb[b][:, t, :]
             nc.scalar.activation(z, z, ACT.Square)
@@ -147,6 +185,8 @@ def tile_attend_ghv_cau_kernel(tc, xT, wT, vT, y, wt, xm, offs, out):
             nc.scalar.activation(z, z, ACT.Square)
             if eng == "s":
                 nc.scalar.activation(z, z, ACT.Copy, scale=wt_sb[:, b, t:t + 1])
+            elif eng == "n":
+                return
             elif eng == "g":
                 nc.gpsimd.tensor_scalar(z, z, wt_sb[:, b, t:t + 1], 0.0, ALU.mult, ALU.add)
             else:
@@ -172,7 +212,7 @@ def tile_attend_ghv_cau_kernel(tc, xT, wT, vT, y, wt, xm, offs, out):
             cols = slice(j * P, (j + 1) * P)
             nc.tensor.matmul_mx(out=bank[:], lhsT=xmq[b][0][:, cols].bitcast(E4M3), lhsT_scale=xmq[b][1][:, cols],
                                 rhs=gq[b][0][:].bitcast(E5M2), rhs_scale=gq[b][1][:], start=True, stop=True)
-            dw[b, j] = dwp.tile([P, N], F32, name="dw")
+            dw[b, j] = dwp.tile([P, N], F32, name=SLOT[f"dw{b}{j}"])
             nc.scalar.activation(dw[b, j][:], bank[:], ACT.Copy)
 
         def scatter(b, j):
@@ -186,105 +226,105 @@ def tile_attend_ghv_cau_kernel(tc, xT, wT, vT, y, wt, xm, offs, out):
         zero(3, "g")
         load_chunk("w", 0, 0)
         load_chunk("w", 0, 1)
-        load_chunk("w", 1, 0)
         load_chunk("w", 1, 1)
+        cast("w", 1, 1, "v", 0, 384)
+        cast("w", 0, 0, "s", 0, 1024)
+        cast("w", 0, 1, "v", 0, 384)
+        load_chunk("w", 1, 0)
         load_half("x", 0, 0)
         load_wt()
+        il("x", 0, "s", 0, 512)
+        load_plane("v", 1)
+        cast("w", 1, 1, "s", 384, 640)
+        cast("w", 0, 1, "s", 384, 640)
+        cast("w", 1, 0, "s", 0, 1024)
+        gpair("w", 1, 0)
+        load_half("x", 1, 0)
+        load_half("xm", 0, 0)
         load_y(0, 0)
         load_y(0, 2)
-        load_plane("v", 0)
-        load_plane("v", 1)
-        load_plane("v", 2)
         load_plane("v", 3)
-        load_half("xm", 0, 0)
-        load_half("x", 1, 0)
-        load_y(1, 0)
-        load_y(1, 2)
-        load_half("xm", 1, 0)
-        cast("w", 0, 0, "s", 0, 1024)
-        cast("w", 0, 1, "s", 0, 384)
-        cast("w", 0, 1, "v", 384, 640)
-        cast("w", 1, 0, "s", 0, 1024)
-        cast("w", 1, 1, "s", 0, 384)
-        cast("w", 1, 1, "v", 384, 640)
+        load_plane("v", 0)
         gpair("w", 0, 0)
-        gpair("w", 1, 0)
-        il("x", 0, "s", 0, 512)
-        ppair("w", 0, "v")
         gpair("w", 0, 1)
-        gpair("w", 1, 1)
-        quant(quantised["w"], 0, "w0")
-        quant(quantised["x"], 0, "x0")
-        residual(0, 0, 0)
-        residual(0, 1, 1)
-        residual(0, 2, 2)
-        residual(0, 3, 3)
-        ppair("w", 1, "s")
-        weight(0, 0, "g")
-        weight(0, 1, "g")
-        weight(0, 2, "g")
-        weight(0, 3, "g")
         gplane("v", 0, 0)
-        gplane("v", 1, 0)
-        gplane("v", 2, 0)
-        gplane("v", 3, 0)
-        il("v", 0, "v", 0, 256)
-        il("v", 0, "s", 256, 256)
-        quant(quantised["v"], 0, "v0")
-        grad(0, 0, 4)
-        grad(0, 1, 5)
-        grad(0, 2, 6)
-        grad(0, 3, 7)
-        il("xm", 0, "g", 0, 128)
-        il("xm", 0, "g", 128, 128)
-        il("xm", 0, "g", 256, 128)
-        il("xm", 0, "g", 384, 128)
-        quant(quantised["xm"], 0, "xm0")
-        quant(quantised["g"], 0, "g0", E5M2)
-        product(0, 0, 0)
-        il("x", 1, "s", 0, 512)
-        quant(quantised["w"], 1, "w1")
-        quant(quantised["x"], 1, "x1")
-        residual(1, 0, 1)
-        residual(1, 1, 2)
-        residual(1, 2, 3)
-        residual(1, 3, 4)
-        product(0, 1, 4)
-        product(0, 2, 3)
-        weight(1, 0, "g")
-        weight(1, 1, "g")
-        weight(1, 2, "g")
-        weight(1, 3, "g")
-        gplane("v", 0, 1)
-        gplane("v", 1, 1)
-        gplane("v", 2, 1)
+        load_plane("v", 2)
+        load_half("xm", 1, 0)
+        ppair("w", 0, "v")
+        quant(quantised["w"], 0, "w0")
         gplane("v", 3, 1)
-        il("v", 1, "s", 0, 512)
-        quant(quantised["v"], 1, "v1")
-        il("xm", 1, "g", 0, 128)
+        gplane("v", 0, 1)
+        gplane("v", 2, 0)
+        gpair("w", 1, 1)
+        il("x", 1, "s", 0, 512)
+        quant(quantised["x"], 0, "x0")
+        gplane("v", 3, 0)
+        gplane("v", 1, 0)
+        load_y(1, 2)
+        residual(0, 3, 3)
+        quant(quantised["x"], 1, "x1")
+        ppair("w", 1, "s")
+        il("v", 0, "v", 0, 256)
+        gplane("v", 2, 1)
+        il("xm", 0, "g", 0, 128)
+        il("xm", 0, "s", 128, 128)
+        residual(0, 2, 7)
+        residual(0, 1, 4)
+        residual(0, 0, 0)
+        quant(quantised["w"], 1, "w1")
+        il("xm", 1, "s", 0, 128)
+        weight(0, 1, "g")
+        weight(0, 0, "g")
+        weight(0, 3, "g")
+        il("v", 0, "s", 256, 256)
         il("xm", 1, "g", 128, 128)
-        il("xm", 1, "g", 256, 128)
-        il("xm", 1, "g", 384, 128)
+        il("xm", 1, "s", 256, 128)
+        weight(0, 2, "s")
+        load_y(1, 0)
+        residual(1, 0, 7)
+        residual(1, 2, 5)
+        quant(quantised["v"], 0, "v0")
+        grad(0, 3, 4)
+        grad(0, 2, 3)
+        grad(0, 1, 5)
+        il("xm", 0, "s", 256, 128)
+        gplane("v", 1, 1)
+        il("xm", 0, "s", 384, 128)
+        grad(0, 0, 6)
+        il("xm", 1, "s", 384, 128)
+        residual(1, 1, 7)
+        quant(quantised["g"], 0, "g0", E5M2)
+        residual(1, 3, 5)
+        weight(1, 0, "g")
+        quant(quantised["xm"], 0, "xm0")
+        il("v", 1, "s", 0, 512)
         quant(quantised["xm"], 1, "xm1")
-        grad(1, 0, 5)
-        grad(1, 1, 6)
-        grad(1, 2, 7)
-        grad(1, 3, 0)
-        quant(quantised["g"], 1, "g1", E5M2)
-        scatter(0, 0)
-        scatter(0, 1)
-        scatter(0, 2)
+        weight(1, 2, "vv")
         product(0, 3, 0)
+        product(0, 0, 4)
+        weight(1, 1, "s")
         scatter(0, 3)
+        weight(1, 3, "s")
+        quant(quantised["v"], 1, "v1")
+        grad(1, 3, 0)
+        product(0, 1, 0)
+        grad(1, 0, 1)
+        grad(1, 1, 2)
+        grad(1, 2, 3)
+        quant(quantised["g"], 1, "g1", E5M2)
+        product(0, 2, 1)
+        product(1, 3, 5)
+        scatter(0, 1)
         product(1, 0, 1)
-        scatter(1, 0)
-        store(0)
-        product(1, 1, 2)
+        scatter(0, 0)
+        product(1, 1, 4)
         scatter(1, 1)
-        store(1)
-        product(1, 2, 3)
+        scatter(0, 2)
+        product(1, 2, 4)
         scatter(1, 2)
-        store(2)
-        product(1, 3, 4)
+        store(1)
+        scatter(1, 0)
         scatter(1, 3)
+        store(0)
+        store(2)
         store(3)

@@ -3,7 +3,6 @@ from contextlib import ExitStack
 import concourse.mybir as mybir
 
 B, N, T, D, R = 2, 512, 2048, 512, 512
-P = 128
 FLOPS = 3 * 2 * B * N * D * R
 
 F32 = mybir.dt.float32
@@ -15,316 +14,203 @@ E4M3 = mybir.dt.float8_e4m3fn_x4
 E5M2 = mybir.dt.float8_e5m2_x4
 ACT = mybir.ActivationFunctionType
 ALU = mybir.AluOpType
-COLS = N // 16
+
+P = 128
+PACK = 4
+RUN = 4
+LIST_COLUMNS = N // 16
+BLOCKS = D // P
+
+STAGE_BUFFER = {
+    ("w", 0): 0,
+    ("x", 0): 1, ("v", 0): 1, ("xm", 1): 1, ("g", 1): 1,
+    ("xm", 0): 2, ("v", 1): 2,
+    ("w", 1): 3,
+    ("x", 1): 4, ("g", 0): 4,
+}
 
 
 def tile_attend_ghv_cau_kernel(tc, xT, wT, vT, y, wt, xm, offs, out):
     nc = tc.nc
     with ExitStack() as ctx:
-        held = ctx.enter_context(tc.tile_pool(name="held", bufs=1))
-        keep = ctx.enter_context(tc.tile_pool(name="keep", bufs=1))
-        stage = ctx.enter_context(tc.tile_pool(name="stage", bufs=1))
-        rawp = ctx.enter_context(tc.tile_pool(name="rawp", bufs=1))
-        dwp = ctx.enter_context(tc.tile_pool(name="dwp", bufs=1))
+        lists = ctx.enter_context(tc.tile_pool(name="lists", bufs=1))
+        sbuf = ctx.enter_context(tc.tile_pool(name="sbuf", bufs=1))
         psum = ctx.enter_context(tc.psum_pool(name="psum", bufs=1))
 
-        SLOT = {"xst0":"s1","wst0":"s4","wst1":"s2","vst0":"s3","xmst0":"s4","gst0":"s3","xst1":"s0","vst1":"s2","xmst1":"s2","gst1":"s2","wg0":"g1","wg1":"g2","vg0":"g1","vg1":"g2","dw00":"d0","dw01":"d2","dw02":"d1","dw03":"d1","dw10":"d0","dw11":"d1","dw12":"d1","dw13":"d0","w0_0":"r0","w0_1":"r3","w1_0":"r2","w1_1":"r1","ac0":"r3","ac1":"r1","avc1":"r2","gt1":"r0"}
-        offsets = held.tile([P, B * COLS], U16, name="offsets")
+        offsets = lists.tile([P, B * LIST_COLUMNS], U16, name="offsets")
         nc.sync.dma_start(offsets[:], offs)
 
-        def listed(b):
-            return offsets[:, b * COLS:(b + 1) * COLS]
+        def group_list(b):
+            return offsets[:, b * LIST_COLUMNS:(b + 1) * LIST_COLUMNS]
 
-        def move(eng, dst, src):
-            if eng == "s":
+        one = sbuf.tile([P, 1], F32, name="one")
+        nc.vector.memset(one[:], 1.0)
+        nc.scalar.activation(one[:], one[:], ACT.Abs_reciprocal_sqrt)
+
+        windows = [sbuf.tile([P, T], F32, name=f"window{j}") for j in range(BLOCKS)]
+        for window in windows:
+            nc.gpsimd.memset(window[:], 0.0)
+
+        table_planes = {}
+        rows = {}
+        weights = [sbuf.tile([P, PACK, N], F32, name=f"weights{b}") for b in range(B)]
+        wt_sb = sbuf.tile([P, B, PACK], F32, name="wt_sb")
+
+        def load_plane(name, table, t):
+            table_planes[name, t] = sbuf.tile([P, T], F32, name=f"plane_{name}{t}")
+            nc.sync.dma_start(table_planes[name, t][:], table.rearrange("(p t) n -> p t n", t=PACK)[:, t, :])
+
+        def load_rows(name, source, b):
+            rows[name, b] = sbuf.tile([P, PACK, source.shape[2]], F32, name=f"rows_{name}{b}")
+            nc.sync.dma_start(rows[name, b][:], source[b].rearrange("(p t) c -> p t c", t=PACK))
+
+        def load_y(b, half):
+            planes = slice(2 * half, 2 * half + 2)
+            nc.sync.dma_start(weights[b][:, planes, :], y[b].rearrange("(p t) n -> p t n", t=PACK)[:, planes, :])
+
+        last = PACK - 1
+        for t in range(PACK):
+            load_plane("w", wT, t)
+        load_rows("x", xT, 0)
+        nc.sync.dma_start(wt_sb[:], wt.rearrange("b (p t) o -> p b (t o)", t=PACK))
+        load_y(0, 0)
+        load_y(0, 1)
+        for t in range(last):
+            load_plane("v", vT, t)
+        load_y(1, 0)
+        load_plane("v", vT, last)
+        load_rows("x", xT, 1)
+        load_rows("xm", xm, 0)
+        load_rows("xm", xm, 1)
+        load_y(1, 1)
+
+        gathered = {name: sbuf.tile([P, PACK, B * N], F32, name=f"gathered_{name}") for name in ("w", "v")}
+        a_sb = sbuf.tile([P, PACK, N], F32, name="a_sb")
+        staged = {}
+        codes = {}
+        scales = {}
+        products = {}
+
+        def gather_both(name, t):
+            nc.vector.tensor_copy(gathered[name][:, t, :], table_planes[name, t][:].indirect(offsets[:]))
+
+        def gather_group(name, t, b):
+            nc.vector.tensor_copy(gathered[name][:, t, b * N:(b + 1) * N], table_planes[name, t][:].indirect(group_list(b)))
+
+        def stage(name, b):
+            staged[name, b] = sbuf.tile([P, PACK * N], BF16, name=f"stage{STAGE_BUFFER[name, b]}", align_bytes=64)
+            return staged[name, b]
+
+        def cast(engine, dst, src):
+            if engine is nc.scalar:
                 nc.scalar.activation(dst, src, ACT.Copy)
-            elif eng == "g":
-                nc.gpsimd.tensor_scalar(dst, src, 1.0, 0.0, ALU.mult, ALU.add)
             else:
                 nc.vector.tensor_copy(dst, src)
 
-        def quantise(name, src, fmt):
-            codes = keep.tile([P, 512], U32, name=name + "_codes", align_bytes=64)
-            scales = keep.tile([P, 512], U8, name=name + "_scales", align_bytes=64)
-            nc.vector.quantize_mx(out=codes[:].bitcast(fmt), scales=scales[:], in_=src[:])
-            return codes, scales
+        def by_runs(planes):
+            return planes.rearrange("p t (c i) -> p c t i", i=RUN)
 
-        warm = keep.tile([P, 1], F32, name="warm")
-        nc.vector.memset(warm[:], 1.0)
-        nc.scalar.activation(warm[:], warm[:], ACT.Abs_reciprocal_sqrt)
+        def interleaved_by_runs(words):
+            return words.rearrange("p (c i t) -> p c t i", i=RUN, t=PACK)
 
-        windows = [keep.tile([P, T], F32, name=f"window{j}") for j in range(4)]
+        def interleave(engine, name, b, planes):
+            cast(engine, interleaved_by_runs(stage(name, b)[:]), by_runs(planes))
 
-        def zero(j, eng):
-            (nc.vector if eng == "v" else nc.gpsimd).memset(windows[j][:], 0.0)
+        def interleave_x(engine, b):
+            cast(engine, stage("x", b)[:].rearrange("p (t m j) -> p m j t", t=PACK, j=PACK),
+                 rows["x", b][:].rearrange("p j (m t) -> p m j t", t=PACK))
 
-        tables = {"w": wT.rearrange("(p t) n -> p t n", t=4), "v": vT.rearrange("(p t) n -> p t n", t=4)}
-        raw, pairs, gath, staged, y_sb = {}, {}, {}, {}, {}
-        wq, vq, xq, xmq, gq, g_bf = {}, {}, {}, {}, {}, {}
-        quantised = {"w": wq, "v": vq, "x": xq, "xm": xmq, "g": gq}
-        wt_sb = keep.tile([P, B, 4], F32, name="wt_sb")
+        def quantise(name, b, fmt=E4M3):
+            codes[name, b] = sbuf.tile([P, N], U32, name=f"codes_{name}{b}", align_bytes=64)
+            scales[name, b] = sbuf.tile([P, N], U8, name=f"scales_{name}{b}", align_bytes=64)
+            nc.vector.quantize_mx(out=codes[name, b][:].bitcast(fmt), scales=scales[name, b][:], in_=staged[name, b][:])
 
-        def load_chunk(tab, u, h):
-            raw[tab, u, h] = rawp.tile([P, 2, 1024], F32, name=SLOT[f"{tab}{u}_{h}"])
-            nc.sync.dma_start(raw[tab, u, h][:], tables[tab][:, 2 * u:2 * u + 2, h * 1024:(h + 1) * 1024])
+        def multiply(result, b, stationary, block, moving, columns=slice(0, N), fmt=E4M3):
+            held = slice(block * P, (block + 1) * P)
+            nc.tensor.matmul_mx(out=result, lhsT=codes[stationary, b][:, held].bitcast(E4M3),
+                                lhsT_scale=scales[stationary, b][:, held], rhs=codes[moving, b][:, columns].bitcast(fmt),
+                                rhs_scale=scales[moving, b][:, columns], start=True, stop=True)
 
-        def load_plane(tab, t):
-            raw[tab, t] = keep.tile([P, T], F32, name=f"plane_{tab}{t}")
-            nc.sync.dma_start(raw[tab, t][:], tables[tab][:, t, :])
-
-        def load_half(nm, b, h):
-            src = {"x": xT, "xm": xm}[nm][b].rearrange("(p j) r -> p j r", j=4)
-            raw[nm, b, h] = keep.tile([P, 4, 512], F32, name=f"raw_{nm}{b}{h}")
-            nc.sync.dma_start(raw[nm, b, h][:], src)
-
-        def load_y(b, t):
-            if b not in y_sb:
-                y_sb[b] = keep.tile([P, 4, N], F32, name=f"y_sb{b}")
-            nc.sync.dma_start(y_sb[b][:, t:t + 2, :], y[b].rearrange("(p t) n -> p t n", t=4)[:, t:t + 2, :])
-
-        def load_wt():
-            nc.sync.dma_start(wt_sb[:], wt.rearrange("b (p t) o -> p b (t o)", t=4))
-
-        def cast(tab, u, h, eng, lo, w):
-            if (tab, u) not in pairs:
-                pairs[tab, u] = keep.tile([P, 2 * T], BF16, name=f"pairs_{tab}{u}")
-            dst = pairs[tab, u][:, 2 * (1024 * h + lo):2 * (1024 * h + lo + w)].rearrange("p (c i e) -> p c e i", i=4, e=2)
-            move(eng, dst, raw[tab, u, h][:, :, lo:lo + w].rearrange("p e (c i) -> p c e i", i=4))
-
-        def gpair(tab, u, b):
-            if (tab, b) not in gath:
-                gath[tab, b] = keep.tile([P, 2, 2 * N], BF16, name=SLOT[f"{tab}g{b}"])
-            nc.vector.tensor_copy(gath[tab, b][:, u, :].bitcast(U32), pairs[tab, u][:].bitcast(U32).indirect(listed(b)))
-
-        def gplane(tab, t, b):
-            if (tab, b) not in gath:
-                gath[tab, b] = keep.tile([P, 4, N], F32, name=SLOT[f"{tab}g{b}"])
-            nc.vector.tensor_copy(gath[tab, b][:, t, :], raw[tab, t][:].indirect(listed(b)))
-
-        def stage_of(nm, b):
-            if (nm, b) not in staged:
-                staged[nm, b] = stage.tile([P, 4 * N], BF16, name=SLOT[f"{nm}st{b}"], align_bytes=64)
-                quantised[nm][b] = staged[nm, b]
-            return staged[nm, b]
-
-        def ppair(tab, b, eng):
-            dst = stage_of(tab, b)[:].rearrange("p (n u e) -> p n u e", u=2, e=2)
-            src = gath[tab, b][:].rearrange("p u (n e) -> p n u e", e=2)
-            if eng == "s":
-                nc.scalar.copy(dst, src)
+        def residual(b, t, on_gpsimd):
+            bank = psum.tile([P, N], F32, name=f"bank{t}")
+            multiply(bank[:], b, "x", t, "w")
+            plane = weights[b][:, t, :]
+            if on_gpsimd:
+                nc.scalar.activation(a_sb[:, t, :], bank[:], ACT.Copy)
+                nc.gpsimd.tensor_tensor(plane, a_sb[:, t, :], plane, ALU.subtract)
             else:
-                nc.vector.tensor_copy(dst, src)
+                nc.vector.tensor_tensor(plane, bank[:], plane, ALU.subtract)
 
-        def il(nm, b, eng, lo, w):
-            st = stage_of(nm, b)
-            if nm == "x":
-                dst = st[:].rearrange("p (t m j) -> p m j t", t=4, j=4)[:, lo // 4:(lo + w) // 4]
-                move(eng, dst, raw[nm, b, 0][:, :, lo:lo + w].rearrange("p j (m t) -> p m j t", t=4))
+        def weight(b, t, on_gpsimd):
+            plane = weights[b][:, t, :]
+            nc.scalar.activation(plane, plane, ACT.Square)
+            nc.scalar.activation(plane, plane, ACT.Abs_reciprocal_sqrt, bias=one[:])
+            nc.scalar.activation(plane, plane, ACT.Square)
+            if on_gpsimd:
+                nc.gpsimd.tensor_scalar(plane, plane, wt_sb[:, b, t:t + 1], 0.0, ALU.mult, ALU.add)
             else:
-                src = (raw[nm, b, 0] if nm == "xm" else gath[nm, b])[:, :, lo:lo + w]
-                if eng == "g":
-                    move(eng, st[:, 4 * lo:4 * (lo + w)].rearrange("p (n t) -> p n t", t=4), src.rearrange("p t n -> p n t"))
-                    return
-                dst = st[:, 4 * lo:4 * (lo + w)].rearrange("p (c i t) -> p c t i", i=4, t=4)
-                move(eng, dst, src.rearrange("p t (c i) -> p c t i", i=4))
+                nc.scalar.activation(plane, plane, ACT.Copy, scale=wt_sb[:, b, t:t + 1])
 
-        def quant(d, key, name, fmt=E4M3):
-            d[key] = quantise(name, d[key], fmt)
+        def form_g(b, first_bank):
+            g = stage("g", b)
+            for c in range(N // P):
+                bank = psum.tile([P, PACK, P], F32, name=f"bank{first_bank + c}")
+                items = slice(c * P, (c + 1) * P)
+                for t in range(PACK):
+                    multiply(bank[:, t, :], b, "x", t, "v", items)
+                nc.vector.tensor_tensor(interleaved_by_runs(g[:, PACK * c * P:PACK * (c + 1) * P]), by_runs(bank[:]),
+                                        by_runs(weights[b][:, :, items]), ALU.mult)
 
-        def residual(b, t, k):
-            bank = psum.tile([P, N], F32, name=f"bank{k}")
-            cols = slice(t * P, (t + 1) * P)
-            nc.tensor.matmul_mx(out=bank[:], lhsT=xq[b][0][:, cols].bitcast(E4M3), lhsT_scale=xq[b][1][:, cols],
-                                rhs=wq[b][0][:].bitcast(E4M3), rhs_scale=wq[b][1][:], start=True, stop=True)
-            nc.vector.tensor_tensor(y_sb[b][:, t, :], bank[:], y_sb[b][:, t, :], ALU.subtract)
-
-        spare = {}
-
-        def spare_tile(key):
-            if key not in spare:
-                spare[key] = rawp.tile([P, 4, N], F32, name=SLOT[f"{key[0]}{key[1]}"])
-            return spare[key]
-
-        def residual_g(b, t, k):
-            bank = psum.tile([P, N], F32, name=f"bank{k}")
-            cols = slice(t * P, (t + 1) * P)
-            nc.tensor.matmul_mx(out=bank[:], lhsT=xq[b][0][:, cols].bitcast(E4M3), lhsT_scale=xq[b][1][:, cols],
-                                rhs=wq[b][0][:].bitcast(E4M3), rhs_scale=wq[b][1][:], start=True, stop=True)
-            a_sb = spare_tile(("ac", b))
-            nc.scalar.activation(a_sb[:, t, :], bank[:], ACT.Copy)
-            nc.gpsimd.tensor_tensor(y_sb[b][:, t, :], a_sb[:, t, :], y_sb[b][:, t, :], ALU.subtract)
-
-        g_rows = {}
-
-        def gradp(b, t, k):
-            bank = psum.tile([P, N], F32, name=f"bank{k}")
-            cols = slice(t * P, (t + 1) * P)
-            nc.tensor.matmul_mx(out=bank[:], lhsT=xq[b][0][:, cols].bitcast(E4M3), lhsT_scale=xq[b][1][:, cols],
-                                rhs=vq[b][0][:].bitcast(E4M3), rhs_scale=vq[b][1][:], start=True, stop=True)
-            avw = spare_tile(("avc", b))
-            if b not in g_rows:
-                g_rows[b] = rawp.tile([P, 4, N], BF16, name=SLOT[f"gt{b}"])
-            nc.scalar.activation(avw[:, t, :], bank[:], ACT.Copy, scale=wt_sb[:, b, t:t + 1])
-            nc.gpsimd.tensor_tensor(g_rows[b][:, t, :], avw[:, t, :], y_sb[b][:, t, :], ALU.mult)
-
-        def ilg(b, lo, eng, w):
-            dst = stage_of("g", b)[:, 4 * lo:4 * (lo + w)].rearrange("p (c i t) -> p c t i", i=4, t=4)
-            src = g_rows[b][:, :, lo:lo + w].rearrange("p t (c i) -> p c t i", i=4)
-            if eng == "s":
-                nc.scalar.copy(dst, src)
-            else:
-                nc.vector.tensor_copy(dst, src)
-
-        def weight(b, t, eng):
-            z = y_sb[b][:, t, :]
-            nc.scalar.activation(z, z, ACT.Square)
-            nc.scalar.activation(z, z, ACT.Abs_reciprocal_sqrt, bias=1.0)
-            if eng == "vv":
-                nc.vector.scalar_tensor_tensor(z, z, wt_sb[:, b, t:t + 1], z, ALU.mult, ALU.mult)
-                return
-            nc.scalar.activation(z, z, ACT.Square)
-            if eng == "s":
-                nc.scalar.activation(z, z, ACT.Copy, scale=wt_sb[:, b, t:t + 1])
-            elif eng == "n":
-                return
-            elif eng == "g":
-                nc.gpsimd.tensor_scalar(z, z, wt_sb[:, b, t:t + 1], 0.0, ALU.mult, ALU.add)
-            else:
-                nc.vector.tensor_scalar(z, z, wt_sb[:, b, t:t + 1], None, ALU.mult)
-
-        def grad(b, c, k):
-            if b not in g_bf:
-                g_bf[b] = stage_of("g", b)
-            bank = psum.tile([P, 4, P], F32, name=f"bank{k}")
-            items = slice(c * P, (c + 1) * P)
-            for t in range(4):
-                cols = slice(t * P, (t + 1) * P)
-                nc.tensor.matmul_mx(out=bank[:, t, :], lhsT=xq[b][0][:, cols].bitcast(E4M3), lhsT_scale=xq[b][1][:, cols],
-                                    rhs=vq[b][0][:, items].bitcast(E4M3), rhs_scale=vq[b][1][:, items], start=True, stop=True)
-            dst = g_bf[b][:, 4 * c * P:4 * (c + 1) * P].rearrange("p (c i t) -> p c t i", i=4, t=4)
-            nc.vector.tensor_tensor(dst, bank[:].rearrange("p t (c i) -> p c t i", i=4),
-                                    y_sb[b][:, :, items].rearrange("p t (c i) -> p c t i", i=4), ALU.mult)
-
-        dw = {}
-
-        def product(b, j, k):
-            bank = psum.tile([P, N], F32, name=f"bank{k}")
-            cols = slice(j * P, (j + 1) * P)
-            nc.tensor.matmul_mx(out=bank[:], lhsT=xmq[b][0][:, cols].bitcast(E4M3), lhsT_scale=xmq[b][1][:, cols],
-                                rhs=gq[b][0][:].bitcast(E5M2), rhs_scale=gq[b][1][:], start=True, stop=True)
-            dw[b, j] = dwp.tile([P, N], F32, name=SLOT[f"dw{b}{j}"])
-            nc.scalar.activation(dw[b, j][:], bank[:], ACT.Copy)
+        def last_product(b, j, bank_number):
+            bank = psum.tile([P, N], F32, name=f"bank{bank_number}")
+            multiply(bank[:], b, "xm", j, "g", fmt=E5M2)
+            products[b, j] = sbuf.tile([P, N], F32, name=f"product{j}", align_bytes=64)
+            nc.scalar.activation(products[b, j][:], bank[:], ACT.Copy)
 
         def scatter(b, j):
-            nc.vector.tensor_copy(windows[j][:].indirect(listed(b)), dw[b, j][:])
+            nc.vector.tensor_copy(windows[j][:].indirect(group_list(b)), products[b, j][:])
 
-        def store(j):
+        for t in range(last):
+            gather_both("w", t)
+        for b in range(B):
+            gather_group("w", last, b)
+        for t in range(PACK):
+            gather_both("v", t)
+
+        interleave_x(nc.vector, 0)
+        for b in range(B):
+            interleave(nc.scalar, "w", b, gathered["w"][:, :, b * N:(b + 1) * N])
+        interleave_x(nc.scalar, 1)
+        interleave(nc.scalar, "xm", 0, rows["xm", 0][:])
+        for name, b in (("x", 0), ("w", 0), ("w", 1), ("x", 1)):
+            quantise(name, b)
+        interleave(nc.vector, "v", 0, gathered["v"][:, :, 0:N])
+        quantise("v", 0)
+
+        for t in range(PACK):
+            residual(0, t, on_gpsimd=t > 0)
+        for t in range(PACK):
+            weight(0, t, on_gpsimd=t < last)
+        form_g(0, first_bank=4)
+        quantise("xm", 0)
+        quantise("g", 0, E5M2)
+        interleave(nc.scalar, "xm", 1, rows["xm", 1][:])
+        quantise("xm", 1)
+        interleave(nc.scalar, "v", 1, gathered["v"][:, :, N:2 * N])
+        for j in range(BLOCKS - 1):
+            last_product(0, j, 4 + j)
+
+        for t in range(PACK):
+            residual(1, t, on_gpsimd=False)
+        quantise("v", 1)
+        for t in range(PACK):
+            weight(1, t, on_gpsimd=False)
+        form_g(1, first_bank=0)
+        last_product(0, BLOCKS - 1, 2)
+        quantise("g", 1, E5M2)
+        for j in range(BLOCKS):
+            scatter(0, j)
+        for j in range(BLOCKS):
+            last_product(1, j, 4 + j)
+            scatter(1, j)
             nc.sync.dma_start(out[j * P:(j + 1) * P, :], windows[j][:])
-        zero(0, "v")
-        zero(1, "v")
-        zero(2, "g")
-        zero(3, "g")
-        load_chunk("w", 0, 0)
-        load_chunk("w", 0, 1)
-        load_chunk("w", 1, 1)
-        cast("w", 1, 1, "v", 0, 384)
-        cast("w", 0, 0, "s", 0, 1024)
-        cast("w", 0, 1, "v", 0, 384)
-        load_chunk("w", 1, 0)
-        load_half("x", 0, 0)
-        load_wt()
-        il("x", 0, "s", 0, 512)
-        load_plane("v", 1)
-        cast("w", 1, 1, "s", 384, 640)
-        cast("w", 0, 1, "s", 384, 640)
-        cast("w", 1, 0, "s", 0, 1024)
-        gpair("w", 1, 0)
-        load_half("x", 1, 0)
-        load_half("xm", 0, 0)
-        load_y(0, 0)
-        load_y(0, 2)
-        load_plane("v", 3)
-        load_plane("v", 0)
-        gpair("w", 0, 0)
-        gpair("w", 0, 1)
-        gplane("v", 0, 0)
-        load_plane("v", 2)
-        load_half("xm", 1, 0)
-        ppair("w", 0, "v")
-        quant(quantised["w"], 0, "w0")
-        gplane("v", 3, 1)
-        gplane("v", 0, 1)
-        gplane("v", 2, 0)
-        gpair("w", 1, 1)
-        il("x", 1, "s", 0, 512)
-        quant(quantised["x"], 0, "x0")
-        gplane("v", 3, 0)
-        gplane("v", 1, 0)
-        load_y(1, 2)
-        residual(0, 3, 3)
-        quant(quantised["x"], 1, "x1")
-        ppair("w", 1, "s")
-        il("v", 0, "v", 0, 256)
-        gplane("v", 2, 1)
-        il("xm", 0, "g", 0, 128)
-        il("xm", 0, "s", 128, 128)
-        residual(0, 2, 7)
-        residual(0, 1, 4)
-        residual(0, 0, 0)
-        quant(quantised["w"], 1, "w1")
-        il("xm", 1, "s", 0, 128)
-        weight(0, 1, "g")
-        weight(0, 0, "g")
-        weight(0, 3, "g")
-        il("v", 0, "s", 256, 256)
-        il("xm", 1, "g", 128, 128)
-        il("xm", 1, "s", 256, 128)
-        weight(0, 2, "s")
-        load_y(1, 0)
-        residual(1, 0, 7)
-        residual(1, 2, 5)
-        quant(quantised["v"], 0, "v0")
-        grad(0, 3, 4)
-        grad(0, 2, 3)
-        grad(0, 1, 5)
-        il("xm", 0, "s", 256, 128)
-        gplane("v", 1, 1)
-        il("xm", 0, "s", 384, 128)
-        grad(0, 0, 6)
-        il("xm", 1, "s", 384, 128)
-        residual(1, 1, 7)
-        quant(quantised["g"], 0, "g0", E5M2)
-        residual(1, 3, 5)
-        weight(1, 0, "g")
-        quant(quantised["xm"], 0, "xm0")
-        il("v", 1, "s", 0, 512)
-        quant(quantised["xm"], 1, "xm1")
-        weight(1, 2, "vv")
-        product(0, 3, 0)
-        product(0, 0, 4)
-        weight(1, 1, "s")
-        scatter(0, 3)
-        weight(1, 3, "s")
-        quant(quantised["v"], 1, "v1")
-        grad(1, 3, 0)
-        product(0, 1, 0)
-        grad(1, 0, 1)
-        grad(1, 1, 2)
-        grad(1, 2, 3)
-        quant(quantised["g"], 1, "g1", E5M2)
-        product(0, 2, 1)
-        product(1, 3, 5)
-        scatter(0, 1)
-        product(1, 0, 1)
-        scatter(0, 0)
-        product(1, 1, 4)
-        scatter(1, 1)
-        scatter(0, 2)
-        product(1, 2, 4)
-        scatter(1, 2)
-        store(1)
-        scatter(1, 0)
-        scatter(1, 3)
-        store(0)
-        store(2)
-        store(3)

@@ -21,13 +21,7 @@ RUN = 4
 LIST_COLUMNS = N // 16
 BLOCKS = D // P
 
-STAGE_BUFFER = {
-    ("w", 0): 0,
-    ("x", 0): 1, ("v", 0): 1, ("xm", 1): 1, ("g", 1): 1,
-    ("xm", 0): 2, ("v", 1): 2,
-    ("w", 1): 3,
-    ("x", 1): 4, ("g", 0): 4,
-}
+PLACES = {("x", 0): 2048, ("v", 0): 0}
 
 
 def tile_attend_ghv_cau_kernel(tc, xT, wT, vT, y, wt, xm, offs, out):
@@ -35,13 +29,14 @@ def tile_attend_ghv_cau_kernel(tc, xT, wT, vT, y, wt, xm, offs, out):
     with ExitStack() as ctx:
         lists = ctx.enter_context(tc.tile_pool(name="lists", bufs=1))
         sbuf = ctx.enter_context(tc.tile_pool(name="sbuf", bufs=1))
+        placed = ctx.enter_context(tc.tile_pool(name="placed", bufs=1))
         psum = ctx.enter_context(tc.psum_pool(name="psum", bufs=1))
 
         offsets = lists.tile([P, B * LIST_COLUMNS], U16, name="offsets")
         nc.sync.dma_start(offsets[:], offs)
 
-        def group_list(b):
-            return offsets[:, b * LIST_COLUMNS:(b + 1) * LIST_COLUMNS]
+        def list_part(first, count):
+            return offsets[:, first // 16:(first + count) // 16]
 
         one = sbuf.tile([P, 1], F32, name="one")
         nc.vector.memset(one[:], 1.0)
@@ -51,59 +46,59 @@ def tile_attend_ghv_cau_kernel(tc, xT, wT, vT, y, wt, xm, offs, out):
         for window in windows:
             nc.gpsimd.memset(window[:], 0.0)
 
+        last = PACK - 1
         table_planes = {}
         rows = {}
-        weights = [sbuf.tile([P, PACK, N], F32, name=f"weights{b}") for b in range(B)]
+        weights = {}
+        gathered = {"w": sbuf.tile([P, PACK, B * N], F32, name="gathered_w")[:]}
         wt_sb = sbuf.tile([P, B, PACK], F32, name="wt_sb")
 
         def load_plane(name, table, t):
             table_planes[name, t] = sbuf.tile([P, T], F32, name=f"plane_{name}{t}")
             nc.sync.dma_start(table_planes[name, t][:], table.rearrange("(p t) n -> p t n", t=PACK)[:, t, :])
 
-        def load_rows(name, source, b):
-            rows[name, b] = sbuf.tile([P, PACK, source.shape[2]], F32, name=f"rows_{name}{b}")
-            nc.sync.dma_start(rows[name, b][:], source[b].rearrange("(p t) c -> p t c", t=PACK))
+        def load_rows(source, b, buffer):
+            loaded = sbuf.tile([P, PACK, source.shape[2]], F32, name=buffer)
+            nc.sync.dma_start(loaded[:], source[b].rearrange("(p t) c -> p t c", t=PACK))
+            return loaded[:]
 
-        def load_y(b, half):
-            planes = slice(2 * half, 2 * half + 2)
-            nc.sync.dma_start(weights[b][:, planes, :], y[b].rearrange("(p t) n -> p t n", t=PACK)[:, planes, :])
-
-        last = PACK - 1
         for t in range(PACK):
             load_plane("w", wT, t)
-        load_rows("x", xT, 0)
+        rows["x", 0] = load_rows(xT, 0, "rows_x0")
         nc.sync.dma_start(wt_sb[:], wt.rearrange("b (p t) o -> p b (t o)", t=PACK))
-        load_y(0, 0)
-        load_y(0, 1)
-        for t in range(last):
+        weights[0] = sbuf.tile([P, PACK, N], F32, name="rows_y0")[:]
+        for t in range(PACK):
             load_plane("v", vT, t)
-        load_y(1, 0)
-        load_plane("v", vT, last)
-        load_rows("x", xT, 1)
-        load_rows("xm", xm, 0)
-        load_rows("xm", xm, 1)
-        load_y(1, 1)
+            if t < 2:
+                planes = slice(2 * t, 2 * t + 2)
+                nc.sync.dma_start(weights[0][:, planes, :], y[0].rearrange("(p t) n -> p t n", t=PACK)[:, planes, :])
 
-        gathered = {name: sbuf.tile([P, PACK, B * N], F32, name=f"gathered_{name}") for name in ("w", "v")}
         a_sb = sbuf.tile([P, PACK, N], F32, name="a_sb")
         staged = {}
         codes = {}
         scales = {}
+        banks = {}
         products = {}
 
         def gather_both(name, t):
             nc.vector.tensor_copy(gathered[name][:, t, :], table_planes[name, t][:].indirect(offsets[:]))
 
         def gather_group(name, t, b):
-            nc.vector.tensor_copy(gathered[name][:, t, b * N:(b + 1) * N], table_planes[name, t][:].indirect(group_list(b)))
+            nc.vector.tensor_copy(gathered[name][:, t, b * N:(b + 1) * N],
+                                  table_planes[name, t][:].indirect(list_part(b * N, N)))
 
         def stage(name, b):
-            staged[name, b] = sbuf.tile([P, PACK * N], BF16, name=f"stage{STAGE_BUFFER[name, b]}", align_bytes=64)
+            if (name, b) in PLACES:
+                staged[name, b] = placed.tile([P, PACK * N], BF16, name=f"stage_{name}{b}", align_bytes=64, offset=PLACES[name, b])
+            else:
+                staged[name, b] = sbuf.tile([P, PACK * N], BF16, name=f"stage_{name}{b}", align_bytes=64)
             return staged[name, b]
 
         def cast(engine, dst, src):
             if engine is nc.scalar:
                 nc.scalar.activation(dst, src, ACT.Copy)
+            elif engine is nc.gpsimd:
+                nc.gpsimd.tensor_scalar(dst, src, 1.0, 0.0, ALU.mult, ALU.add)
             else:
                 nc.vector.tensor_copy(dst, src)
 
@@ -113,15 +108,27 @@ def tile_attend_ghv_cau_kernel(tc, xT, wT, vT, y, wt, xm, offs, out):
         def interleaved_by_runs(words):
             return words.rearrange("p (c i t) -> p c t i", i=RUN, t=PACK)
 
-        def interleave(engine, name, b, planes):
-            cast(engine, interleaved_by_runs(stage(name, b)[:]), by_runs(planes))
+        def interleave(engine, name, b, planes, parts=1):
+            words = stage(name, b)
+            width = N // parts
+            for part in range(parts):
+                dst = words[:, PACK * part * width:PACK * (part + 1) * width]
+                src = planes[:, :, part * width:(part + 1) * width]
+                if engine is nc.gpsimd:
+                    cast(engine, dst.rearrange("p (c t) -> p c t", t=PACK), src.rearrange("p t c -> p c t"))
+                else:
+                    cast(engine, interleaved_by_runs(dst), by_runs(src))
 
         def interleave_x(engine, b):
-            cast(engine, stage("x", b)[:].rearrange("p (t m j) -> p m j t", t=PACK, j=PACK),
-                 rows["x", b][:].rearrange("p j (m t) -> p m j t", t=PACK))
+            order = "p t m j" if engine is nc.gpsimd else "p m j t"
+            cast(engine, stage("x", b)[:].rearrange("p (t m j) -> " + order, t=PACK, j=PACK),
+                 rows["x", b].rearrange("p j (m t) -> " + order, t=PACK))
 
-        def quantise(name, b, fmt=E4M3):
-            codes[name, b] = sbuf.tile([P, N], U32, name=f"codes_{name}{b}", align_bytes=64)
+        def quantise(name, b, fmt=E4M3, buffer=None):
+            if (name, b) == ("w", 1):
+                codes[name, b] = placed.tile([P, N], U32, name="codes_w1", align_bytes=64, offset=0)
+            else:
+                codes[name, b] = sbuf.tile([P, N], U32, name=buffer or f"codes_{name}{b}", align_bytes=64)
             scales[name, b] = sbuf.tile([P, N], U8, name=f"scales_{name}{b}", align_bytes=64)
             nc.vector.quantize_mx(out=codes[name, b][:].bitcast(fmt), scales=scales[name, b][:], in_=staged[name, b][:])
 
@@ -141,15 +148,18 @@ def tile_attend_ghv_cau_kernel(tc, xT, wT, vT, y, wt, xm, offs, out):
             else:
                 nc.vector.tensor_tensor(plane, bank[:], plane, ALU.subtract)
 
-        def weight(b, t, on_gpsimd):
+        def weight(b, t):
             plane = weights[b][:, t, :]
+            root = plane
+            if (b, t) == (1, last):
+                root = sbuf.tile([P, N], F32, name="stage_xm1", align_bytes=64)[:]
             nc.scalar.activation(plane, plane, ACT.Square)
-            nc.scalar.activation(plane, plane, ACT.Abs_reciprocal_sqrt, bias=one[:])
-            nc.scalar.activation(plane, plane, ACT.Square)
-            if on_gpsimd:
-                nc.gpsimd.tensor_scalar(plane, plane, wt_sb[:, b, t:t + 1], 0.0, ALU.mult, ALU.add)
-            else:
-                nc.scalar.activation(plane, plane, ACT.Copy, scale=wt_sb[:, b, t:t + 1])
+            nc.scalar.activation(root, plane, ACT.Abs_reciprocal_sqrt, bias=one[:])
+            square = plane
+            if (b, t) == (0, last):
+                square = sbuf.tile([P, N], F32, name="stage_v1", align_bytes=64)[:]
+            nc.scalar.activation(square, root, ACT.Square)
+            nc.gpsimd.tensor_scalar(plane, square, wt_sb[:, b, t:t + 1], 0.0, ALU.mult, ALU.add)
 
         def form_g(b, first_bank):
             g = stage("g", b)
@@ -162,55 +172,73 @@ def tile_attend_ghv_cau_kernel(tc, xT, wT, vT, y, wt, xm, offs, out):
                                         by_runs(weights[b][:, :, items]), ALU.mult)
 
         def last_product(b, j, bank_number):
-            bank = psum.tile([P, N], F32, name=f"bank{bank_number}")
-            multiply(bank[:], b, "xm", j, "g", fmt=E5M2)
-            products[b, j] = sbuf.tile([P, N], F32, name=f"product{j}", align_bytes=64)
-            nc.scalar.activation(products[b, j][:], bank[:], ACT.Copy)
+            banks[b, j] = psum.tile([P, N], F32, name=f"bank{bank_number}")
+            multiply(banks[b, j][:], b, "xm", j, "g", fmt=E5M2)
 
-        def scatter(b, j):
-            nc.vector.tensor_copy(windows[j][:].indirect(group_list(b)), products[b, j][:])
+        def empty_bank(b, j, buffer, first=0, count=N):
+            products[b, j, first] = sbuf.tile([P, count], F32, name=buffer, align_bytes=64 if buffer.startswith("stage") else None)
+            nc.scalar.activation(products[b, j, first][:], banks[b, j][:, first:first + count], ACT.Copy)
+
+        def scatter(b, j, first=0, count=N):
+            nc.vector.tensor_copy(windows[j][:].indirect(list_part(b * N + first, count)), products[b, j, first][:])
 
         for t in range(last):
             gather_both("w", t)
         for b in range(B):
             gather_group("w", last, b)
-        for t in range(PACK):
-            gather_both("v", t)
+        rows["xm", 0] = load_rows(xm, 0, "plane_w0")
+        rows["x", 1] = load_rows(xT, 1, "plane_w1")
+        weights[1] = load_rows(y, 1, "plane_w3")
+        rows["xm", 1] = load_rows(xm, 1, "plane_w2")
 
-        interleave_x(nc.vector, 0)
-        for b in range(B):
-            interleave(nc.scalar, "w", b, gathered["w"][:, :, b * N:(b + 1) * N])
-        interleave_x(nc.scalar, 1)
-        interleave(nc.scalar, "xm", 0, rows["xm", 0][:])
-        for name, b in (("x", 0), ("w", 0), ("w", 1), ("x", 1)):
-            quantise(name, b)
-        interleave(nc.vector, "v", 0, gathered["v"][:, :, 0:N])
+        interleave(nc.scalar, "w", 0, gathered["w"][:, :, 0:N])
+        interleave(nc.scalar, "w", 1, gathered["w"][:, :, N:2 * N])
+        interleave_x(nc.gpsimd, 0)
+        quantise("w", 0)
+        quantise("x", 0)
+        words_v0 = stage("v", 0)[:].rearrange("p (c t) -> p c t", t=PACK)
+        gathered_v1 = placed.tile([P, PACK, N], F32, name="gathered_v1", align_bytes=64, offset=4096)
+        for t in range(PACK):
+            nc.vector.tensor_copy(words_v0[:, :, t], table_planes["v", t][:].indirect(list_part(0, N)))
+            nc.vector.tensor_copy(gathered_v1[:, t, :], table_planes["v", t][:].indirect(list_part(N, N)))
+
+        for t in range(PACK):
+            residual(0, t, on_gpsimd=True)
+        for t in range(PACK):
+            weight(0, t)
         quantise("v", 0)
-
-        for t in range(PACK):
-            residual(0, t, on_gpsimd=t > 0)
-        for t in range(PACK):
-            weight(0, t, on_gpsimd=t < last)
+        quantise("w", 1)
         form_g(0, first_bank=4)
+        interleave(nc.scalar, "xm", 0, rows["xm", 0])
+        interleave_x(nc.scalar, 1)
         quantise("xm", 0)
         quantise("g", 0, E5M2)
-        interleave(nc.scalar, "xm", 1, rows["xm", 1][:])
+        quantise("x", 1)
+        interleave(nc.gpsimd, "v", 1, gathered_v1[:])
+        quantise("v", 1, buffer="stage_g0")
+        last_product(0, 0, 4)
+        empty_bank(0, 0, "product0")
+        for t in range(PACK):
+            residual(1, t, on_gpsimd=True)
+        for j in range(1, BLOCKS):
+            last_product(0, j, j - 1)
+        for j in range(1, BLOCKS - 1):
+            empty_bank(0, j, f"product{j}")
+        half = N // 2
+        empty_bank(0, last, "product3", 0, half)
+        for t in range(PACK):
+            weight(1, t)
+        interleave(nc.scalar, "xm", 1, rows["xm", 1])
         quantise("xm", 1)
-        interleave(nc.scalar, "v", 1, gathered["v"][:, :, N:2 * N])
-        for j in range(BLOCKS - 1):
-            last_product(0, j, 4 + j)
-
-        for t in range(PACK):
-            residual(1, t, on_gpsimd=False)
-        quantise("v", 1)
-        for t in range(PACK):
-            weight(1, t, on_gpsimd=False)
-        form_g(1, first_bank=0)
-        last_product(0, BLOCKS - 1, 2)
+        form_g(1, first_bank=4)
         quantise("g", 1, E5M2)
-        for j in range(BLOCKS):
+        empty_bank(0, last, "plane_w3", half, half)
+        for j in range(BLOCKS - 1):
             scatter(0, j)
+        scatter(0, last, 0, half)
+        scatter(0, last, half, half)
         for j in range(BLOCKS):
-            last_product(1, j, 4 + j)
+            last_product(1, j, (0, 1, 3, 4)[j])
+            empty_bank(1, j, f"late_product{j}")
             scatter(1, j)
             nc.sync.dma_start(out[j * P:(j + 1) * P, :], windows[j][:])

@@ -21,7 +21,7 @@ RUN = 4
 LIST_COLUMNS = N // 16
 BLOCKS = D // P
 
-PLACES = {("x", 0): 2048, ("v", 0): 0}
+PLACES = {("v", 0): 0, ("v", 1): 2048}
 
 
 def tile_attend_ghv_cau_kernel(tc, xT, wT, vT, y, wt, xm, offs, out):
@@ -50,7 +50,7 @@ def tile_attend_ghv_cau_kernel(tc, xT, wT, vT, y, wt, xm, offs, out):
         table_planes = {}
         rows = {}
         weights = {}
-        gathered = {"w": sbuf.tile([P, PACK, B * N], F32, name="gathered_w")[:]}
+        gathered = {name: sbuf.tile([P, PACK, B * N], F32, name=f"gathered_{name}")[:] for name in ("w", "v")}
         wt_sb = sbuf.tile([P, B, PACK], F32, name="wt_sb")
 
         def load_plane(name, table, t):
@@ -73,8 +73,10 @@ def tile_attend_ghv_cau_kernel(tc, xT, wT, vT, y, wt, xm, offs, out):
                 planes = slice(2 * t, 2 * t + 2)
                 nc.sync.dma_start(weights[0][:, planes, :], y[0].rearrange("(p t) n -> p t n", t=PACK)[:, planes, :])
 
-        a_sb = sbuf.tile([P, PACK, N], F32, name="a_sb")
+        a_sb = {}
+        factors = {}
         staged = {}
+        g0_x1 = sbuf.tile([P, 3 * PACK * N // 2], BF16, name="stage_g0", align_bytes=64)
         codes = {}
         scales = {}
         banks = {}
@@ -88,7 +90,11 @@ def tile_attend_ghv_cau_kernel(tc, xT, wT, vT, y, wt, xm, offs, out):
                                   table_planes[name, t][:].indirect(list_part(b * N, N)))
 
         def stage(name, b):
-            if (name, b) in PLACES:
+            if (name, b) == ("x", 1):
+                staged[name, b] = g0_x1[:, PACK * N // 2:]
+            elif (name, b) == ("g", 0):
+                staged[name, b] = g0_x1[:, 0:PACK * N]
+            elif (name, b) in PLACES:
                 staged[name, b] = placed.tile([P, PACK * N], BF16, name=f"stage_{name}{b}", align_bytes=64, offset=PLACES[name, b])
             else:
                 staged[name, b] = sbuf.tile([P, PACK * N], BF16, name=f"stage_{name}{b}", align_bytes=64)
@@ -120,17 +126,16 @@ def tile_attend_ghv_cau_kernel(tc, xT, wT, vT, y, wt, xm, offs, out):
                     cast(engine, interleaved_by_runs(dst), by_runs(src))
 
         def interleave_x(engine, b):
-            order = "p t m j" if engine is nc.gpsimd else "p m j t"
-            cast(engine, stage("x", b)[:].rearrange("p (t m j) -> " + order, t=PACK, j=PACK),
-                 rows["x", b].rearrange("p j (m t) -> " + order, t=PACK))
+            cast(engine, stage("x", b)[:].rearrange("p (t m j) -> p m j t", t=PACK, j=PACK),
+                 rows["x", b].rearrange("p j (m t) -> p m j t", t=PACK))
 
-        def quantise(name, b, fmt=E4M3, buffer=None):
-            if (name, b) == ("w", 1):
-                codes[name, b] = placed.tile([P, N], U32, name="codes_w1", align_bytes=64, offset=0)
-            else:
+        def quantise(name, b, fmt=E4M3, buffer=None, first=0, count=N):
+            if first == 0:
                 codes[name, b] = sbuf.tile([P, N], U32, name=buffer or f"codes_{name}{b}", align_bytes=64)
-            scales[name, b] = sbuf.tile([P, N], U8, name=f"scales_{name}{b}", align_bytes=64)
-            nc.vector.quantize_mx(out=codes[name, b][:].bitcast(fmt), scales=scales[name, b][:], in_=staged[name, b][:])
+                scales[name, b] = sbuf.tile([P, N], U8, name=f"scales_{name}{b}", align_bytes=64)
+            columns = slice(first, first + count)
+            nc.vector.quantize_mx(out=codes[name, b][:, columns].bitcast(fmt), scales=scales[name, b][:, columns],
+                                  in_=staged[name, b][:, PACK * first:PACK * (first + count)])
 
         def multiply(result, b, stationary, block, moving, columns=slice(0, N), fmt=E4M3):
             held = slice(block * P, (block + 1) * P)
@@ -138,15 +143,14 @@ def tile_attend_ghv_cau_kernel(tc, xT, wT, vT, y, wt, xm, offs, out):
                                 lhsT_scale=scales[stationary, b][:, held], rhs=codes[moving, b][:, columns].bitcast(fmt),
                                 rhs_scale=scales[moving, b][:, columns], start=True, stop=True)
 
-        def residual(b, t, on_gpsimd):
+        def residual(b, t):
             bank = psum.tile([P, N], F32, name=f"bank{t}")
             multiply(bank[:], b, "x", t, "w")
             plane = weights[b][:, t, :]
-            if on_gpsimd:
-                nc.scalar.activation(a_sb[:, t, :], bank[:], ACT.Copy)
-                nc.gpsimd.tensor_tensor(plane, a_sb[:, t, :], plane, ALU.subtract)
-            else:
-                nc.vector.tensor_tensor(plane, bank[:], plane, ALU.subtract)
+            if t == 0:
+                a_sb[b] = sbuf.tile([P, PACK, N], F32, name="a_sb")
+            nc.scalar.activation(a_sb[b][:, t, :], bank[:], ACT.Copy)
+            nc.gpsimd.tensor_tensor(plane, a_sb[b][:, t, :], plane, ALU.subtract)
 
         def weight(b, t):
             plane = weights[b][:, t, :]
@@ -157,9 +161,14 @@ def tile_attend_ghv_cau_kernel(tc, xT, wT, vT, y, wt, xm, offs, out):
             nc.scalar.activation(root, plane, ACT.Abs_reciprocal_sqrt, bias=one[:])
             square = plane
             if (b, t) == (0, last):
-                square = sbuf.tile([P, N], F32, name="stage_v1", align_bytes=64)[:]
+                square = placed.tile([P, N], F32, name="square", align_bytes=64, offset=4096)[:]
             nc.scalar.activation(square, root, ACT.Square)
-            nc.gpsimd.tensor_scalar(plane, square, wt_sb[:, b, t:t + 1], 0.0, ALU.mult, ALU.add)
+            if t == 0:
+                factors[b] = sbuf.tile([P, PACK, N], F32, name="a_sb")
+            if (b, t) == (1, last):
+                nc.scalar.activation(factors[b][:, t, :], square, ACT.Copy, scale=wt_sb[:, b, t:t + 1])
+            else:
+                nc.gpsimd.tensor_scalar(factors[b][:, t, :], square, wt_sb[:, b, t:t + 1], 0.0, ALU.mult, ALU.add)
 
         def form_g(b, first_bank):
             g = stage("g", b)
@@ -169,7 +178,7 @@ def tile_attend_ghv_cau_kernel(tc, xT, wT, vT, y, wt, xm, offs, out):
                 for t in range(PACK):
                     multiply(bank[:, t, :], b, "x", t, "v", items)
                 nc.vector.tensor_tensor(interleaved_by_runs(g[:, PACK * c * P:PACK * (c + 1) * P]), by_runs(bank[:]),
-                                        by_runs(weights[b][:, :, items]), ALU.mult)
+                                        by_runs(factors[b][:, :, items]), ALU.mult)
 
         def last_product(b, j, bank_number):
             banks[b, j] = psum.tile([P, N], F32, name=f"bank{bank_number}")
@@ -186,45 +195,44 @@ def tile_attend_ghv_cau_kernel(tc, xT, wT, vT, y, wt, xm, offs, out):
             gather_both("w", t)
         for b in range(B):
             gather_group("w", last, b)
-        rows["xm", 0] = load_rows(xm, 0, "plane_w0")
-        rows["x", 1] = load_rows(xT, 1, "plane_w1")
+        for t in range(PACK):
+            gather_both("v", t)
+        rows["x", 1] = load_rows(xT, 1, "plane_w0")
+        rows["xm", 0] = load_rows(xm, 0, "plane_w1")
         weights[1] = load_rows(y, 1, "plane_w3")
         rows["xm", 1] = load_rows(xm, 1, "plane_w2")
 
         interleave(nc.scalar, "w", 0, gathered["w"][:, :, 0:N])
         interleave(nc.scalar, "w", 1, gathered["w"][:, :, N:2 * N])
-        interleave_x(nc.gpsimd, 0)
+        interleave_x(nc.vector, 0)
         quantise("w", 0)
         quantise("x", 0)
-        words_v0 = stage("v", 0)[:].rearrange("p (c t) -> p c t", t=PACK)
-        gathered_v1 = placed.tile([P, PACK, N], F32, name="gathered_v1", align_bytes=64, offset=4096)
+        quantise("w", 1)
         for t in range(PACK):
-            nc.vector.tensor_copy(words_v0[:, :, t], table_planes["v", t][:].indirect(list_part(0, N)))
-            nc.vector.tensor_copy(gathered_v1[:, t, :], table_planes["v", t][:].indirect(list_part(N, N)))
-
-        for t in range(PACK):
-            residual(0, t, on_gpsimd=True)
+            residual(0, t)
         for t in range(PACK):
             weight(0, t)
-        quantise("v", 0)
-        quantise("w", 1)
-        form_g(0, first_bank=4)
-        interleave(nc.scalar, "xm", 0, rows["xm", 0])
-        interleave_x(nc.scalar, 1)
-        quantise("xm", 0)
-        quantise("g", 0, E5M2)
-        quantise("x", 1)
-        interleave(nc.gpsimd, "v", 1, gathered_v1[:])
-        quantise("v", 1, buffer="stage_g0")
-        last_product(0, 0, 4)
-        empty_bank(0, 0, "product0")
-        for t in range(PACK):
-            residual(1, t, on_gpsimd=True)
-        for j in range(1, BLOCKS):
-            last_product(0, j, j - 1)
-        for j in range(1, BLOCKS - 1):
-            empty_bank(0, j, f"product{j}")
+        interleave(nc.vector, "v", 0, gathered["v"][:, :, 0:N], parts=2)
         half = N // 2
+        for first in (0, half):
+            quantise("v", 0, first=first, count=half)
+        interleave_x(nc.scalar, 1)
+        interleave(nc.scalar, "xm", 0, rows["xm", 0], parts=2)
+        quantise("x", 1)
+        form_g(0, first_bank=4)
+        quantise("xm", 0, first=0, count=half)
+        quantise("g", 0, E5M2)
+        interleave(nc.gpsimd, "v", 1, gathered["v"][:, :, N:2 * N])
+        quantise("v", 1, buffer="stage_g0")
+        quantise("xm", 0, first=half, count=half)
+        for j in range(2):
+            last_product(0, j, 2 + j)
+            empty_bank(0, j, f"product{j}")
+        for t in range(PACK):
+            residual(1, t)
+        for j in range(2, BLOCKS):
+            last_product(0, j, j - 2)
+        empty_bank(0, 2, "product2")
         empty_bank(0, last, "product3", 0, half)
         for t in range(PACK):
             weight(1, t)
@@ -232,13 +240,13 @@ def tile_attend_ghv_cau_kernel(tc, xT, wT, vT, y, wt, xm, offs, out):
         quantise("xm", 1)
         form_g(1, first_bank=4)
         quantise("g", 1, E5M2)
-        empty_bank(0, last, "plane_w3", half, half)
+        empty_bank(0, last, "a_sb", half, half)
         for j in range(BLOCKS - 1):
             scatter(0, j)
         scatter(0, last, 0, half)
         scatter(0, last, half, half)
         for j in range(BLOCKS):
-            last_product(1, j, (0, 1, 3, 4)[j])
+            last_product(1, j, (0, 2, 3, 4)[j])
             empty_bank(1, j, f"late_product{j}")
             scatter(1, j)
             nc.sync.dma_start(out[j * P:(j + 1) * P, :], windows[j][:])

@@ -21,15 +21,12 @@ RUN = 4
 LIST_COLUMNS = N // 16
 BLOCKS = D // P
 
-PLACES = {("v", 0): 0, ("v", 1): 2048}
-
 
 def tile_attend_ghv_cau_kernel(tc, xT, wT, vT, y, wt, xm, offs, out):
     nc = tc.nc
     with ExitStack() as ctx:
         lists = ctx.enter_context(tc.tile_pool(name="lists", bufs=1))
         sbuf = ctx.enter_context(tc.tile_pool(name="sbuf", bufs=1))
-        placed = ctx.enter_context(tc.tile_pool(name="placed", bufs=1))
         psum = ctx.enter_context(tc.psum_pool(name="psum", bufs=1))
 
         offsets = lists.tile([P, B * LIST_COLUMNS], U16, name="offsets")
@@ -54,11 +51,11 @@ def tile_attend_ghv_cau_kernel(tc, xT, wT, vT, y, wt, xm, offs, out):
         wt_sb = sbuf.tile([P, B, PACK], F32, name="wt_sb")
 
         def load_plane(name, table, t):
-            table_planes[name, t] = sbuf.tile([P, T], F32, name=f"plane_{name}{t}")
+            table_planes[name, t] = sbuf.tile([P, T], F32, name=f"plane_{name}{t}", align_bytes=64)
             nc.sync.dma_start(table_planes[name, t][:], table.rearrange("(p t) n -> p t n", t=PACK)[:, t, :])
 
         def load_rows(source, b, buffer):
-            loaded = sbuf.tile([P, PACK, source.shape[2]], F32, name=buffer)
+            loaded = sbuf.tile([P, PACK, source.shape[2]], F32, name=buffer, align_bytes=64)
             nc.sync.dma_start(loaded[:], source[b].rearrange("(p t) c -> p t c", t=PACK))
             return loaded[:]
 
@@ -75,8 +72,8 @@ def tile_attend_ghv_cau_kernel(tc, xT, wT, vT, y, wt, xm, offs, out):
 
         a_sb = {}
         factors = {}
+        residuals = {}
         staged = {}
-        g0_x1 = sbuf.tile([P, 3 * PACK * N // 2], BF16, name="stage_g0", align_bytes=64)
         codes = {}
         scales = {}
         banks = {}
@@ -89,16 +86,9 @@ def tile_attend_ghv_cau_kernel(tc, xT, wT, vT, y, wt, xm, offs, out):
             nc.vector.tensor_copy(gathered[name][:, t, b * N:(b + 1) * N],
                                   table_planes[name, t][:].indirect(list_part(b * N, N)))
 
-        def stage(name, b):
-            if (name, b) == ("x", 1):
-                staged[name, b] = g0_x1[:, PACK * N // 2:]
-            elif (name, b) == ("g", 0):
-                staged[name, b] = g0_x1[:, 0:PACK * N]
-            elif (name, b) in PLACES:
-                staged[name, b] = placed.tile([P, PACK * N], BF16, name=f"stage_{name}{b}", align_bytes=64, offset=PLACES[name, b])
-            else:
-                staged[name, b] = sbuf.tile([P, PACK * N], BF16, name=f"stage_{name}{b}", align_bytes=64)
-            return staged[name, b]
+        def stage(name, b, buffer=None, first=0, count=N):
+            staged[name, b, first] = sbuf.tile([P, PACK * count], BF16, name=buffer or f"stage_{name}{b}_{first}", align_bytes=64)
+            return staged[name, b, first]
 
         def cast(engine, dst, src):
             if engine is nc.scalar:
@@ -114,16 +104,13 @@ def tile_attend_ghv_cau_kernel(tc, xT, wT, vT, y, wt, xm, offs, out):
         def interleaved_by_runs(words):
             return words.rearrange("p (c i t) -> p c t i", i=RUN, t=PACK)
 
-        def interleave(engine, name, b, planes, parts=1):
-            words = stage(name, b)
-            width = N // parts
-            for part in range(parts):
-                dst = words[:, PACK * part * width:PACK * (part + 1) * width]
-                src = planes[:, :, part * width:(part + 1) * width]
-                if engine is nc.gpsimd:
-                    cast(engine, dst.rearrange("p (c t) -> p c t", t=PACK), src.rearrange("p t c -> p c t"))
-                else:
-                    cast(engine, interleaved_by_runs(dst), by_runs(src))
+        def interleave(engine, name, b, planes, buffer=None, first=0, count=N):
+            dst = stage(name, b, buffer, first, count)[:]
+            src = planes[:, :, first:first + count]
+            if engine is nc.gpsimd:
+                cast(engine, dst.rearrange("p (c t) -> p c t", t=PACK), src.rearrange("p t c -> p c t"))
+            else:
+                cast(engine, interleaved_by_runs(dst), by_runs(src))
 
         def interleave_x(engine, b):
             cast(engine, stage("x", b)[:].rearrange("p (t m j) -> p m j t", t=PACK, j=PACK),
@@ -135,7 +122,7 @@ def tile_attend_ghv_cau_kernel(tc, xT, wT, vT, y, wt, xm, offs, out):
                 scales[name, b] = sbuf.tile([P, N], U8, name=f"scales_{name}{b}", align_bytes=64)
             columns = slice(first, first + count)
             nc.vector.quantize_mx(out=codes[name, b][:, columns].bitcast(fmt), scales=scales[name, b][:, columns],
-                                  in_=staged[name, b][:, PACK * first:PACK * (first + count)])
+                                  in_=staged[name, b, first][:])
 
         def multiply(result, b, stationary, block, moving, columns=slice(0, N), fmt=E4M3):
             held = slice(block * P, (block + 1) * P)
@@ -146,26 +133,25 @@ def tile_attend_ghv_cau_kernel(tc, xT, wT, vT, y, wt, xm, offs, out):
         def residual(b, t):
             bank = psum.tile([P, N], F32, name=f"bank{t}")
             multiply(bank[:], b, "x", t, "w")
-            plane = weights[b][:, t, :]
             if t == 0:
                 a_sb[b] = sbuf.tile([P, PACK, N], F32, name="a_sb")
+                residuals[b] = weights[b]
+                if b == 1:
+                    residuals[b] = sbuf.tile([P, PACK, N], F32, name=f"stage_xm0_{N // 2}", align_bytes=64)[:]
             nc.scalar.activation(a_sb[b][:, t, :], bank[:], ACT.Copy)
-            nc.gpsimd.tensor_tensor(plane, a_sb[b][:, t, :], plane, ALU.subtract)
+            nc.gpsimd.tensor_tensor(residuals[b][:, t, :], a_sb[b][:, t, :], weights[b][:, t, :], ALU.subtract)
 
         def weight(b, t):
-            plane = weights[b][:, t, :]
-            root = plane
-            if (b, t) == (1, last):
-                root = sbuf.tile([P, N], F32, name="stage_xm1", align_bytes=64)[:]
+            plane = residuals[b][:, t, :]
             nc.scalar.activation(plane, plane, ACT.Square)
-            nc.scalar.activation(root, plane, ACT.Abs_reciprocal_sqrt, bias=one[:])
+            nc.scalar.activation(plane, plane, ACT.Abs_reciprocal_sqrt, bias=one[:])
             square = plane
-            if (b, t) == (0, last):
-                square = placed.tile([P, N], F32, name="square", align_bytes=64, offset=4096)[:]
-            nc.scalar.activation(square, root, ACT.Square)
+            if (b, t) == (1, last):
+                square = sbuf.tile([P, N], F32, name="stage_xm1_0", align_bytes=64)[:]
+            nc.scalar.activation(square, plane, ACT.Square)
             if t == 0:
                 factors[b] = sbuf.tile([P, PACK, N], F32, name="a_sb")
-            if (b, t) == (1, last):
+            if t >= 2 + b:
                 nc.scalar.activation(factors[b][:, t, :], square, ACT.Copy, scale=wt_sb[:, b, t:t + 1])
             else:
                 nc.gpsimd.tensor_scalar(factors[b][:, t, :], square, wt_sb[:, b, t:t + 1], 0.0, ALU.mult, ALU.add)
@@ -207,23 +193,25 @@ def tile_attend_ghv_cau_kernel(tc, xT, wT, vT, y, wt, xm, offs, out):
         interleave_x(nc.vector, 0)
         quantise("w", 0)
         quantise("x", 0)
-        quantise("w", 1)
         for t in range(PACK):
             residual(0, t)
         for t in range(PACK):
             weight(0, t)
-        interleave(nc.vector, "v", 0, gathered["v"][:, :, 0:N], parts=2)
         half = N // 2
         for first in (0, half):
+            interleave(nc.vector, "v", 0, gathered["v"][:, :, 0:N], first=first, count=half)
+        for first in (0, half):
             quantise("v", 0, first=first, count=half)
-        interleave_x(nc.scalar, 1)
-        interleave(nc.scalar, "xm", 0, rows["xm", 0], parts=2)
-        quantise("x", 1)
+        quantise("w", 1, buffer=f"stage_v0_{half}")
         form_g(0, first_bank=4)
+        interleave_x(nc.scalar, 1)
+        for first in (0, half):
+            interleave(nc.scalar, "xm", 0, rows["xm", 0], first=first, count=half)
+        quantise("x", 1)
         quantise("xm", 0, first=0, count=half)
         quantise("g", 0, E5M2)
-        interleave(nc.gpsimd, "v", 1, gathered["v"][:, :, N:2 * N])
-        quantise("v", 1, buffer="stage_g0")
+        interleave(nc.gpsimd, "v", 1, gathered["v"][:, :, N:2 * N], buffer="stage_w1_0")
+        quantise("v", 1, buffer="stage_g0_0")
         quantise("xm", 0, first=half, count=half)
         for j in range(2):
             last_product(0, j, 2 + j)

@@ -47,7 +47,10 @@ def tile_attend_ghv_cau_kernel(tc, xT, wT, vT, y, wt, xm, offs, out):
         table_planes = {}
         rows = {}
         weights = {}
-        gathered = {name: sbuf.tile([P, PACK, B * N], F32, name=f"gathered_{name}")[:] for name in ("w", "v")}
+        gathered = {"w": sbuf.tile([P, PACK, B * N], F32, name="gathered_w")[:]}
+        shared = sbuf.tile([P, PACK * B * N + N], F32, name="shared", align_bytes=64)
+        gathered["v"] = shared[:, 0:PACK * B * N].rearrange("p (t n) -> p t n", t=PACK)
+        staged_g0 = shared[:, PACK * B * N - N:].bitcast(BF16)
         wt_sb = sbuf.tile([P, B, PACK], F32, name="wt_sb")
 
         def load_plane(name, table, t):
@@ -134,12 +137,15 @@ def tile_attend_ghv_cau_kernel(tc, xT, wT, vT, y, wt, xm, offs, out):
             bank = psum.tile([P, N], F32, name=f"bank{t}")
             multiply(bank[:], b, "x", t, "w")
             if t == 0:
-                a_sb[b] = sbuf.tile([P, PACK, N], F32, name="a_sb")
+                a_sb[b] = sbuf.tile([P, PACK, N], F32, name="a_sb", align_bytes=64)
                 residuals[b] = weights[b]
                 if b == 1:
                     residuals[b] = sbuf.tile([P, PACK, N], F32, name=f"stage_xm0_{N // 2}", align_bytes=64)[:]
-            nc.scalar.activation(a_sb[b][:, t, :], bank[:], ACT.Copy)
-            nc.gpsimd.tensor_tensor(residuals[b][:, t, :], a_sb[b][:, t, :], weights[b][:, t, :], ALU.subtract)
+            if (b, t) == (0, 0):
+                nc.vector.tensor_tensor(residuals[b][:, t, :], bank[:], weights[b][:, t, :], ALU.subtract)
+            else:
+                nc.scalar.activation(a_sb[b][:, t, :], bank[:], ACT.Copy)
+                nc.gpsimd.tensor_tensor(residuals[b][:, t, :], a_sb[b][:, t, :], weights[b][:, t, :], ALU.subtract)
 
         def weight(b, t):
             plane = residuals[b][:, t, :]
@@ -150,14 +156,18 @@ def tile_attend_ghv_cau_kernel(tc, xT, wT, vT, y, wt, xm, offs, out):
                 square = sbuf.tile([P, N], F32, name="stage_xm1_0", align_bytes=64)[:]
             nc.scalar.activation(square, plane, ACT.Square)
             if t == 0:
-                factors[b] = sbuf.tile([P, PACK, N], F32, name="a_sb")
+                factors[b] = sbuf.tile([P, PACK, N], F32, name="a_sb", align_bytes=64)
             if t >= 2 + b:
                 nc.scalar.activation(factors[b][:, t, :], square, ACT.Copy, scale=wt_sb[:, b, t:t + 1])
             else:
                 nc.gpsimd.tensor_scalar(factors[b][:, t, :], square, wt_sb[:, b, t:t + 1], 0.0, ALU.mult, ALU.add)
 
         def form_g(b, first_bank):
-            g = stage("g", b)
+            if b == 0:
+                staged["g", 0, 0] = staged_g0
+            else:
+                stage("g", b)
+            g = staged["g", b, 0]
             for c in range(N // P):
                 bank = psum.tile([P, PACK, P], F32, name=f"bank{first_bank + c}")
                 items = slice(c * P, (c + 1) * P)
@@ -170,9 +180,9 @@ def tile_attend_ghv_cau_kernel(tc, xT, wT, vT, y, wt, xm, offs, out):
             banks[b, j] = psum.tile([P, N], F32, name=f"bank{bank_number}")
             multiply(banks[b, j][:], b, "xm", j, "g", fmt=E5M2)
 
-        def empty_bank(b, j, buffer, first=0, count=N):
-            products[b, j, first] = sbuf.tile([P, count], F32, name=buffer, align_bytes=64 if buffer.startswith("stage") else None)
-            nc.scalar.activation(products[b, j, first][:], banks[b, j][:, first:first + count], ACT.Copy)
+        def empty_bank(b, j, buffer, first=0, count=N, engine=nc.scalar):
+            products[b, j, first] = sbuf.tile([P, count], F32, name=buffer, align_bytes=64)
+            cast(engine, products[b, j, first][:], banks[b, j][:, first:first + count])
 
         def scatter(b, j, first=0, count=N):
             nc.vector.tensor_copy(windows[j][:].indirect(list_part(b * N + first, count)), products[b, j, first][:])
@@ -181,8 +191,9 @@ def tile_attend_ghv_cau_kernel(tc, xT, wT, vT, y, wt, xm, offs, out):
             gather_both("w", t)
         for b in range(B):
             gather_group("w", last, b)
-        for t in range(PACK):
+        for t in range(last):
             gather_both("v", t)
+        gather_group("v", last, 0)
         rows["x", 1] = load_rows(xT, 1, "plane_w0")
         rows["xm", 0] = load_rows(xm, 0, "plane_w1")
         weights[1] = load_rows(y, 1, "plane_w3")
@@ -205,13 +216,12 @@ def tile_attend_ghv_cau_kernel(tc, xT, wT, vT, y, wt, xm, offs, out):
         quantise("w", 1, buffer=f"stage_v0_{half}")
         form_g(0, first_bank=4)
         interleave_x(nc.scalar, 1)
-        for first in (0, half):
-            interleave(nc.scalar, "xm", 0, rows["xm", 0], first=first, count=half)
+        interleave(nc.gpsimd, "xm", 0, rows["xm", 0], buffer="stage_w1_0", first=0, count=half)
+        interleave(nc.scalar, "xm", 0, rows["xm", 0], first=half, count=half)
         quantise("x", 1)
         quantise("xm", 0, first=0, count=half)
         quantise("g", 0, E5M2)
-        interleave(nc.gpsimd, "v", 1, gathered["v"][:, :, N:2 * N], buffer="stage_w1_0")
-        quantise("v", 1, buffer="stage_g0_0")
+        gather_group("v", last, 1)
         quantise("xm", 0, first=half, count=half)
         for j in range(2):
             last_product(0, j, 2 + j)
@@ -221,17 +231,20 @@ def tile_attend_ghv_cau_kernel(tc, xT, wT, vT, y, wt, xm, offs, out):
         for j in range(2, BLOCKS):
             last_product(0, j, j - 2)
         empty_bank(0, 2, "product2")
-        empty_bank(0, last, "product3", 0, half)
+        interleave(nc.gpsimd, "v", 1, gathered["v"][:, :, N:2 * N], buffer="plane_w3")
         for t in range(PACK):
             weight(1, t)
         interleave(nc.scalar, "xm", 1, rows["xm", 1])
-        quantise("xm", 1)
+        for j in range(BLOCKS - 2):
+            scatter(0, j)
+        empty_bank(0, last, "shared", 0, half, nc.vector)
+        quantise("v", 1)
+        scatter(0, 2)
+        scatter(0, last, 0, half)
         form_g(1, first_bank=4)
+        quantise("xm", 1)
         quantise("g", 1, E5M2)
         empty_bank(0, last, "a_sb", half, half)
-        for j in range(BLOCKS - 1):
-            scatter(0, j)
-        scatter(0, last, 0, half)
         scatter(0, last, half, half)
         for j in range(BLOCKS):
             last_product(1, j, (0, 2, 3, 4)[j])

@@ -17,9 +17,13 @@ ALU = mybir.AluOpType
 
 P = 128
 PACK = 4
+LAST = PACK - 1
 RUN = 4
-LIST_COLUMNS = N // 16
+BAND = 16
+HALF = N // 2
 BLOCKS = D // P
+ALIGN = 64
+AV_BANK = 4
 
 
 def tile_attend_ghv_cau_kernel(tc, xT, wT, vT, y, wt, xm, offs, out):
@@ -29,11 +33,11 @@ def tile_attend_ghv_cau_kernel(tc, xT, wT, vT, y, wt, xm, offs, out):
         sbuf = ctx.enter_context(tc.tile_pool(name="sbuf", bufs=1))
         psum = ctx.enter_context(tc.psum_pool(name="psum", bufs=1))
 
-        offsets = lists.tile([P, B * LIST_COLUMNS], U16, name="offsets")
+        offsets = lists.tile([P, B * N // BAND], U16, name="offsets")
         nc.sync.dma_start(offsets[:], offs)
 
         def list_part(first, count):
-            return offsets[:, first // 16:(first + count) // 16]
+            return offsets[:, first // BAND:(first + count) // BAND]
 
         one = sbuf.tile([P, 1], F32, name="one")
         nc.vector.memset(one[:], 1.0)
@@ -43,22 +47,21 @@ def tile_attend_ghv_cau_kernel(tc, xT, wT, vT, y, wt, xm, offs, out):
         for window in windows:
             nc.gpsimd.memset(window[:], 0.0)
 
-        last = PACK - 1
         table_planes = {}
         rows = {}
-        weights = {}
+        targets = {}
         gathered = {"w": sbuf.tile([P, PACK, B * N], F32, name="gathered_w")[:]}
-        shared = sbuf.tile([P, PACK * B * N + N], F32, name="shared", align_bytes=64)
-        gathered["v"] = shared[:, 0:PACK * B * N].rearrange("p (t n) -> p t n", t=PACK)
-        staged_g0 = shared[:, PACK * B * N - N:].bitcast(BF16)
+        v_and_g = sbuf.tile([P, PACK * B * N + N], F32, name="v_and_g", align_bytes=ALIGN)
+        gathered["v"] = v_and_g[:, 0:PACK * B * N].rearrange("p (t n) -> p t n", t=PACK)
+        staged_g0 = v_and_g[:, PACK * B * N - N:].bitcast(BF16)
         wt_sb = sbuf.tile([P, B, PACK], F32, name="wt_sb")
 
         def load_plane(name, table, t):
-            table_planes[name, t] = sbuf.tile([P, T], F32, name=f"plane_{name}{t}", align_bytes=64)
+            table_planes[name, t] = sbuf.tile([P, T], F32, name=f"plane_{name}{t}", align_bytes=ALIGN)
             nc.sync.dma_start(table_planes[name, t][:], table.rearrange("(p t) n -> p t n", t=PACK)[:, t, :])
 
         def load_rows(source, b, buffer):
-            loaded = sbuf.tile([P, PACK, source.shape[2]], F32, name=buffer, align_bytes=64)
+            loaded = sbuf.tile([P, PACK, source.shape[2]], F32, name=buffer, align_bytes=ALIGN)
             nc.sync.dma_start(loaded[:], source[b].rearrange("(p t) c -> p t c", t=PACK))
             return loaded[:]
 
@@ -66,16 +69,16 @@ def tile_attend_ghv_cau_kernel(tc, xT, wT, vT, y, wt, xm, offs, out):
             load_plane("w", wT, t)
         rows["x", 0] = load_rows(xT, 0, "rows_x0")
         nc.sync.dma_start(wt_sb[:], wt.rearrange("b (p t) o -> p b (t o)", t=PACK))
-        weights[0] = sbuf.tile([P, PACK, N], F32, name="rows_y0")[:]
+        targets[0] = sbuf.tile([P, PACK, N], F32, name="rows_y0")[:]
         for t in range(PACK):
             load_plane("v", vT, t)
-            if t < 2:
+            if t < PACK // 2:
                 planes = slice(2 * t, 2 * t + 2)
-                nc.sync.dma_start(weights[0][:, planes, :], y[0].rearrange("(p t) n -> p t n", t=PACK)[:, planes, :])
+                nc.sync.dma_start(targets[0][:, planes, :], y[0].rearrange("(p t) n -> p t n", t=PACK)[:, planes, :])
 
         a_sb = {}
-        factors = {}
         residuals = {}
+        factors = {}
         staged = {}
         codes = {}
         scales = {}
@@ -90,7 +93,8 @@ def tile_attend_ghv_cau_kernel(tc, xT, wT, vT, y, wt, xm, offs, out):
                                   table_planes[name, t][:].indirect(list_part(b * N, N)))
 
         def stage(name, b, buffer=None, first=0, count=N):
-            staged[name, b, first] = sbuf.tile([P, PACK * count], BF16, name=buffer or f"stage_{name}{b}_{first}", align_bytes=64)
+            staged[name, b, first] = sbuf.tile([P, PACK * count], BF16, name=buffer or f"stage_{name}{b}_{first}",
+                                               align_bytes=ALIGN)
             return staged[name, b, first]
 
         def cast(engine, dst, src):
@@ -121,8 +125,8 @@ def tile_attend_ghv_cau_kernel(tc, xT, wT, vT, y, wt, xm, offs, out):
 
         def quantise(name, b, fmt=E4M3, buffer=None, first=0, count=N):
             if first == 0:
-                codes[name, b] = sbuf.tile([P, N], U32, name=buffer or f"codes_{name}{b}", align_bytes=64)
-                scales[name, b] = sbuf.tile([P, N], U8, name=f"scales_{name}{b}", align_bytes=64)
+                codes[name, b] = sbuf.tile([P, N], U32, name=buffer or f"codes_{name}{b}", align_bytes=ALIGN)
+                scales[name, b] = sbuf.tile([P, N], U8, name=f"scales_{name}{b}", align_bytes=ALIGN)
             columns = slice(first, first + count)
             nc.vector.quantize_mx(out=codes[name, b][:, columns].bitcast(fmt), scales=scales[name, b][:, columns],
                                   in_=staged[name, b, first][:])
@@ -133,43 +137,36 @@ def tile_attend_ghv_cau_kernel(tc, xT, wT, vT, y, wt, xm, offs, out):
                                 lhsT_scale=scales[stationary, b][:, held], rhs=codes[moving, b][:, columns].bitcast(fmt),
                                 rhs_scale=scales[moving, b][:, columns], start=True, stop=True)
 
-        def residual(b, t):
+        def residual(b, t, on_vector=False):
             bank = psum.tile([P, N], F32, name=f"bank{t}")
             multiply(bank[:], b, "x", t, "w")
-            if t == 0:
-                a_sb[b] = sbuf.tile([P, PACK, N], F32, name="a_sb", align_bytes=64)
-                residuals[b] = weights[b]
-                if b == 1:
-                    residuals[b] = sbuf.tile([P, PACK, N], F32, name=f"stage_xm0_{N // 2}", align_bytes=64)[:]
-            if (b, t) == (0, 0):
-                nc.vector.tensor_tensor(residuals[b][:, t, :], bank[:], weights[b][:, t, :], ALU.subtract)
+            if on_vector:
+                nc.vector.tensor_tensor(residuals[b][:, t, :], bank[:], targets[b][:, t, :], ALU.subtract)
             else:
                 nc.scalar.activation(a_sb[b][:, t, :], bank[:], ACT.Copy)
-                nc.gpsimd.tensor_tensor(residuals[b][:, t, :], a_sb[b][:, t, :], weights[b][:, t, :], ALU.subtract)
+                nc.gpsimd.tensor_tensor(residuals[b][:, t, :], a_sb[b][:, t, :], targets[b][:, t, :], ALU.subtract)
 
-        def weight(b, t):
+        def through(buffer, plane):
+            return sbuf.tile([P, N], F32, name=buffer, align_bytes=ALIGN)[:] if buffer else plane
+
+        def factor(b, t, wt_on_scalar, q_squared_buffer=None, inverse_buffer=None):
             plane = residuals[b][:, t, :]
-            nc.scalar.activation(plane, plane, ACT.Square)
-            nc.scalar.activation(plane, plane, ACT.Abs_reciprocal_sqrt, bias=one[:])
-            square = plane
-            if (b, t) == (1, last):
-                square = sbuf.tile([P, N], F32, name="stage_xm1_0", align_bytes=64)[:]
-            nc.scalar.activation(square, plane, ACT.Square)
+            q_squared = through(q_squared_buffer, plane)
+            nc.scalar.activation(q_squared, plane, ACT.Square)
+            nc.scalar.activation(plane, q_squared, ACT.Abs_reciprocal_sqrt, bias=one[:])
+            inverse = through(inverse_buffer, plane)
+            nc.scalar.activation(inverse, plane, ACT.Square)
             if t == 0:
-                factors[b] = sbuf.tile([P, PACK, N], F32, name="a_sb", align_bytes=64)
-            if t >= 2 + b:
-                nc.scalar.activation(factors[b][:, t, :], square, ACT.Copy, scale=wt_sb[:, b, t:t + 1])
+                factors[b] = sbuf.tile([P, PACK, N], F32, name="a_sb", align_bytes=ALIGN)
+            if wt_on_scalar:
+                nc.scalar.activation(factors[b][:, t, :], inverse, ACT.Copy, scale=wt_sb[:, b, t:t + 1])
             else:
-                nc.gpsimd.tensor_scalar(factors[b][:, t, :], square, wt_sb[:, b, t:t + 1], 0.0, ALU.mult, ALU.add)
+                nc.gpsimd.tensor_scalar(factors[b][:, t, :], inverse, wt_sb[:, b, t:t + 1], 0.0, ALU.mult, ALU.add)
 
-        def form_g(b, first_bank):
-            if b == 0:
-                staged["g", 0, 0] = staged_g0
-            else:
-                stage("g", b)
+        def form_g(b):
             g = staged["g", b, 0]
             for c in range(N // P):
-                bank = psum.tile([P, PACK, P], F32, name=f"bank{first_bank + c}")
+                bank = psum.tile([P, PACK, P], F32, name=f"bank{AV_BANK + c}")
                 items = slice(c * P, (c + 1) * P)
                 for t in range(PACK):
                     multiply(bank[:, t, :], b, "x", t, "v", items)
@@ -180,74 +177,86 @@ def tile_attend_ghv_cau_kernel(tc, xT, wT, vT, y, wt, xm, offs, out):
             banks[b, j] = psum.tile([P, N], F32, name=f"bank{bank_number}")
             multiply(banks[b, j][:], b, "xm", j, "g", fmt=E5M2)
 
-        def empty_bank(b, j, buffer, first=0, count=N, engine=nc.scalar):
-            products[b, j, first] = sbuf.tile([P, count], F32, name=buffer, align_bytes=64)
-            cast(engine, products[b, j, first][:], banks[b, j][:, first:first + count])
+        def empty_bank(b, j, buffer, first=0, count=N):
+            products[b, j, first] = sbuf.tile([P, count], F32, name=buffer, align_bytes=ALIGN)
+            nc.scalar.activation(products[b, j, first][:], banks[b, j][:, first:first + count], ACT.Copy)
 
         def scatter(b, j, first=0, count=N):
             nc.vector.tensor_copy(windows[j][:].indirect(list_part(b * N + first, count)), products[b, j, first][:])
 
-        for t in range(last):
+        for t in range(LAST):
             gather_both("w", t)
         for b in range(B):
-            gather_group("w", last, b)
-        for t in range(last):
+            gather_group("w", LAST, b)
+        for t in range(LAST):
             gather_both("v", t)
-        gather_group("v", last, 0)
+        gather_group("v", LAST, 0)
+
         rows["x", 1] = load_rows(xT, 1, "plane_w0")
         rows["xm", 0] = load_rows(xm, 0, "plane_w1")
-        weights[1] = load_rows(y, 1, "plane_w3")
+        targets[1] = load_rows(y, 1, "plane_w3")
         rows["xm", 1] = load_rows(xm, 1, "plane_w2")
 
-        interleave(nc.scalar, "w", 0, gathered["w"][:, :, 0:N])
-        interleave(nc.scalar, "w", 1, gathered["w"][:, :, N:2 * N])
+        for b in range(B):
+            interleave(nc.scalar, "w", b, gathered["w"][:, :, b * N:(b + 1) * N])
         interleave_x(nc.vector, 0)
         quantise("w", 0)
         quantise("x", 0)
+        a_sb[0] = sbuf.tile([P, PACK, N], F32, name="a_sb", align_bytes=ALIGN)
+        residuals[0] = targets[0]
         for t in range(PACK):
-            residual(0, t)
+            residual(0, t, on_vector=t == 0)
         for t in range(PACK):
-            weight(0, t)
-        half = N // 2
-        for first in (0, half):
-            interleave(nc.vector, "v", 0, gathered["v"][:, :, 0:N], first=first, count=half)
-        for first in (0, half):
-            quantise("v", 0, first=first, count=half)
-        quantise("w", 1, buffer=f"stage_v0_{half}")
-        form_g(0, first_bank=4)
+            factor(0, t, wt_on_scalar=t >= PACK // 2)
+
+        for first in (0, HALF):
+            interleave(nc.vector, "v", 0, gathered["v"][:, :, 0:N], first=first, count=HALF)
+        for first in (0, HALF):
+            quantise("v", 0, first=first, count=HALF)
+        quantise("w", 1, buffer=f"stage_v0_{HALF}")
+        staged["g", 0, 0] = staged_g0
+        form_g(0)
         interleave_x(nc.scalar, 1)
-        interleave(nc.gpsimd, "xm", 0, rows["xm", 0], buffer="stage_w1_0", first=0, count=half)
-        interleave(nc.scalar, "xm", 0, rows["xm", 0], first=half, count=half)
+        interleave(nc.gpsimd, "xm", 0, rows["xm", 0], buffer="stage_w1_0", first=0, count=HALF)
+        interleave(nc.scalar, "xm", 0, rows["xm", 0], first=HALF, count=HALF)
         quantise("x", 1)
-        quantise("xm", 0, first=0, count=half)
+        quantise("xm", 0, first=0, count=HALF)
         quantise("g", 0, E5M2)
-        gather_group("v", last, 1)
-        quantise("xm", 0, first=half, count=half)
-        for j in range(2):
-            last_product(0, j, 2 + j)
+        gather_group("v", LAST, 1)
+        quantise("xm", 0, first=HALF, count=HALF)
+
+        for j in range(BLOCKS // 2):
+            last_product(0, j, BLOCKS // 2 + j)
             empty_bank(0, j, f"product{j}")
+        a_sb[1] = sbuf.tile([P, PACK, N], F32, name="a_sb", align_bytes=ALIGN)
+        residuals[1] = sbuf.tile([P, PACK, N], F32, name=f"stage_xm0_{HALF}", align_bytes=ALIGN)[:]
         for t in range(PACK):
             residual(1, t)
-        for j in range(2, BLOCKS):
-            last_product(0, j, j - 2)
+        for j in range(BLOCKS // 2, BLOCKS):
+            last_product(0, j, j - BLOCKS // 2)
         empty_bank(0, 2, "product2")
         interleave(nc.gpsimd, "v", 1, gathered["v"][:, :, N:2 * N], buffer="plane_w3")
-        for t in range(PACK):
-            weight(1, t)
+
+        for t in range(LAST):
+            factor(1, t, wt_on_scalar=False)
+        factor(1, LAST, wt_on_scalar=True, q_squared_buffer="product3", inverse_buffer="stage_xm1_0")
+        empty_bank(0, LAST, "product3", 0, HALF)
         interleave(nc.scalar, "xm", 1, rows["xm", 1])
-        for j in range(BLOCKS - 2):
+        for j in range(BLOCKS // 2):
             scatter(0, j)
-        empty_bank(0, last, "shared", 0, half, nc.vector)
         quantise("v", 1)
         scatter(0, 2)
-        scatter(0, last, 0, half)
-        form_g(1, first_bank=4)
+        scatter(0, LAST, 0, HALF)
+
+        stage("g", 1)
+        form_g(1)
         quantise("xm", 1)
         quantise("g", 1, E5M2)
-        empty_bank(0, last, "a_sb", half, half)
-        scatter(0, last, half, half)
+        empty_bank(0, LAST, "a_sb", HALF, HALF)
+        scatter(0, LAST, HALF, HALF)
+        free_banks = (0, 2, 3, AV_BANK)
         for j in range(BLOCKS):
-            last_product(1, j, (0, 2, 3, 4)[j])
+            last_product(1, j, free_banks[j])
             empty_bank(1, j, f"late_product{j}")
             scatter(1, j)
             nc.sync.dma_start(out[j * P:(j + 1) * P, :], windows[j][:])

@@ -156,8 +156,6 @@ def tile_attend_ghv_cau_kernel(tc, xT, wT, vT, y, wt, xm, offs, out):
             nc.scalar.activation(plane, q_squared, ACT.Abs_reciprocal_sqrt, bias=one[:])
             inverse = through(inverse_buffer, plane)
             nc.scalar.activation(inverse, plane, ACT.Square)
-            if t == 0:
-                factors[b] = sbuf.tile([P, PACK, N], F32, name="a_sb", align_bytes=ALIGN)
             if wt_on_scalar:
                 nc.scalar.activation(factors[b][:, t, :], inverse, ACT.Copy, scale=wt_sb[:, b, t:t + 1])
             else:
@@ -184,8 +182,13 @@ def tile_attend_ghv_cau_kernel(tc, xT, wT, vT, y, wt, xm, offs, out):
         def scatter(b, j, first=0, count=N):
             nc.vector.tensor_copy(windows[j][:].indirect(list_part(b * N + first, count)), products[b, j, first][:])
 
-        for t in range(LAST):
-            gather_both("w", t)
+        words_w1 = stage("w", 1)[:].rearrange("p (c t) -> p c t", t=PACK)
+        for t, buffer in enumerate(("stage_x1_0", "stage_g1_0")):
+            gather_group("w", t, 0)
+            rounded = sbuf.tile([P, T], BF16, name=buffer, align_bytes=ALIGN)
+            nc.scalar.activation(rounded[:], table_planes["w", t][:], ACT.Copy)
+            nc.scalar.activation(words_w1[:, :, t], rounded[:].indirect(list_part(N, N)), ACT.Copy)
+        gather_both("w", 2)
         for b in range(B):
             gather_group("w", LAST, b)
         for t in range(LAST):
@@ -197,8 +200,8 @@ def tile_attend_ghv_cau_kernel(tc, xT, wT, vT, y, wt, xm, offs, out):
         targets[1] = load_rows(y, 1, "plane_w3")
         rows["xm", 1] = load_rows(xm, 1, "plane_w2")
 
-        for b in range(B):
-            interleave(nc.scalar, "w", b, gathered["w"][:, :, b * N:(b + 1) * N])
+        interleave(nc.scalar, "w", 0, gathered["w"][:, :, 0:N])
+        cast(nc.scalar, interleaved_by_runs(staged["w", 1, 0][:])[:, :, 2:, :], by_runs(gathered["w"][:, 2:, N:2 * N]))
         interleave_x(nc.vector, 0)
         quantise("w", 0)
         quantise("x", 0)
@@ -206,6 +209,7 @@ def tile_attend_ghv_cau_kernel(tc, xT, wT, vT, y, wt, xm, offs, out):
         residuals[0] = targets[0]
         for t in range(PACK):
             residual(0, t, on_vector=t == 0)
+        factors[0] = sbuf.tile([P, PACK, N], F32, name="a_sb", align_bytes=ALIGN)[:]
         for t in range(PACK):
             factor(0, t, wt_on_scalar=t >= PACK // 2)
 
@@ -235,24 +239,27 @@ def tile_attend_ghv_cau_kernel(tc, xT, wT, vT, y, wt, xm, offs, out):
         for j in range(BLOCKS // 2, BLOCKS):
             last_product(0, j, j - BLOCKS // 2)
         empty_bank(0, 2, "product2")
-        interleave(nc.gpsimd, "v", 1, gathered["v"][:, :, N:2 * N], buffer="plane_w3")
+        v_and_factors = sbuf.tile([P, PACK * N], F32, name="plane_w3", align_bytes=ALIGN)
+        factors[1] = v_and_factors[:].rearrange("p (t n) -> p t n", t=PACK)
+        staged["v", 1, 0] = v_and_factors[:, PACK * HALF:].bitcast(BF16)
+        cast(nc.gpsimd, staged["v", 1, 0].rearrange("p (c t) -> p c t", t=PACK),
+             gathered["v"][:, :, N:2 * N].rearrange("p t c -> p c t"))
+        quantise("v", 1)
 
         for t in range(LAST):
             factor(1, t, wt_on_scalar=False)
         factor(1, LAST, wt_on_scalar=True, q_squared_buffer="product3", inverse_buffer="stage_xm1_0")
         empty_bank(0, LAST, "product3", 0, HALF)
         interleave(nc.scalar, "xm", 1, rows["xm", 1])
-        for j in range(BLOCKS // 2):
+        for j in range(LAST):
             scatter(0, j)
-        quantise("v", 1)
-        scatter(0, 2)
         scatter(0, LAST, 0, HALF)
 
         stage("g", 1)
         form_g(1)
         quantise("xm", 1)
         quantise("g", 1, E5M2)
-        empty_bank(0, LAST, "a_sb", HALF, HALF)
+        empty_bank(0, LAST, "plane_w3", HALF, HALF)
         scatter(0, LAST, HALF, HALF)
         free_banks = (0, 2, 3, AV_BANK)
         for j in range(BLOCKS):

@@ -34,7 +34,6 @@ def tile_attend_ghv_cau_kernel(tc, xT, wT, vT, y, wt, xm, offs, out):
         psum = ctx.enter_context(tc.psum_pool(name="psum", bufs=1))
 
         offsets = lists.tile([P, B * N // BAND], U16, name="offsets")
-        nc.sync.dma_start(offsets[:], offs)
 
         def list_part(first, count):
             return offsets[:, first // BAND:(first + count) // BAND]
@@ -67,8 +66,10 @@ def tile_attend_ghv_cau_kernel(tc, xT, wT, vT, y, wt, xm, offs, out):
 
         for t in range(PACK):
             load_plane("w", wT, t)
+            if t == 0:
+                nc.sync.dma_start(offsets[:], offs)
         rows["x", 0] = load_rows(xT, 0, "rows_x0")
-        nc.sync.dma_start(wt_sb[:], wt.rearrange("b (p t) o -> p b (t o)", t=PACK))
+        nc.scalar.dma_start(wt_sb[:], wt.rearrange("b (p t) o -> p b (t o)", t=PACK))
         targets[0] = sbuf.tile([P, PACK, N], F32, name="rows_y0")[:]
         for t in range(PACK):
             load_plane("v", vT, t)
@@ -141,16 +142,16 @@ def tile_attend_ghv_cau_kernel(tc, xT, wT, vT, y, wt, xm, offs, out):
             bank = psum.tile([P, N], F32, name=f"bank{t}")
             multiply(bank[:], b, "x", t, "w")
             if on_vector:
-                nc.vector.tensor_tensor(residuals[b][:, t, :], bank[:], targets[b][:, t, :], ALU.subtract)
+                nc.vector.tensor_tensor(residuals[b][t], bank[:], targets[b][:, t, :], ALU.subtract)
             else:
                 nc.scalar.activation(a_sb[b][:, t, :], bank[:], ACT.Copy)
-                nc.gpsimd.tensor_tensor(residuals[b][:, t, :], a_sb[b][:, t, :], targets[b][:, t, :], ALU.subtract)
+                nc.gpsimd.tensor_tensor(residuals[b][t], a_sb[b][:, t, :], targets[b][:, t, :], ALU.subtract)
 
         def through(buffer, plane):
             return sbuf.tile([P, N], F32, name=buffer, align_bytes=ALIGN)[:] if buffer else plane
 
         def factor(b, t, wt_on_scalar, q_squared_buffer=None, inverse_buffer=None):
-            plane = residuals[b][:, t, :]
+            plane = residuals[b][t]
             q_squared = through(q_squared_buffer, plane)
             nc.scalar.activation(q_squared, plane, ACT.Square)
             nc.scalar.activation(plane, q_squared, ACT.Abs_reciprocal_sqrt, bias=one[:])
@@ -206,7 +207,8 @@ def tile_attend_ghv_cau_kernel(tc, xT, wT, vT, y, wt, xm, offs, out):
         quantise("w", 0)
         quantise("x", 0)
         a_sb[0] = sbuf.tile([P, PACK, N], F32, name="a_sb", align_bytes=ALIGN)
-        residuals[0] = targets[0]
+        residuals[0] = [targets[0][:, t, :] for t in range(PACK)]
+        residuals[0][0] = through("plane_v0", None)
         for t in range(PACK):
             residual(0, t, on_vector=t == 0)
         factors[0] = sbuf.tile([P, PACK, N], F32, name="a_sb", align_bytes=ALIGN)[:]
@@ -233,7 +235,8 @@ def tile_attend_ghv_cau_kernel(tc, xT, wT, vT, y, wt, xm, offs, out):
             last_product(0, j, BLOCKS // 2 + j)
             empty_bank(0, j, f"product{j}")
         a_sb[1] = sbuf.tile([P, PACK, N], F32, name="a_sb", align_bytes=ALIGN)
-        residuals[1] = sbuf.tile([P, PACK, N], F32, name=f"stage_xm0_{HALF}", align_bytes=ALIGN)[:]
+        q1 = sbuf.tile([P, PACK, N], F32, name=f"stage_xm0_{HALF}", align_bytes=ALIGN)
+        residuals[1] = [q1[:, t, :] for t in range(PACK)]
         for t in range(PACK):
             residual(1, t)
         for j in range(BLOCKS // 2, BLOCKS):

@@ -23,6 +23,7 @@ BAND = 16
 HALF = N // 2
 BLOCKS = D // P
 ALIGN = 64
+EARLY = 2
 AV_BANK = 4
 
 
@@ -49,10 +50,9 @@ def tile_attend_ghv_cau_kernel(tc, xT, wT, vT, y, wt, xm, offs, out):
         table_planes = {}
         rows = {}
         targets = {}
-        gathered = {"w": sbuf.tile([P, PACK, B * N], F32, name="gathered_w")[:]}
-        v_and_g = sbuf.tile([P, PACK * B * N + N], F32, name="v_and_g", align_bytes=ALIGN)
-        gathered["v"] = v_and_g[:, 0:PACK * B * N].rearrange("p (t n) -> p t n", t=PACK)
-        staged_g0 = v_and_g[:, PACK * B * N - N:].bitcast(BF16)
+        gathered = {"w": sbuf.tile([P, PACK, B * N], F32, name="gathered_w", align_bytes=ALIGN)[:]}
+        gathered_v = sbuf.tile([P, PACK * B * N], F32, name="gathered_v", align_bytes=ALIGN)
+        gathered["v"] = gathered_v[:].rearrange("p (t n) -> p t n", t=PACK)
         wt_sb = sbuf.tile([P, B, PACK], F32, name="wt_sb")
 
         def load_plane(name, table, t):
@@ -70,7 +70,7 @@ def tile_attend_ghv_cau_kernel(tc, xT, wT, vT, y, wt, xm, offs, out):
                 nc.sync.dma_start(offsets[:], offs)
         rows["x", 0] = load_rows(xT, 0, "rows_x0")
         nc.scalar.dma_start(wt_sb[:], wt.rearrange("b (p t) o -> p b (t o)", t=PACK))
-        targets[0] = sbuf.tile([P, PACK, N], F32, name="rows_y0")[:]
+        targets[0] = sbuf.tile([P, PACK, N], F32, name="rows_y0", align_bytes=ALIGN)[:]
         for t in range(PACK):
             load_plane("v", vT, t)
             if t < PACK // 2:
@@ -124,9 +124,11 @@ def tile_attend_ghv_cau_kernel(tc, xT, wT, vT, y, wt, xm, offs, out):
             cast(engine, stage("x", b)[:].rearrange("p (t m j) -> p m j t", t=PACK, j=PACK),
                  rows["x", b].rearrange("p j (m t) -> p m j t", t=PACK))
 
-        def quantise(name, b, fmt=E4M3, buffer=None, first=0, count=N):
-            if first == 0:
-                codes[name, b] = sbuf.tile([P, N], U32, name=buffer or f"codes_{name}{b}", align_bytes=ALIGN)
+        def quantise(name, b, fmt=E4M3, buffer=None, first=0, count=N, into=None):
+            if (name, b) not in codes:
+                if into is None:
+                    into = sbuf.tile([P, N], U32, name=buffer or f"codes_{name}{b}", align_bytes=ALIGN)
+                codes[name, b] = into
                 scales[name, b] = sbuf.tile([P, N], U8, name=f"scales_{name}{b}", align_bytes=ALIGN)
             columns = slice(first, first + count)
             nc.vector.quantize_mx(out=codes[name, b][:, columns].bitcast(fmt), scales=scales[name, b][:, columns],
@@ -162,9 +164,8 @@ def tile_attend_ghv_cau_kernel(tc, xT, wT, vT, y, wt, xm, offs, out):
             else:
                 nc.gpsimd.tensor_scalar(factors[b][:, t, :], inverse, wt_sb[:, b, t:t + 1], 0.0, ALU.mult, ALU.add)
 
-        def form_g(b):
-            g = staged["g", b, 0]
-            for c in range(N // P):
+        def form_g(b, g, blocks):
+            for c in blocks:
                 bank = psum.tile([P, PACK, P], F32, name=f"bank{AV_BANK + c}")
                 items = slice(c * P, (c + 1) * P)
                 for t in range(PACK):
@@ -174,7 +175,10 @@ def tile_attend_ghv_cau_kernel(tc, xT, wT, vT, y, wt, xm, offs, out):
 
         def last_product(b, j, bank_number):
             banks[b, j] = psum.tile([P, N], F32, name=f"bank{bank_number}")
-            multiply(banks[b, j][:], b, "xm", j, "g", fmt=E5M2)
+            if ("xm_late", b) in codes and j >= BLOCKS // 2:
+                multiply(banks[b, j][:], b, "xm_late", j - BLOCKS // 2, "g", fmt=E5M2)
+            else:
+                multiply(banks[b, j][:], b, "xm", j, "g", fmt=E5M2)
 
         def empty_bank(b, j, buffer, first=0, count=N):
             products[b, j, first] = sbuf.tile([P, count], F32, name=buffer, align_bytes=ALIGN)
@@ -182,6 +186,11 @@ def tile_attend_ghv_cau_kernel(tc, xT, wT, vT, y, wt, xm, offs, out):
 
         def scatter(b, j, first=0, count=N):
             nc.vector.tensor_copy(windows[j][:].indirect(list_part(b * N + first, count)), products[b, j, first][:])
+
+        codes["g", 1] = sbuf.tile([P, N], U32, name="codes_g1", align_bytes=ALIGN)
+        scales["g", 1] = sbuf.tile([P, N], U8, name="scales_g1", align_bytes=ALIGN)
+        nc.gpsimd.memset(codes["g", 1][:, HALF:], 0)
+        nc.gpsimd.memset(scales["g", 1][:, HALF:].bitcast(U32), 0)
 
         words_w1 = stage("w", 1)[:].rearrange("p (c t) -> p c t", t=PACK)
         for t, buffer in enumerate(("stage_x1_0", "stage_g1_0")):
@@ -196,8 +205,8 @@ def tile_attend_ghv_cau_kernel(tc, xT, wT, vT, y, wt, xm, offs, out):
             gather_both("v", t)
         gather_group("v", LAST, 0)
 
-        rows["x", 1] = load_rows(xT, 1, "plane_w0")
-        rows["xm", 0] = load_rows(xm, 0, "plane_w1")
+        rows["xm", 0] = load_rows(xm, 0, "plane_w0")
+        rows["x", 1] = load_rows(xT, 1, "plane_w1")
         targets[1] = load_rows(y, 1, "plane_w3")
         rows["xm", 1] = load_rows(xm, 1, "plane_w2")
 
@@ -206,67 +215,137 @@ def tile_attend_ghv_cau_kernel(tc, xT, wT, vT, y, wt, xm, offs, out):
         interleave_x(nc.vector, 0)
         quantise("w", 0)
         quantise("x", 0)
+        quantise("w", 1)
         a_sb[0] = sbuf.tile([P, PACK, N], F32, name="a_sb", align_bytes=ALIGN)
         residuals[0] = [targets[0][:, t, :] for t in range(PACK)]
-        residuals[0][0] = through("plane_v0", None)
         for t in range(PACK):
             residual(0, t, on_vector=t == 0)
         factors[0] = sbuf.tile([P, PACK, N], F32, name="a_sb", align_bytes=ALIGN)[:]
         for t in range(PACK):
             factor(0, t, wt_on_scalar=t >= PACK // 2)
 
-        for first in (0, HALF):
-            interleave(nc.vector, "v", 0, gathered["v"][:, :, 0:N], first=first, count=HALF)
+        staged["v", 0, 0] = gathered_v[:, PACK * B * N - N:].bitcast(BF16)
+        cast(nc.vector, interleaved_by_runs(staged["v", 0, 0]), by_runs(gathered["v"][:, :, 0:HALF]))
+        interleave(nc.vector, "v", 0, gathered["v"][:, :, 0:N], first=HALF, count=HALF)
         for first in (0, HALF):
             quantise("v", 0, first=first, count=HALF)
-        quantise("w", 1, buffer=f"stage_v0_{HALF}")
-        staged["g", 0, 0] = staged_g0
-        form_g(0)
-        interleave_x(nc.scalar, 1)
-        interleave(nc.gpsimd, "xm", 0, rows["xm", 0], buffer="stage_w1_0", first=0, count=HALF)
-        interleave(nc.scalar, "xm", 0, rows["xm", 0], first=HALF, count=HALF)
-        quantise("x", 1)
-        quantise("xm", 0, first=0, count=HALF)
-        quantise("g", 0, E5M2)
         gather_group("v", LAST, 1)
-        quantise("xm", 0, first=HALF, count=HALF)
+        form_g(0, stage("g", 0), range(BLOCKS))
+        interleave(nc.gpsimd, "xm", 0, rows["xm", 0], buffer=f"stage_v0_{HALF}", first=0, count=HALF)
+        interleave(nc.gpsimd, "v", 1, gathered["v"][:, :, N:2 * N])
+        interleave_x(nc.scalar, 1)
+        interleave(nc.scalar, "xm", 0, rows["xm", 0], buffer="stage_xm0_late", first=HALF, count=HALF)
+        x_and_xm = sbuf.tile([P, N + HALF], U32, name="a_sb", align_bytes=ALIGN)
+        quantise("x", 1, into=x_and_xm[:, 0:N])
+        quantise("xm", 0, into=x_and_xm[:, N:], first=0, count=HALF)
+        quantise("g", 0, E5M2, buffer="stage_x1_0")
+        v_and_xm = sbuf.tile([P, N + HALF], U32, name="stage_g0_0", align_bytes=ALIGN)
+        quantise("v", 1, into=v_and_xm[:, 0:N])
+        staged["xm_late", 0, 0] = staged["xm", 0, HALF]
+        quantise("xm_late", 0, into=v_and_xm[:, N:], count=HALF)
 
-        for j in range(BLOCKS // 2):
-            last_product(0, j, BLOCKS // 2 + j)
-            empty_bank(0, j, f"product{j}")
-        a_sb[1] = sbuf.tile([P, PACK, N], F32, name="a_sb", align_bytes=ALIGN)
-        q1 = sbuf.tile([P, PACK, N], F32, name=f"stage_xm0_{HALF}", align_bytes=ALIGN)
-        residuals[1] = [q1[:, t, :] for t in range(PACK)]
-        for t in range(PACK):
-            residual(1, t)
-        for j in range(BLOCKS // 2, BLOCKS):
-            last_product(0, j, j - BLOCKS // 2)
+        last_product(0, 0, AV_BANK)
+        empty_bank(0, 0, "product0")
+        late = sbuf.tile([P, (BLOCKS + 1) * N], F32, name="stage_xm0_late", align_bytes=ALIGN)
+        q_blocks = [late[:, place * N:(place + 1) * N] for place in (0, 1, 2, BLOCKS)]
+        staged["xm", 1, 0] = late[:, LAST * N:BLOCKS * N].bitcast(BF16)
+        staged["xm", 1, HALF] = late[:, BLOCKS * N:].bitcast(BF16)
+        a_blocks = sbuf.tile([P, BLOCKS * N], F32, name="plane_v1", align_bytes=ALIGN)
+        inverses = [sbuf.tile([P, N], F32, name=buffer, align_bytes=ALIGN)
+                    for buffer in ("rows_x0", "plane_v2", "plane_v3", "stage_x0_0")]
+        weighted_av = {first: sbuf.tile([P, PACK, HALF], F32, name=buffer, align_bytes=ALIGN)
+                       for first, buffer in ((0, "gathered_w"), (HALF, "rows_y0"))}
+        stage("g", 1, buffer="stage_g1_0", count=HALF)
+
+        def as_planes(block):
+            return block.rearrange("p (t i) -> p t i", t=PACK)
+
+        def as_items(block):
+            return block.rearrange("p (i t) -> p i t", t=PACK)
+
+        def by_items(planes):
+            return planes.rearrange("p t i -> p i t")
+
+        def residual_block(c):
+            bank = psum.tile([P, PACK, P], F32, name=f"bank{c}")
+            for t in range(PACK):
+                multiply(bank[:, t, :], 1, "x", t, "w", slice(c * P, (c + 1) * P))
+            a_block = a_blocks[:, c * N:(c + 1) * N]
+            nc.scalar.activation(a_block, bank[:].rearrange("p t i -> p (t i)"), ACT.Copy)
+            nc.gpsimd.tensor_tensor(as_planes(q_blocks[c]), as_planes(a_block), targets[1][:, :, c * P:(c + 1) * P],
+                                    ALU.subtract)
+
+        squares = {}
+
+        def square(c, buffer=None):
+            squares[c] = through(buffer, q_blocks[c])
+            nc.scalar.activation(squares[c], q_blocks[c], ACT.Square)
+
+        def root(c):
+            nc.scalar.activation(q_blocks[c], squares[c], ACT.Abs_reciprocal_sqrt, bias=one[:])
+
+        def inverse(c):
+            nc.scalar.activation(as_items(inverses[c][:]), by_items(as_planes(q_blocks[c])), ACT.Square)
+
+        def product(engine, c, half):
+            engine.tensor_tensor(as_items(half[:, PACK * (c % 2) * P:PACK * (c % 2 + 1) * P]),
+                                 by_items(weighted_av[c // 2 * HALF][:, :, c % 2 * P:(c % 2 + 1) * P]), as_items(inverses[c][:]), ALU.mult)
+
+        def copy_av_half(first):
+            items = slice(first, first + HALF)
+            for pair in range(PACK // 2):
+                bank = psum.tile([P, 2, HALF], F32, name=f"bank{AV_BANK + 2 + pair}")
+                for t in (2 * pair, 2 * pair + 1):
+                    multiply(bank[:, t % 2, :], 1, "x", t, "v", items)
+                for t in (2 * pair, 2 * pair + 1):
+                    nc.scalar.activation(weighted_av[first][:, t, :], bank[:, t % 2, :], ACT.Copy, scale=wt_sb[:, 1, t:t + 1])
+
+        for c in range(BLOCKS):
+            residual_block(c)
+        cast(nc.gpsimd, as_items(staged["xm", 1, 0]), by_items(rows["xm", 1][:, :, 0:HALF]))
+        scatter(0, 0)
+        last_product(0, 1, AV_BANK + 1)
+        empty_bank(0, 1, "product1")
+        scatter(0, 1)
+        copy_av_half(0)
+        for step in (square, root):
+            for c in (0, 1):
+                step(c)
+        last_product(0, 2, AV_BANK)
         empty_bank(0, 2, "product2")
-        v_and_factors = sbuf.tile([P, PACK * N], F32, name="plane_w3", align_bytes=ALIGN)
-        factors[1] = v_and_factors[:].rearrange("p (t n) -> p t n", t=PACK)
-        staged["v", 1, 0] = v_and_factors[:, PACK * HALF:].bitcast(BF16)
-        cast(nc.gpsimd, staged["v", 1, 0].rearrange("p (c t) -> p c t", t=PACK),
-             gathered["v"][:, :, N:2 * N].rearrange("p t c -> p c t"))
-        quantise("v", 1)
-
-        for t in range(LAST):
-            factor(1, t, wt_on_scalar=False)
-        factor(1, LAST, wt_on_scalar=True, q_squared_buffer="product3", inverse_buffer="stage_xm1_0")
+        scatter(0, 2)
+        for c in (0, 1):
+            inverse(c)
+            product(nc.gpsimd, c, staged["g", 1, 0])
+        last_product(0, LAST, AV_BANK + 1)
         empty_bank(0, LAST, "product3", 0, HALF)
-        interleave(nc.scalar, "xm", 1, rows["xm", 1])
-        for j in range(LAST):
-            scatter(0, j)
         scatter(0, LAST, 0, HALF)
-
-        stage("g", 1)
-        form_g(1)
-        quantise("xm", 1)
-        quantise("g", 1, E5M2)
-        empty_bank(0, LAST, "plane_w3", HALF, HALF)
+        copy_av_half(HALF)
+        quantise("g", 1, E5M2, first=0, count=HALF)
+        quantise("xm", 1, buffer="plane_v2", first=0, count=HALF)
+        empty_bank(0, LAST, "gathered_w", HALF, HALF)
         scatter(0, LAST, HALF, HALF)
-        free_banks = (0, 2, 3, AV_BANK)
+        staged["g", 1, HALF] = staged["xm", 1, 0]
+        square(2)
+        square(LAST, "early_product0")
+        root(2)
+        inverse(2)
+        product(nc.gpsimd, 2, staged["g", 1, HALF])
+        root(LAST)
+        last_product(1, 0, 0)
+        empty_bank(1, 0, "early_product0", 0, HALF)
+        inverse(LAST)
+        product(nc.gpsimd, LAST, staged["g", 1, HALF])
+        last_product(1, 1, 1)
+        empty_bank(1, 1, "rows_y0", 0, HALF)
+        cast(nc.scalar, interleaved_by_runs(staged["xm", 1, HALF]), by_runs(rows["xm", 1][:, :, HALF:]))
+        scatter(1, 0, 0, HALF)
+        quantise("g", 1, E5M2, first=HALF, count=HALF)
+        quantise("xm", 1, first=HALF, count=HALF)
+        scatter(1, 1, 0, HALF)
         for j in range(BLOCKS):
-            last_product(1, j, free_banks[j])
-            empty_bank(1, j, f"late_product{j}")
-            scatter(1, j)
+            first = HALF if j < EARLY else 0
+            last_product(1, j, (2, 3, 0, 1)[j])
+            empty_bank(1, j, f"late_product{j}", first, N - first)
+            scatter(1, j, first, N - first)
             nc.sync.dma_start(out[j * P:(j + 1) * P, :], windows[j][:])

@@ -23,7 +23,7 @@ BAND = 16
 HALF = N // 2
 BLOCKS = D // P
 ALIGN = 64
-EARLY = 2
+EARLY = 3
 AV_BANK = 4
 
 
@@ -32,6 +32,7 @@ def tile_attend_ghv_cau_kernel(tc, xT, wT, vT, y, wt, xm, offs, out):
     with ExitStack() as ctx:
         lists = ctx.enter_context(tc.tile_pool(name="lists", bufs=1))
         sbuf = ctx.enter_context(tc.tile_pool(name="sbuf", bufs=1))
+        placed = ctx.enter_context(tc.tile_pool(name="placed", bufs=1))
         psum = ctx.enter_context(tc.psum_pool(name="psum", bufs=1))
 
         offsets = lists.tile([P, B * N // BAND], U16, name="offsets")
@@ -244,17 +245,17 @@ def tile_attend_ghv_cau_kernel(tc, xT, wT, vT, y, wt, xm, offs, out):
         staged["xm_late", 0, 0] = staged["xm", 0, HALF]
         quantise("xm_late", 0, into=v_and_xm[:, N:], count=HALF)
 
-        last_product(0, 0, AV_BANK)
-        empty_bank(0, 0, "product0")
-        late = sbuf.tile([P, (BLOCKS + 1) * N], F32, name="stage_xm0_late", align_bytes=ALIGN)
-        q_blocks = [late[:, place * N:(place + 1) * N] for place in (0, 1, 2, BLOCKS)]
-        staged["xm", 1, 0] = late[:, LAST * N:BLOCKS * N].bitcast(BF16)
-        staged["xm", 1, HALF] = late[:, BLOCKS * N:].bitcast(BF16)
+        for j in (0, 1):
+            last_product(0, j, 2 + j)
+            empty_bank(0, j, f"product{j}")
+        late = sbuf.tile([P, (BLOCKS + 2) * N], F32, name="stage_xm0_late", align_bytes=ALIGN)
+        q_blocks = [late[:, c * N:(c + 1) * N] for c in range(BLOCKS)]
+        staged["xm", 1, 0] = late[:, BLOCKS * N:].bitcast(BF16)
         a_blocks = sbuf.tile([P, BLOCKS * N], F32, name="plane_v1", align_bytes=ALIGN)
         inverses = [sbuf.tile([P, N], F32, name=buffer, align_bytes=ALIGN)
                     for buffer in ("rows_x0", "plane_v2", "plane_v3", "stage_x0_0")]
-        weighted_av = {first: sbuf.tile([P, PACK, HALF], F32, name=buffer, align_bytes=ALIGN)
-                       for first, buffer in ((0, "gathered_w"), (HALF, "rows_y0"))}
+        inverses[1] = placed.tile([P, N], F32, name="inverse1", align_bytes=ALIGN, offset=4 * HALF)
+        weighted_av = sbuf.tile([P, PACK, N], F32, name="rows_y0", align_bytes=ALIGN)
         stage("g", 1, buffer="stage_g1_0", count=HALF)
 
         def as_planes(block):
@@ -270,15 +271,18 @@ def tile_attend_ghv_cau_kernel(tc, xT, wT, vT, y, wt, xm, offs, out):
             bank = psum.tile([P, PACK, P], F32, name=f"bank{c}")
             for t in range(PACK):
                 multiply(bank[:, t, :], 1, "x", t, "w", slice(c * P, (c + 1) * P))
-            a_block = a_blocks[:, c * N:(c + 1) * N]
-            nc.scalar.activation(a_block, bank[:].rearrange("p t i -> p (t i)"), ACT.Copy)
-            nc.gpsimd.tensor_tensor(as_planes(q_blocks[c]), as_planes(a_block), targets[1][:, :, c * P:(c + 1) * P],
-                                    ALU.subtract)
+            y_block = targets[1][:, :, c * P:(c + 1) * P]
+            if c == 0:
+                nc.vector.tensor_tensor(as_planes(q_blocks[c]), bank[:], y_block, ALU.subtract)
+            else:
+                a_block = a_blocks[:, c * N:(c + 1) * N]
+                nc.scalar.activation(a_block, bank[:].rearrange("p t i -> p (t i)"), ACT.Copy)
+                nc.gpsimd.tensor_tensor(as_planes(q_blocks[c]), as_planes(a_block), y_block, ALU.subtract)
 
         squares = {}
 
-        def square(c, buffer=None):
-            squares[c] = through(buffer, q_blocks[c])
+        def square(c):
+            squares[c] = q_blocks[min(c, LAST - c)]
             nc.scalar.activation(squares[c], q_blocks[c], ACT.Square)
 
         def root(c):
@@ -289,63 +293,58 @@ def tile_attend_ghv_cau_kernel(tc, xT, wT, vT, y, wt, xm, offs, out):
 
         def product(engine, c, half):
             engine.tensor_tensor(as_items(half[:, PACK * (c % 2) * P:PACK * (c % 2 + 1) * P]),
-                                 by_items(weighted_av[c // 2 * HALF][:, :, c % 2 * P:(c % 2 + 1) * P]), as_items(inverses[c][:]), ALU.mult)
+                                 by_items(weighted_av[:, :, c * P:(c + 1) * P]), as_items(inverses[c][:]), ALU.mult)
 
-        def copy_av_half(first):
-            items = slice(first, first + HALF)
-            for pair in range(PACK // 2):
-                bank = psum.tile([P, 2, HALF], F32, name=f"bank{AV_BANK + 2 + pair}")
-                for t in (2 * pair, 2 * pair + 1):
-                    multiply(bank[:, t % 2, :], 1, "x", t, "v", items)
-                for t in (2 * pair, 2 * pair + 1):
-                    nc.scalar.activation(weighted_av[first][:, t, :], bank[:, t % 2, :], ACT.Copy, scale=wt_sb[:, 1, t:t + 1])
+        def copy_av(t):
+            bank = psum.tile([P, N], F32, name=f"bank{AV_BANK + 2 + t % 2}")
+            multiply(bank[:], 1, "x", t, "v")
+            nc.scalar.activation(weighted_av[:, t, :], bank[:], ACT.Copy, scale=wt_sb[:, 1, t:t + 1])
 
         for c in range(BLOCKS):
             residual_block(c)
-        cast(nc.gpsimd, as_items(staged["xm", 1, 0]), by_items(rows["xm", 1][:, :, 0:HALF]))
+        cast(nc.gpsimd, as_items(staged["xm", 1, 0]), by_items(rows["xm", 1]))
         scatter(0, 0)
-        last_product(0, 1, AV_BANK + 1)
-        empty_bank(0, 1, "product1")
         scatter(0, 1)
-        copy_av_half(0)
-        for step in (square, root):
-            for c in (0, 1):
-                step(c)
+        for t in range(PACK):
+            copy_av(t)
+        for c in (0, 1):
+            square(c)
+        root(0)
         last_product(0, 2, AV_BANK)
         empty_bank(0, 2, "product2")
         scatter(0, 2)
-        for c in (0, 1):
-            inverse(c)
-            product(nc.gpsimd, c, staged["g", 1, 0])
+        inverse(0)
+        product(nc.gpsimd, 0, staged["g", 1, 0])
+        root(1)
+        inverse(1)
+        product(nc.gpsimd, 1, staged["g", 1, 0])
         last_product(0, LAST, AV_BANK + 1)
         empty_bank(0, LAST, "product3", 0, HALF)
         scatter(0, LAST, 0, HALF)
-        copy_av_half(HALF)
         quantise("g", 1, E5M2, first=0, count=HALF)
-        quantise("xm", 1, buffer="plane_v2", first=0, count=HALF)
-        empty_bank(0, LAST, "gathered_w", HALF, HALF)
+        quantise("xm", 1, into=placed.tile([P, N], U32, name="codes_xm1", align_bytes=ALIGN, offset=0))
+        products[0, LAST, HALF] = placed.tile([P, HALF], F32, name="product3_second", align_bytes=ALIGN, offset=4 * N)
+        nc.scalar.activation(products[0, LAST, HALF][:], banks[0, LAST][:, HALF:], ACT.Copy)
         scatter(0, LAST, HALF, HALF)
-        staged["g", 1, HALF] = staged["xm", 1, 0]
-        square(2)
-        square(LAST, "early_product0")
-        root(2)
-        inverse(2)
-        product(nc.gpsimd, 2, staged["g", 1, HALF])
-        root(LAST)
-        last_product(1, 0, 0)
-        empty_bank(1, 0, "early_product0", 0, HALF)
-        inverse(LAST)
-        product(nc.gpsimd, LAST, staged["g", 1, HALF])
-        last_product(1, 1, 1)
-        empty_bank(1, 1, "rows_y0", 0, HALF)
-        cast(nc.scalar, interleaved_by_runs(staged["xm", 1, HALF]), by_runs(rows["xm", 1][:, :, HALF:]))
-        scatter(1, 0, 0, HALF)
+        staged["g", 1, HALF] = staged["xm", 1, 0][:, 0:PACK * HALF]
+        for step in (square, root):
+            for c in (2, 3):
+                step(c)
+        for c in (2, 3):
+            inverse(c)
+            product(nc.gpsimd, c, staged["g", 1, HALF])
+        for j in (0, 1):
+            last_product(1, j, j)
+            products[1, j, 0] = q_blocks[LAST][:, j * HALF:(j + 1) * HALF]
+            nc.scalar.activation(products[1, j, 0], banks[1, j][:, 0:HALF], ACT.Copy)
+            scatter(1, j, 0, HALF)
+        last_product(1, 2, 2)
+        empty_bank(1, 2, "rows_y0", 0, HALF)
         quantise("g", 1, E5M2, first=HALF, count=HALF)
-        quantise("xm", 1, first=HALF, count=HALF)
-        scatter(1, 1, 0, HALF)
+        scatter(1, 2, 0, HALF)
         for j in range(BLOCKS):
             first = HALF if j < EARLY else 0
-            last_product(1, j, (2, 3, 0, 1)[j])
+            last_product(1, j, (3, 4, 0, 3)[j])
             empty_bank(1, j, f"late_product{j}", first, N - first)
             scatter(1, j, first, N - first)
             nc.sync.dma_start(out[j * P:(j + 1) * P, :], windows[j][:])

@@ -233,9 +233,12 @@ def tile_attend_ghv_cau_kernel(tc, xT, wT, vT, y, wt, xm, offs, out):
         gather_group("v", LAST, 1)
         form_g(0, stage("g", 0), range(BLOCKS))
         interleave(nc.gpsimd, "xm", 0, rows["xm", 0], buffer=f"stage_v0_{HALF}", first=0, count=HALF)
-        interleave(nc.gpsimd, "v", 1, gathered["v"][:, :, N:2 * N])
+        staged_v1 = stage("v", 1)[:]
+        cast(nc.gpsimd, staged_v1[:, 0:PACK * LAST * P].rearrange("p (c t) -> p c t", t=PACK),
+             gathered["v"][:, :, N:N + LAST * P].rearrange("p t c -> p c t"))
         interleave_x(nc.scalar, 1)
         interleave(nc.scalar, "xm", 0, rows["xm", 0], buffer="stage_xm0_late", first=HALF, count=HALF)
+        cast(nc.scalar, interleaved_by_runs(staged_v1[:, PACK * LAST * P:]), by_runs(gathered["v"][:, :, N + LAST * P:]))
         x_and_xm = sbuf.tile([P, N + HALF], U32, name="a_sb", align_bytes=ALIGN)
         quantise("x", 1, into=x_and_xm[:, 0:N])
         quantise("xm", 0, into=x_and_xm[:, N:], first=0, count=HALF)

@@ -207,7 +207,10 @@ def tile_attend_ghv_cau_kernel(tc, xT, wT, vT, y, wt, xm, offs, out):
         gather_group("v", LAST, 0)
 
         rows["xm", 0] = load_rows(xm, 0, "plane_w0")
-        rows["x", 1] = load_rows(xT, 1, "plane_w1")
+        v_and_x = sbuf.tile([P, 2 * LAST * P + PACK * R], F32, name="plane_w1", align_bytes=ALIGN)
+        staged["v", 1, 0] = v_and_x[:, 0:2 * N].bitcast(BF16)
+        rows["x", 1] = v_and_x[:, 2 * LAST * P:].rearrange("p (t c) -> p t c", t=PACK)
+        nc.sync.dma_start(rows["x", 1], xT[1].rearrange("(p t) c -> p t c", t=PACK))
         targets[1] = load_rows(y, 1, "plane_w3")
         rows["xm", 1] = load_rows(xm, 1, "plane_w2")
 
@@ -233,7 +236,7 @@ def tile_attend_ghv_cau_kernel(tc, xT, wT, vT, y, wt, xm, offs, out):
         gather_group("v", LAST, 1)
         form_g(0, stage("g", 0), range(BLOCKS))
         interleave(nc.gpsimd, "xm", 0, rows["xm", 0], buffer=f"stage_v0_{HALF}", first=0, count=HALF)
-        staged_v1 = stage("v", 1)[:]
+        staged_v1 = staged["v", 1, 0]
         cast(nc.gpsimd, staged_v1[:, 0:PACK * LAST * P].rearrange("p (c t) -> p c t", t=PACK),
              gathered["v"][:, :, N:N + LAST * P].rearrange("p t c -> p c t"))
         interleave_x(nc.scalar, 1)

@@ -23,6 +23,7 @@ BAND = 16
 HALF = N // 2
 BLOCKS = D // P
 ALIGN = 64
+X_OFFSET = 6 * N
 EARLY = 3
 AV_BANK = 4
 
@@ -73,10 +74,10 @@ def tile_attend_ghv_cau_kernel(tc, xT, wT, vT, y, wt, xm, offs, out):
         nc.scalar.dma_start(wt_sb[:], wt.rearrange("b (p t) o -> p b (t o)", t=PACK))
         targets[0] = sbuf.tile([P, PACK, N], F32, name="rows_y0", align_bytes=ALIGN)[:]
         for t in range(PACK):
-            load_plane("v", vT, t)
             if t < PACK // 2:
                 planes = slice(2 * t, 2 * t + 2)
                 nc.sync.dma_start(targets[0][:, planes, :], y[0].rearrange("(p t) n -> p t n", t=PACK)[:, planes, :])
+            load_plane("v", vT, t)
 
         a_sb = {}
         residuals = {}
@@ -122,15 +123,16 @@ def tile_attend_ghv_cau_kernel(tc, xT, wT, vT, y, wt, xm, offs, out):
                 cast(engine, interleaved_by_runs(dst), by_runs(src))
 
         def interleave_x(engine, b):
-            cast(engine, stage("x", b)[:].rearrange("p (t m j) -> p m j t", t=PACK, j=PACK),
+            cast(engine, staged["x", b, 0][:].rearrange("p (t m j) -> p m j t", t=PACK, j=PACK),
                  rows["x", b].rearrange("p j (m t) -> p m j t", t=PACK))
 
-        def quantise(name, b, fmt=E4M3, buffer=None, first=0, count=N, into=None):
+        def quantise(name, b, fmt=E4M3, buffer=None, first=0, count=N, into=None, scales_buffer=None):
             if (name, b) not in codes:
                 if into is None:
                     into = sbuf.tile([P, N], U32, name=buffer or f"codes_{name}{b}", align_bytes=ALIGN)
                 codes[name, b] = into
-                scales[name, b] = sbuf.tile([P, N], U8, name=f"scales_{name}{b}", align_bytes=ALIGN)
+                if (name, b) not in scales:
+                    scales[name, b] = sbuf.tile([P, N], U8, name=scales_buffer or f"scales_{name}{b}", align_bytes=ALIGN)
             columns = slice(first, first + count)
             nc.vector.quantize_mx(out=codes[name, b][:, columns].bitcast(fmt), scales=scales[name, b][:, columns],
                                   in_=staged[name, b, first][:])
@@ -216,6 +218,7 @@ def tile_attend_ghv_cau_kernel(tc, xT, wT, vT, y, wt, xm, offs, out):
 
         interleave(nc.scalar, "w", 0, gathered["w"][:, :, 0:N])
         cast(nc.scalar, interleaved_by_runs(staged["w", 1, 0][:])[:, :, 2:, :], by_runs(gathered["w"][:, 2:, N:2 * N]))
+        stage("x", 0)
         interleave_x(nc.vector, 0)
         quantise("w", 0)
         quantise("x", 0)
@@ -223,9 +226,9 @@ def tile_attend_ghv_cau_kernel(tc, xT, wT, vT, y, wt, xm, offs, out):
         a_sb[0] = sbuf.tile([P, PACK, N], F32, name="a_sb", align_bytes=ALIGN)
         residuals[0] = [targets[0][:, t, :] for t in range(PACK)]
         for t in range(PACK):
-            residual(0, t, on_vector=t == 0)
+            residual(0, t, on_vector=t == LAST)
         factors[0] = sbuf.tile([P, PACK, N], F32, name="a_sb", align_bytes=ALIGN)[:]
-        for t in range(PACK):
+        for t in (0, 1, 3, 2):
             factor(0, t, wt_on_scalar=t >= PACK // 2)
 
         staged["v", 0, 0] = gathered_v[:, PACK * B * N - N:].bitcast(BF16)
@@ -239,23 +242,30 @@ def tile_attend_ghv_cau_kernel(tc, xT, wT, vT, y, wt, xm, offs, out):
         staged_v1 = staged["v", 1, 0]
         cast(nc.gpsimd, staged_v1[:, 0:PACK * LAST * P].rearrange("p (c t) -> p c t", t=PACK),
              gathered["v"][:, :, N:N + LAST * P].rearrange("p t c -> p c t"))
+        staged["x", 1, 0] = placed.tile([P, PACK * N], BF16, name="stage_x1", align_bytes=ALIGN, offset=X_OFFSET)
         interleave_x(nc.scalar, 1)
         interleave(nc.scalar, "xm", 0, rows["xm", 0], buffer="stage_xm0_late", first=HALF, count=HALF)
         cast(nc.scalar, interleaved_by_runs(staged_v1[:, PACK * LAST * P:]), by_runs(gathered["v"][:, :, N + LAST * P:]))
-        x_and_xm = sbuf.tile([P, N + HALF], U32, name="a_sb", align_bytes=ALIGN)
-        quantise("x", 1, into=x_and_xm[:, 0:N])
-        quantise("xm", 0, into=x_and_xm[:, N:], first=0, count=HALF)
-        quantise("g", 0, E5M2, buffer="stage_x1_0")
-        v_and_xm = sbuf.tile([P, N + HALF], U32, name="stage_g0_0", align_bytes=ALIGN)
-        quantise("v", 1, into=v_and_xm[:, 0:N])
+        quantise("xm", 0, buffer="codes_v0", first=0, count=HALF)
+        quantise("g", 0, E5M2, buffer="stage_w0_0")
+        quantise("x", 1, buffer="codes_x0")
+        quantise("v", 1, scales_buffer="scales_x0")
         staged["xm_late", 0, 0] = staged["xm", 0, HALF]
-        quantise("xm_late", 0, into=v_and_xm[:, N:], count=HALF)
+        scales["xm_late", 0] = placed.tile([P, N], U8, name="scales_xm_late", align_bytes=ALIGN, offset=X_OFFSET + 4 * N)
+        quantise("xm_late", 0, count=HALF)
+        q_first = sbuf.tile([P, N], F32, name="stage_g0_0", align_bytes=ALIGN)
 
-        for j in (0, 1):
-            last_product(0, j, 2 + j)
-            empty_bank(0, j, f"product{j}")
+        first_products = [placed.tile([P, N], F32, name="product0", align_bytes=ALIGN, offset=X_OFFSET),
+                          sbuf.tile([P, N], F32, name="product1", align_bytes=ALIGN)]
+
+        def first_product(j, bank_number):
+            last_product(0, j, bank_number)
+            products[0, j, 0] = first_products[j][:]
+            nc.scalar.activation(products[0, j, 0], banks[0, j][:], ACT.Copy)
+
+        first_product(0, 2)
         late = sbuf.tile([P, (BLOCKS + 2) * N], F32, name="stage_xm0_late", align_bytes=ALIGN)
-        q_blocks = [late[:, c * N:(c + 1) * N] for c in range(BLOCKS)]
+        q_blocks = [q_first[:]] + [late[:, c * N:(c + 1) * N] for c in range(1, BLOCKS)]
         staged["xm", 1, 0] = late[:, BLOCKS * N:].bitcast(BF16)
         a_blocks = sbuf.tile([P, BLOCKS * N], F32, name="plane_v1", align_bytes=ALIGN)
         inverses = [sbuf.tile([P, N], F32, name=buffer, align_bytes=ALIGN)
@@ -295,7 +305,7 @@ def tile_attend_ghv_cau_kernel(tc, xT, wT, vT, y, wt, xm, offs, out):
             nc.scalar.activation(q_blocks[c], squares[c], ACT.Abs_reciprocal_sqrt, bias=one[:])
 
         def inverse(c):
-            nc.scalar.activation(as_items(inverses[c][:]), by_items(as_planes(q_blocks[c])), ACT.Square)
+            nc.scalar.activation(interleaved_by_runs(inverses[c][:]), by_runs(as_planes(q_blocks[c])), ACT.Square)
 
         def product(engine, c, half):
             engine.tensor_tensor(as_items(half[:, PACK * (c % 2) * P:PACK * (c % 2 + 1) * P]),
@@ -306,7 +316,9 @@ def tile_attend_ghv_cau_kernel(tc, xT, wT, vT, y, wt, xm, offs, out):
             multiply(bank[:], 1, "x", t, "v")
             nc.scalar.activation(weighted_av[:, t, :], bank[:], ACT.Copy, scale=wt_sb[:, 1, t:t + 1])
 
-        for c in range(BLOCKS):
+        residual_block(0)
+        first_product(1, 0)
+        for c in range(1, BLOCKS):
             residual_block(c)
         cast(nc.gpsimd, as_items(staged["xm", 1, 0]), by_items(rows["xm", 1]))
         scatter(0, 0)

@@ -24,6 +24,7 @@ HALF = N // 2
 BLOCKS = D // P
 ALIGN = 64
 X_OFFSET = 6 * N
+ON_VECTOR = 2
 EARLY = 3
 AV_BANK = 4
 
@@ -91,9 +92,10 @@ def tile_attend_ghv_cau_kernel(tc, xT, wT, vT, y, wt, xm, offs, out):
         def gather_both(name, t):
             nc.vector.tensor_copy(gathered[name][:, t, :], table_planes[name, t][:].indirect(offsets[:]))
 
-        def gather_group(name, t, b):
-            nc.vector.tensor_copy(gathered[name][:, t, b * N:(b + 1) * N],
-                                  table_planes[name, t][:].indirect(list_part(b * N, N)))
+        def gather_group(name, t, b, first=0, count=N):
+            start = b * N + first
+            nc.vector.tensor_copy(gathered[name][:, t, start:start + count],
+                                  table_planes[name, t][:].indirect(list_part(start, count)))
 
         def stage(name, b, buffer=None, first=0, count=N):
             staged[name, b, first] = sbuf.tile([P, PACK * count], BF16, name=buffer or f"stage_{name}{b}_{first}",
@@ -126,13 +128,13 @@ def tile_attend_ghv_cau_kernel(tc, xT, wT, vT, y, wt, xm, offs, out):
             cast(engine, staged["x", b, 0][:].rearrange("p (t m j) -> p m j t", t=PACK, j=PACK),
                  rows["x", b].rearrange("p j (m t) -> p m j t", t=PACK))
 
-        def quantise(name, b, fmt=E4M3, buffer=None, first=0, count=N, into=None, scales_buffer=None):
+        def quantise(name, b, fmt=E4M3, buffer=None, first=0, count=N, into=None):
             if (name, b) not in codes:
                 if into is None:
                     into = sbuf.tile([P, N], U32, name=buffer or f"codes_{name}{b}", align_bytes=ALIGN)
                 codes[name, b] = into
                 if (name, b) not in scales:
-                    scales[name, b] = sbuf.tile([P, N], U8, name=scales_buffer or f"scales_{name}{b}", align_bytes=ALIGN)
+                    scales[name, b] = sbuf.tile([P, N], U8, name=f"scales_{name}{b}", align_bytes=ALIGN)
             columns = slice(first, first + count)
             nc.vector.quantize_mx(out=codes[name, b][:, columns].bitcast(fmt), scales=scales[name, b][:, columns],
                                   in_=staged[name, b, first][:])
@@ -152,20 +154,15 @@ def tile_attend_ghv_cau_kernel(tc, xT, wT, vT, y, wt, xm, offs, out):
                 nc.scalar.activation(a_sb[b][:, t, :], bank[:], ACT.Copy)
                 nc.gpsimd.tensor_tensor(residuals[b][t], a_sb[b][:, t, :], targets[b][:, t, :], ALU.subtract)
 
-        def through(buffer, plane):
-            return sbuf.tile([P, N], F32, name=buffer, align_bytes=ALIGN)[:] if buffer else plane
-
-        def factor(b, t, wt_on_scalar, q_squared_buffer=None, inverse_buffer=None):
+        def factor(b, t, wt_on_scalar):
             plane = residuals[b][t]
-            q_squared = through(q_squared_buffer, plane)
-            nc.scalar.activation(q_squared, plane, ACT.Square)
-            nc.scalar.activation(plane, q_squared, ACT.Abs_reciprocal_sqrt, bias=one[:])
-            inverse = through(inverse_buffer, plane)
-            nc.scalar.activation(inverse, plane, ACT.Square)
+            nc.scalar.activation(plane, plane, ACT.Square)
+            nc.scalar.activation(plane, plane, ACT.Abs_reciprocal_sqrt, bias=one[:])
+            nc.scalar.activation(plane, plane, ACT.Square)
             if wt_on_scalar:
-                nc.scalar.activation(factors[b][:, t, :], inverse, ACT.Copy, scale=wt_sb[:, b, t:t + 1])
+                nc.scalar.activation(factors[b][:, t, :], plane, ACT.Copy, scale=wt_sb[:, b, t:t + 1])
             else:
-                nc.gpsimd.tensor_scalar(factors[b][:, t, :], inverse, wt_sb[:, b, t:t + 1], 0.0, ALU.mult, ALU.add)
+                nc.gpsimd.tensor_scalar(factors[b][:, t, :], plane, wt_sb[:, b, t:t + 1], 0.0, ALU.mult, ALU.add)
 
         def form_g(b, g, blocks):
             for c in blocks:
@@ -196,7 +193,7 @@ def tile_attend_ghv_cau_kernel(tc, xT, wT, vT, y, wt, xm, offs, out):
         nc.gpsimd.memset(scales["g", 1][:, HALF:].bitcast(U32), 0)
 
         words_w1 = stage("w", 1)[:].rearrange("p (c t) -> p c t", t=PACK)
-        for t, buffer in enumerate(("stage_x1_0", "stage_g1_0")):
+        for t, buffer in enumerate(("rounded_w0", "stage_g1_0")):
             gather_group("w", t, 0)
             rounded = sbuf.tile([P, T], BF16, name=buffer, align_bytes=ALIGN)
             nc.scalar.activation(rounded[:], table_planes["w", t][:], ACT.Copy)
@@ -206,7 +203,8 @@ def tile_attend_ghv_cau_kernel(tc, xT, wT, vT, y, wt, xm, offs, out):
             gather_group("w", LAST, b)
         for t in range(LAST):
             gather_both("v", t)
-        gather_group("v", LAST, 0)
+        for first in (0, HALF):
+            gather_group("v", LAST, 0, first, HALF)
 
         rows["xm", 0] = load_rows(xm, 0, "plane_w0")
         v_and_x = sbuf.tile([P, 2 * LAST * P + PACK * R], F32, name="plane_w1", align_bytes=ALIGN)
@@ -228,7 +226,7 @@ def tile_attend_ghv_cau_kernel(tc, xT, wT, vT, y, wt, xm, offs, out):
         for t in range(PACK):
             residual(0, t, on_vector=t == LAST)
         factors[0] = sbuf.tile([P, PACK, N], F32, name="a_sb", align_bytes=ALIGN)[:]
-        for t in (0, 1, 3, 2):
+        for t in (0, 1, LAST, 2):
             factor(0, t, wt_on_scalar=t >= PACK // 2)
 
         staged["v", 0, 0] = gathered_v[:, PACK * B * N - N:].bitcast(BF16)
@@ -244,16 +242,16 @@ def tile_attend_ghv_cau_kernel(tc, xT, wT, vT, y, wt, xm, offs, out):
              gathered["v"][:, :, N:N + LAST * P].rearrange("p t c -> p c t"))
         staged["x", 1, 0] = placed.tile([P, PACK * N], BF16, name="stage_x1", align_bytes=ALIGN, offset=X_OFFSET)
         interleave_x(nc.scalar, 1)
-        interleave(nc.scalar, "xm", 0, rows["xm", 0], buffer="stage_xm0_late", first=HALF, count=HALF)
-        cast(nc.scalar, interleaved_by_runs(staged_v1[:, PACK * LAST * P:]), by_runs(gathered["v"][:, :, N + LAST * P:]))
+        interleave(nc.scalar, "xm", 0, rows["xm", 0], first=HALF, count=HALF)
         quantise("xm", 0, buffer="codes_v0", first=0, count=HALF)
         quantise("g", 0, E5M2, buffer="stage_w0_0")
         quantise("x", 1, buffer="codes_x0")
-        quantise("v", 1, scales_buffer="scales_x0")
+        cast(nc.vector, interleaved_by_runs(staged_v1[:, PACK * LAST * P:]), by_runs(gathered["v"][:, :, N + LAST * P:]))
         staged["xm_late", 0, 0] = staged["xm", 0, HALF]
         scales["xm_late", 0] = placed.tile([P, N], U8, name="scales_xm_late", align_bytes=ALIGN, offset=X_OFFSET + 4 * N)
         quantise("xm_late", 0, count=HALF)
-        q_first = sbuf.tile([P, N], F32, name="stage_g0_0", align_bytes=ALIGN)
+        quantise("v", 1)
+        q_first = sbuf.tile([P, ON_VECTOR * N], F32, name="stage_g0_0", align_bytes=ALIGN)
 
         first_products = [placed.tile([P, N], F32, name="product0", align_bytes=ALIGN, offset=X_OFFSET),
                           sbuf.tile([P, N], F32, name="product1", align_bytes=ALIGN)]
@@ -264,12 +262,13 @@ def tile_attend_ghv_cau_kernel(tc, xT, wT, vT, y, wt, xm, offs, out):
             nc.scalar.activation(products[0, j, 0], banks[0, j][:], ACT.Copy)
 
         first_product(0, 2)
-        late = sbuf.tile([P, (BLOCKS + 2) * N], F32, name="stage_xm0_late", align_bytes=ALIGN)
-        q_blocks = [q_first[:]] + [late[:, c * N:(c + 1) * N] for c in range(1, BLOCKS)]
-        staged["xm", 1, 0] = late[:, BLOCKS * N:].bitcast(BF16)
+        late = sbuf.tile([P, (BLOCKS - ON_VECTOR + 2) * N], F32, name="plane_w1", align_bytes=ALIGN)
+        q_blocks = ([q_first[:, c * N:(c + 1) * N] for c in range(ON_VECTOR)]
+                    + [late[:, c * N:(c + 1) * N] for c in range(BLOCKS - ON_VECTOR)])
+        staged["xm", 1, 0] = late[:, (BLOCKS - ON_VECTOR) * N:].bitcast(BF16)
         a_blocks = sbuf.tile([P, BLOCKS * N], F32, name="plane_v1", align_bytes=ALIGN)
-        inverses = [sbuf.tile([P, N], F32, name=buffer, align_bytes=ALIGN)
-                    for buffer in ("rows_x0", "plane_v2", "plane_v3", "stage_x0_0")]
+        inverses = {c: sbuf.tile([P, N], F32, name=buffer, align_bytes=ALIGN)
+                    for c, buffer in ((0, "rows_x0"), (2, "plane_v3"), (3, "stage_x0_0"))}
         inverses[1] = placed.tile([P, N], F32, name="inverse1", align_bytes=ALIGN, offset=4 * HALF)
         weighted_av = sbuf.tile([P, PACK, N], F32, name="rows_y0", align_bytes=ALIGN)
         stage("g", 1, buffer="stage_g1_0", count=HALF)
@@ -288,7 +287,7 @@ def tile_attend_ghv_cau_kernel(tc, xT, wT, vT, y, wt, xm, offs, out):
             for t in range(PACK):
                 multiply(bank[:, t, :], 1, "x", t, "w", slice(c * P, (c + 1) * P))
             y_block = targets[1][:, :, c * P:(c + 1) * P]
-            if c == 0:
+            if c < ON_VECTOR:
                 nc.vector.tensor_tensor(as_planes(q_blocks[c]), bank[:], y_block, ALU.subtract)
             else:
                 a_block = a_blocks[:, c * N:(c + 1) * N]
@@ -307,9 +306,9 @@ def tile_attend_ghv_cau_kernel(tc, xT, wT, vT, y, wt, xm, offs, out):
         def inverse(c):
             nc.scalar.activation(interleaved_by_runs(inverses[c][:]), by_runs(as_planes(q_blocks[c])), ACT.Square)
 
-        def product(engine, c, half):
-            engine.tensor_tensor(as_items(half[:, PACK * (c % 2) * P:PACK * (c % 2 + 1) * P]),
-                                 by_items(weighted_av[:, :, c * P:(c + 1) * P]), as_items(inverses[c][:]), ALU.mult)
+        def product(c, half):
+            nc.gpsimd.tensor_tensor(as_items(half[:, PACK * (c % 2) * P:PACK * (c % 2 + 1) * P]),
+                                    by_items(weighted_av[:, :, c * P:(c + 1) * P]), as_items(inverses[c][:]), ALU.mult)
 
         def copy_av(t):
             bank = psum.tile([P, N], F32, name=f"bank{AV_BANK + 2 + t % 2}")
@@ -332,10 +331,10 @@ def tile_attend_ghv_cau_kernel(tc, xT, wT, vT, y, wt, xm, offs, out):
         empty_bank(0, 2, "product2")
         scatter(0, 2)
         inverse(0)
-        product(nc.gpsimd, 0, staged["g", 1, 0])
+        product(0, staged["g", 1, 0])
         root(1)
         inverse(1)
-        product(nc.gpsimd, 1, staged["g", 1, 0])
+        product(1, staged["g", 1, 0])
         last_product(0, LAST, AV_BANK + 1)
         empty_bank(0, LAST, "product3", 0, HALF)
         scatter(0, LAST, 0, HALF)
@@ -350,7 +349,7 @@ def tile_attend_ghv_cau_kernel(tc, xT, wT, vT, y, wt, xm, offs, out):
                 step(c)
         for c in (2, 3):
             inverse(c)
-            product(nc.gpsimd, c, staged["g", 1, HALF])
+            product(c, staged["g", 1, HALF])
         for j in (0, 1):
             last_product(1, j, j)
             products[1, j, 0] = q_blocks[LAST][:, j * HALF:(j + 1) * HALF]

@@ -23,10 +23,6 @@ BAND = 16
 HALF = N // 2
 BLOCKS = D // P
 ALIGN = 64
-X_OFFSET = 6 * N
-ON_VECTOR = 2
-EARLY = 3
-AV_BANK = 4
 
 
 def tile_attend_ghv_cau_kernel(tc, xT, wT, vT, y, wt, xm, offs, out):
@@ -34,7 +30,6 @@ def tile_attend_ghv_cau_kernel(tc, xT, wT, vT, y, wt, xm, offs, out):
     with ExitStack() as ctx:
         lists = ctx.enter_context(tc.tile_pool(name="lists", bufs=1))
         sbuf = ctx.enter_context(tc.tile_pool(name="sbuf", bufs=1))
-        placed = ctx.enter_context(tc.tile_pool(name="placed", bufs=1))
         psum = ctx.enter_context(tc.psum_pool(name="psum", bufs=1))
 
         offsets = lists.tile([P, B * N // BAND], U16, name="offsets")
@@ -42,67 +37,43 @@ def tile_attend_ghv_cau_kernel(tc, xT, wT, vT, y, wt, xm, offs, out):
         def list_part(first, count):
             return offsets[:, first // BAND:(first + count) // BAND]
 
-        one = sbuf.tile([P, 1], F32, name="one")
+        def tile(shape, dtype, name):
+            return sbuf.tile(shape, dtype, name=name, align_bytes=ALIGN)
+
+        one = tile([P, 1], F32, "one")
         nc.vector.memset(one[:], 1.0)
         nc.scalar.activation(one[:], one[:], ACT.Abs_reciprocal_sqrt)
 
-        windows = [sbuf.tile([P, T], F32, name=f"window{j}") for j in range(BLOCKS)]
+        windows = [tile([P, T], F32, f"window{j}") for j in range(BLOCKS)]
         for window in windows:
             nc.gpsimd.memset(window[:], 0.0)
 
         table_planes = {}
         rows = {}
-        targets = {}
-        gathered = {"w": sbuf.tile([P, PACK, B * N], F32, name="gathered_w", align_bytes=ALIGN)[:]}
-        gathered_v = sbuf.tile([P, PACK * B * N], F32, name="gathered_v", align_bytes=ALIGN)
-        gathered["v"] = gathered_v[:].rearrange("p (t n) -> p t n", t=PACK)
-        wt_sb = sbuf.tile([P, B, PACK], F32, name="wt_sb")
-
-        def load_plane(name, table, t):
-            table_planes[name, t] = sbuf.tile([P, T], F32, name=f"plane_{name}{t}", align_bytes=ALIGN)
-            nc.sync.dma_start(table_planes[name, t][:], table.rearrange("(p t) n -> p t n", t=PACK)[:, t, :])
-
-        def load_rows(source, b, buffer):
-            loaded = sbuf.tile([P, PACK, source.shape[2]], F32, name=buffer, align_bytes=ALIGN)
-            nc.sync.dma_start(loaded[:], source[b].rearrange("(p t) c -> p t c", t=PACK))
-            return loaded[:]
-
-        for t in range(PACK):
-            load_plane("w", wT, t)
-            if t == 0:
-                nc.sync.dma_start(offsets[:], offs)
-        rows["x", 0] = load_rows(xT, 0, "rows_x0")
-        nc.scalar.dma_start(wt_sb[:], wt.rearrange("b (p t) o -> p b (t o)", t=PACK))
-        targets[0] = sbuf.tile([P, PACK, N], F32, name="rows_y0", align_bytes=ALIGN)[:]
-        for t in range(PACK):
-            if t < PACK // 2:
-                planes = slice(2 * t, 2 * t + 2)
-                nc.sync.dma_start(targets[0][:, planes, :], y[0].rearrange("(p t) n -> p t n", t=PACK)[:, planes, :])
-            load_plane("v", vT, t)
-
-        a_sb = {}
-        residuals = {}
-        factors = {}
+        gathered = {(name, b): tile([P, PACK, N], F32, f"gathered_{name}{b}") for name in "wv" for b in range(B)}
+        wt_sb = tile([P, B, PACK], F32, "wt_sb")
         staged = {}
         codes = {}
         scales = {}
-        banks = {}
         products = {}
 
-        def gather_both(name, t):
-            nc.vector.tensor_copy(gathered[name][:, t, :], table_planes[name, t][:].indirect(offsets[:]))
+        def by_planes(source):
+            return source.rearrange("(p t) c -> p t c", t=PACK)
 
-        def gather_group(name, t, b, first=0, count=N):
-            start = b * N + first
-            nc.vector.tensor_copy(gathered[name][:, t, start:start + count],
-                                  table_planes[name, t][:].indirect(list_part(start, count)))
+        def load_plane(name, table, t):
+            table_planes[name, t] = tile([P, T], F32, f"plane_{name}{t}")
+            nc.sync.dma_start(table_planes[name, t][:], by_planes(table)[:, t, :])
 
-        def stage(name, b, buffer=None, first=0, count=N):
-            staged[name, b, first] = sbuf.tile([P, PACK * count], BF16, name=buffer or f"stage_{name}{b}_{first}",
-                                               align_bytes=ALIGN)
-            return staged[name, b, first]
+        def load_rows(name, source, b, buffer, first=0, count=N):
+            rows[name, b, first] = tile([P, PACK, count], F32, buffer)
+            nc.sync.dma_start(rows[name, b, first][:], by_planes(source[b])[:, :, first:first + count])
 
-        def cast(engine, dst, src):
+        def load_targets(b):
+            rows["y", b, 0] = tile([P, PACK, N], F32, f"rows_y{b}")
+            for planes in (slice(0, 2), slice(2, PACK)):
+                nc.sync.dma_start(rows["y", b, 0][:, planes, :], by_planes(y[b])[:, planes, :])
+
+        def move(engine, dst, src):
             if engine is nc.scalar:
                 nc.scalar.activation(dst, src, ACT.Copy)
             elif engine is nc.gpsimd:
@@ -110,31 +81,35 @@ def tile_attend_ghv_cau_kernel(tc, xT, wT, vT, y, wt, xm, offs, out):
             else:
                 nc.vector.tensor_copy(dst, src)
 
+        def gather(engine, name, t, b, first=0, count=N):
+            move(engine, gathered[name, b][:, t, first:first + count],
+                 table_planes[name, t][:].indirect(list_part(b * N + first, count)))
+
         def by_runs(planes):
             return planes.rearrange("p t (c i) -> p c t i", i=RUN)
 
         def interleaved_by_runs(words):
             return words.rearrange("p (c i t) -> p c t i", i=RUN, t=PACK)
 
-        def interleave(engine, name, b, planes, buffer=None, first=0, count=N):
-            dst = stage(name, b, buffer, first, count)[:]
-            src = planes[:, :, first:first + count]
+        def stage(name, b, first=0, count=N, buffer=None):
+            staged[name, b, first] = tile([P, PACK * count], BF16, buffer or f"stage_{name}{b}_{first}")
+            return staged[name, b, first][:]
+
+        def interleave(engine, name, b, planes, first=0, buffer=None):
+            dst = stage(name, b, first, planes.shape[2], buffer)
             if engine is nc.gpsimd:
-                cast(engine, dst.rearrange("p (c t) -> p c t", t=PACK), src.rearrange("p t c -> p c t"))
+                move(engine, dst.rearrange("p (c t) -> p c t", t=PACK), planes.rearrange("p t c -> p c t"))
             else:
-                cast(engine, interleaved_by_runs(dst), by_runs(src))
+                move(engine, interleaved_by_runs(dst), by_runs(planes))
 
         def interleave_x(engine, b):
-            cast(engine, staged["x", b, 0][:].rearrange("p (t m j) -> p m j t", t=PACK, j=PACK),
-                 rows["x", b].rearrange("p j (m t) -> p m j t", t=PACK))
+            move(engine, stage("x", b).rearrange("p (t m j) -> p m j t", t=PACK, j=PACK),
+                 rows["x", b, 0][:].rearrange("p j (m t) -> p m j t", t=PACK))
 
-        def quantise(name, b, fmt=E4M3, buffer=None, first=0, count=N, into=None):
+        def quantise(name, b, first=0, count=N, fmt=E4M3):
             if (name, b) not in codes:
-                if into is None:
-                    into = sbuf.tile([P, N], U32, name=buffer or f"codes_{name}{b}", align_bytes=ALIGN)
-                codes[name, b] = into
-                if (name, b) not in scales:
-                    scales[name, b] = sbuf.tile([P, N], U8, name=f"scales_{name}{b}", align_bytes=ALIGN)
+                codes[name, b] = tile([P, N], U32, f"codes_{name}{b}")
+                scales[name, b] = tile([P, N], U8, f"scales_{name}{b}")
             columns = slice(first, first + count)
             nc.vector.quantize_mx(out=codes[name, b][:, columns].bitcast(fmt), scales=scales[name, b][:, columns],
                                   in_=staged[name, b, first][:])
@@ -145,223 +120,126 @@ def tile_attend_ghv_cau_kernel(tc, xT, wT, vT, y, wt, xm, offs, out):
                                 lhsT_scale=scales[stationary, b][:, held], rhs=codes[moving, b][:, columns].bitcast(fmt),
                                 rhs_scale=scales[moving, b][:, columns], start=True, stop=True)
 
-        def residual(b, t, on_vector=False):
-            bank = psum.tile([P, N], F32, name=f"bank{t}")
+        def factor(b, t, square_on_scalar):
+            plane = rows["y", b, 0][:, t, :]
+            bank = psum.tile([P, N], F32, name=f"bank{PACK * b + t}")
             multiply(bank[:], b, "x", t, "w")
-            if on_vector:
-                nc.vector.tensor_tensor(residuals[b][t], bank[:], targets[b][:, t, :], ALU.subtract)
-            else:
-                nc.scalar.activation(a_sb[b][:, t, :], bank[:], ACT.Copy)
-                nc.gpsimd.tensor_tensor(residuals[b][t], a_sb[b][:, t, :], targets[b][:, t, :], ALU.subtract)
-
-        def factor(b, t, wt_on_scalar):
-            plane = residuals[b][t]
+            nc.vector.tensor_tensor(plane, bank[:], plane, ALU.subtract)
             nc.scalar.activation(plane, plane, ACT.Square)
             nc.scalar.activation(plane, plane, ACT.Abs_reciprocal_sqrt, bias=one[:])
-            nc.scalar.activation(plane, plane, ACT.Square)
-            if wt_on_scalar:
-                nc.scalar.activation(factors[b][:, t, :], plane, ACT.Copy, scale=wt_sb[:, b, t:t + 1])
+            if square_on_scalar:
+                nc.scalar.activation(plane, plane, ACT.Square)
+                nc.gpsimd.tensor_scalar(plane, plane, wt_sb[:, b, t:t + 1], 0.0, ALU.mult, ALU.add)
             else:
-                nc.gpsimd.tensor_scalar(factors[b][:, t, :], plane, wt_sb[:, b, t:t + 1], 0.0, ALU.mult, ALU.add)
+                weighted = tile([P, N], F32, f"weighted_root{t % 2}")
+                nc.gpsimd.tensor_scalar(weighted[:], plane, wt_sb[:, b, t:t + 1], 0.0, ALU.mult, ALU.add)
+                nc.gpsimd.tensor_tensor(plane, plane, weighted[:], ALU.mult)
 
-        def form_g(b, g, blocks):
-            for c in blocks:
-                bank = psum.tile([P, PACK, P], F32, name=f"bank{AV_BANK + c}")
+        def form_g(b, first=0, count=N):
+            g = stage("g", b, first, count)
+            for c in range(first // P, (first + count) // P):
+                bank = psum.tile([P, PACK, P], F32, name=f"bank{PACK * b + c}")
                 items = slice(c * P, (c + 1) * P)
                 for t in range(PACK):
                     multiply(bank[:, t, :], b, "x", t, "v", items)
-                nc.vector.tensor_tensor(interleaved_by_runs(g[:, PACK * c * P:PACK * (c + 1) * P]), by_runs(bank[:]),
-                                        by_runs(factors[b][:, :, items]), ALU.mult)
+                words = g[:, PACK * (c * P - first):PACK * ((c + 1) * P - first)]
+                nc.vector.tensor_tensor(interleaved_by_runs(words), by_runs(bank[:]),
+                                        by_runs(rows["y", b, 0][:, :, items]), ALU.mult)
 
-        def last_product(b, j, bank_number):
-            banks[b, j] = psum.tile([P, N], F32, name=f"bank{bank_number}")
-            if ("xm_late", b) in codes and j >= BLOCKS // 2:
-                multiply(banks[b, j][:], b, "xm_late", j - BLOCKS // 2, "g", fmt=E5M2)
-            else:
-                multiply(banks[b, j][:], b, "xm", j, "g", fmt=E5M2)
+        def last_product(engine, b, j, bank_number, buffer, first=0, count=N):
+            bank = psum.tile([P, count], F32, name=f"bank{bank_number}")
+            multiply(bank[:], b, "xm", j, "g", slice(first, first + count), E5M2)
+            product = tile([P, count], F32, buffer)
+            move(engine, product[:], bank[:])
+            for start in range(first, first + count, HALF):
+                products[b, j, start] = (product, start - first)
 
-        def empty_bank(b, j, buffer, first=0, count=N):
-            products[b, j, first] = sbuf.tile([P, count], F32, name=buffer, align_bytes=ALIGN)
-            nc.scalar.activation(products[b, j, first][:], banks[b, j][:, first:first + count], ACT.Copy)
+        def scatter(engine, b, j, first=0, count=N):
+            piece = HALF if engine is nc.scalar else count
+            for start in range(first, first + count, piece):
+                product, column = products[b, j, start]
+                move(engine, windows[j][:].indirect(list_part(b * N + start, piece)), product[:, column:column + piece])
 
-        def scatter(b, j, first=0, count=N):
-            nc.vector.tensor_copy(windows[j][:].indirect(list_part(b * N + first, count)), products[b, j, first][:])
+        def store(j):
+            nc.sync.dma_start(out[j * P:(j + 1) * P, :], windows[j][:])
 
-        codes["g", 1] = sbuf.tile([P, N], U32, name="codes_g1", align_bytes=ALIGN)
-        scales["g", 1] = sbuf.tile([P, N], U8, name="scales_g1", align_bytes=ALIGN)
-        nc.gpsimd.memset(codes["g", 1][:, HALF:], 0)
-        nc.gpsimd.memset(scales["g", 1][:, HALF:].bitcast(U32), 0)
-
-        words_w1 = stage("w", 1)[:].rearrange("p (c t) -> p c t", t=PACK)
-        for t, buffer in enumerate(("rounded_w0", "stage_g1_0")):
-            gather_group("w", t, 0)
-            rounded = sbuf.tile([P, T], BF16, name=buffer, align_bytes=ALIGN)
-            nc.scalar.activation(rounded[:], table_planes["w", t][:], ACT.Copy)
-            nc.scalar.activation(words_w1[:, :, t], rounded[:].indirect(list_part(N, N)), ACT.Copy)
-        gather_both("w", 2)
+        for t in range(PACK):
+            load_plane("w", wT, t)
+            if t == 0:
+                nc.sync.dma_start(offsets[:], offs)
+        load_rows("x", xT, 0, "rows_x0")
+        nc.scalar.dma_start(wt_sb[:], wt.rearrange("b (p t) o -> p b (t o)", t=PACK))
+        load_rows("x", xT, 1, "rows_x1")
         for b in range(B):
-            gather_group("w", LAST, b)
-        for t in range(LAST):
-            gather_both("v", t)
+            load_targets(b)
+        for t in range(PACK):
+            load_plane("v", vT, t)
+
+        for t in range(PACK):
+            gather(nc.vector, "w", t, 0)
+            gather(nc.scalar, "w", t, 1)
         for first in (0, HALF):
-            gather_group("v", LAST, 0, first, HALF)
-
-        rows["xm", 0] = load_rows(xm, 0, "plane_w0")
-        v_and_x = sbuf.tile([P, 2 * LAST * P + PACK * R], F32, name="plane_w1", align_bytes=ALIGN)
-        staged["v", 1, 0] = v_and_x[:, 0:2 * N].bitcast(BF16)
-        rows["x", 1] = v_and_x[:, 2 * LAST * P:].rearrange("p (t c) -> p t c", t=PACK)
-        nc.sync.dma_start(rows["x", 1], xT[1].rearrange("(p t) c -> p t c", t=PACK))
-        targets[1] = load_rows(y, 1, "plane_w3")
-        rows["xm", 1] = load_rows(xm, 1, "plane_w2")
-
-        interleave(nc.scalar, "w", 0, gathered["w"][:, :, 0:N])
-        cast(nc.scalar, interleaved_by_runs(staged["w", 1, 0][:])[:, :, 2:, :], by_runs(gathered["w"][:, 2:, N:2 * N]))
-        stage("x", 0)
+            load_rows("xm", xm, 0, f"plane_w{first // HALF}", first, HALF)
+        load_rows("xm", xm, 1, "plane_w2")
+        interleave(nc.vector, "w", 0, gathered["w", 0][:])
+        interleave(nc.scalar, "w", 1, gathered["w", 1][:])
         interleave_x(nc.vector, 0)
+        interleave_x(nc.scalar, 1)
         quantise("w", 0)
         quantise("x", 0)
         quantise("w", 1)
-        a_sb[0] = sbuf.tile([P, PACK, N], F32, name="a_sb", align_bytes=ALIGN)
-        residuals[0] = [targets[0][:, t, :] for t in range(PACK)]
+        quantise("x", 1)
         for t in range(PACK):
-            residual(0, t, on_vector=t == LAST)
-        factors[0] = sbuf.tile([P, PACK, N], F32, name="a_sb", align_bytes=ALIGN)[:]
-        for t in (0, 1, LAST, 2):
-            factor(0, t, wt_on_scalar=t >= PACK // 2)
-
-        staged["v", 0, 0] = gathered_v[:, PACK * B * N - N:].bitcast(BF16)
-        cast(nc.vector, interleaved_by_runs(staged["v", 0, 0]), by_runs(gathered["v"][:, :, 0:HALF]))
-        interleave(nc.vector, "v", 0, gathered["v"][:, :, 0:N], first=HALF, count=HALF)
+            factor(0, t, False)
+        for t in range(LAST):
+            gather(nc.vector, "v", t, 0)
+        gather(nc.vector, "v", LAST, 0, 0, HALF)
+        gather(nc.scalar, "v", LAST, 0, HALF, HALF)
+        for t in range(PACK):
+            gather(nc.vector if t < 2 else nc.scalar, "v", t, 1)
         for first in (0, HALF):
-            quantise("v", 0, first=first, count=HALF)
-        gather_group("v", LAST, 1)
-        form_g(0, stage("g", 0), range(BLOCKS))
-        interleave(nc.gpsimd, "xm", 0, rows["xm", 0], buffer=f"stage_v0_{HALF}", first=0, count=HALF)
-        staged_v1 = staged["v", 1, 0]
-        cast(nc.gpsimd, staged_v1[:, 0:PACK * LAST * P].rearrange("p (c t) -> p c t", t=PACK),
-             gathered["v"][:, :, N:N + LAST * P].rearrange("p t c -> p c t"))
-        staged["x", 1, 0] = placed.tile([P, PACK * N], BF16, name="stage_x1", align_bytes=ALIGN, offset=X_OFFSET)
-        interleave_x(nc.scalar, 1)
-        interleave(nc.scalar, "xm", 0, rows["xm", 0], first=HALF, count=HALF)
-        quantise("xm", 0, buffer="codes_v0", first=0, count=HALF)
-        quantise("g", 0, E5M2, buffer="stage_w0_0")
-        quantise("x", 1, buffer="codes_x0")
-        cast(nc.vector, interleaved_by_runs(staged_v1[:, PACK * LAST * P:]), by_runs(gathered["v"][:, :, N + LAST * P:]))
-        staged["xm_late", 0, 0] = staged["xm", 0, HALF]
-        scales["xm_late", 0] = placed.tile([P, N], U8, name="scales_xm_late", align_bytes=ALIGN, offset=X_OFFSET + 4 * N)
-        quantise("xm_late", 0, count=HALF)
-        quantise("v", 1)
-        q_first = sbuf.tile([P, ON_VECTOR * N], F32, name="stage_g0_0", align_bytes=ALIGN)
-
-        first_products = [placed.tile([P, N], F32, name="product0", align_bytes=ALIGN, offset=X_OFFSET),
-                          sbuf.tile([P, N], F32, name="product1", align_bytes=ALIGN)]
-
-        def first_product(j, bank_number):
-            last_product(0, j, bank_number)
-            products[0, j, 0] = first_products[j][:]
-            nc.scalar.activation(products[0, j, 0], banks[0, j][:], ACT.Copy)
-
-        first_product(0, 2)
-        late = sbuf.tile([P, (BLOCKS - ON_VECTOR + 2) * N], F32, name="plane_w1", align_bytes=ALIGN)
-        q_blocks = ([q_first[:, c * N:(c + 1) * N] for c in range(ON_VECTOR)]
-                    + [late[:, c * N:(c + 1) * N] for c in range(BLOCKS - ON_VECTOR)])
-        staged["xm", 1, 0] = late[:, (BLOCKS - ON_VECTOR) * N:].bitcast(BF16)
-        a_blocks = sbuf.tile([P, BLOCKS * N], F32, name="plane_v1", align_bytes=ALIGN)
-        inverses = {c: sbuf.tile([P, N], F32, name=buffer, align_bytes=ALIGN)
-                    for c, buffer in ((0, "rows_x0"), (2, "plane_v3"), (3, "stage_x0_0"))}
-        inverses[1] = placed.tile([P, N], F32, name="inverse1", align_bytes=ALIGN, offset=4 * HALF)
-        weighted_av = sbuf.tile([P, PACK, N], F32, name="rows_y0", align_bytes=ALIGN)
-        stage("g", 1, buffer="stage_g1_0", count=HALF)
-
-        def as_planes(block):
-            return block.rearrange("p (t i) -> p t i", t=PACK)
-
-        def as_items(block):
-            return block.rearrange("p (i t) -> p i t", t=PACK)
-
-        def by_items(planes):
-            return planes.rearrange("p t i -> p i t")
-
-        def residual_block(c):
-            bank = psum.tile([P, PACK, P], F32, name=f"bank{c}")
-            for t in range(PACK):
-                multiply(bank[:, t, :], 1, "x", t, "w", slice(c * P, (c + 1) * P))
-            y_block = targets[1][:, :, c * P:(c + 1) * P]
-            if c < ON_VECTOR:
-                nc.vector.tensor_tensor(as_planes(q_blocks[c]), bank[:], y_block, ALU.subtract)
-            else:
-                a_block = a_blocks[:, c * N:(c + 1) * N]
-                nc.scalar.activation(a_block, bank[:].rearrange("p t i -> p (t i)"), ACT.Copy)
-                nc.gpsimd.tensor_tensor(as_planes(q_blocks[c]), as_planes(a_block), y_block, ALU.subtract)
-
-        squares = {}
-
-        def square(c):
-            squares[c] = q_blocks[min(c, LAST - c)]
-            nc.scalar.activation(squares[c], q_blocks[c], ACT.Square)
-
-        def root(c):
-            nc.scalar.activation(q_blocks[c], squares[c], ACT.Abs_reciprocal_sqrt, bias=one[:])
-
-        def inverse(c):
-            nc.scalar.activation(interleaved_by_runs(inverses[c][:]), by_runs(as_planes(q_blocks[c])), ACT.Square)
-
-        def product(c, half):
-            nc.gpsimd.tensor_tensor(as_items(half[:, PACK * (c % 2) * P:PACK * (c % 2 + 1) * P]),
-                                    by_items(weighted_av[:, :, c * P:(c + 1) * P]), as_items(inverses[c][:]), ALU.mult)
-
-        def copy_av(t):
-            bank = psum.tile([P, N], F32, name=f"bank{AV_BANK + 2 + t % 2}")
-            multiply(bank[:], 1, "x", t, "v")
-            nc.scalar.activation(weighted_av[:, t, :], bank[:], ACT.Copy, scale=wt_sb[:, 1, t:t + 1])
-
-        residual_block(0)
-        first_product(1, 0)
-        for c in range(1, BLOCKS):
-            residual_block(c)
-        cast(nc.gpsimd, as_items(staged["xm", 1, 0]), by_items(rows["xm", 1]))
-        scatter(0, 0)
-        scatter(0, 1)
+            interleave(nc.scalar, "xm", 0, rows["xm", 0, first][:], first)
         for t in range(PACK):
-            copy_av(t)
-        for c in (0, 1):
-            square(c)
-        root(0)
-        last_product(0, 2, AV_BANK)
-        empty_bank(0, 2, "product2")
-        scatter(0, 2)
-        inverse(0)
-        product(0, staged["g", 1, 0])
-        root(1)
-        inverse(1)
-        product(1, staged["g", 1, 0])
-        last_product(0, LAST, AV_BANK + 1)
-        empty_bank(0, LAST, "product3", 0, HALF)
-        scatter(0, LAST, 0, HALF)
-        quantise("g", 1, E5M2, first=0, count=HALF)
-        quantise("xm", 1, into=placed.tile([P, N], U32, name="codes_xm1", align_bytes=ALIGN, offset=0))
-        products[0, LAST, HALF] = placed.tile([P, HALF], F32, name="product3_second", align_bytes=ALIGN, offset=4 * N)
-        nc.scalar.activation(products[0, LAST, HALF][:], banks[0, LAST][:, HALF:], ACT.Copy)
-        scatter(0, LAST, HALF, HALF)
-        staged["g", 1, HALF] = staged["xm", 1, 0][:, 0:PACK * HALF]
-        for step in (square, root):
-            for c in (2, 3):
-                step(c)
-        for c in (2, 3):
-            inverse(c)
-            product(c, staged["g", 1, HALF])
-        for j in (0, 1):
-            last_product(1, j, j)
-            products[1, j, 0] = q_blocks[LAST][:, j * HALF:(j + 1) * HALF]
-            nc.scalar.activation(products[1, j, 0], banks[1, j][:, 0:HALF], ACT.Copy)
-            scatter(1, j, 0, HALF)
-        last_product(1, 2, 2)
-        empty_bank(1, 2, "rows_y0", 0, HALF)
-        quantise("g", 1, E5M2, first=HALF, count=HALF)
-        scatter(1, 2, 0, HALF)
-        for j in range(BLOCKS):
-            first = HALF if j < EARLY else 0
-            last_product(1, j, (3, 4, 0, 3)[j])
-            empty_bank(1, j, f"late_product{j}", first, N - first)
-            scatter(1, j, first, N - first)
-            nc.sync.dma_start(out[j * P:(j + 1) * P, :], windows[j][:])
+            factor(1, t, t >= 1)
+
+        for first in (0, HALF):
+            interleave(nc.vector, "v", 0, gathered["v", 0][:, :, first:first + HALF], first)
+        for first in (0, HALF):
+            quantise("v", 0, first, HALF)
+        interleave(nc.gpsimd, "v", 1, gathered["v", 1][:, :, 0:HALF], 0, f"stage_v0_{HALF}")
+        form_g(0, 0, HALF)
+        quantise("xm", 0, 0, HALF)
+        quantise("g", 0, 0, HALF, E5M2)
+        last_product(nc.scalar, 0, 0, 0, "product_s0", 0, HALF)
+        interleave(nc.gpsimd, "v", 1, gathered["v", 1][:, :, HALF:], HALF, "stage_g0_0")
+        form_g(0, HALF, HALF)
+        quantise("g", 0, HALF, HALF, E5M2)
+        scatter(nc.scalar, 0, 0, 0, HALF)
+        last_product(nc.scalar, 0, 0, 1, "product_s1", HALF, HALF)
+        quantise("xm", 0, HALF, HALF)
+        for first in (0, HALF):
+            quantise("v", 1, first, HALF)
+        interleave(nc.gpsimd, "xm", 1, rows["xm", 1, 0][:], buffer="stage_g0_0")
+        form_g(1)
+        quantise("xm", 1)
+        quantise("g", 1, fmt=E5M2)
+        scatter(nc.scalar, 0, 0, HALF, HALF)
+        last_product(nc.scalar, 0, 3, 2, "product_shared")
+        scatter(nc.scalar, 0, 3)
+        last_product(nc.vector, 0, 2, 3, "rows_y1")
+        scatter(nc.vector, 0, 2)
+        last_product(nc.scalar, 1, 0, 4, "product_s1")
+        scatter(nc.scalar, 1, 0)
+        store(0)
+        last_product(nc.vector, 1, 2, 5, "product_v1")
+        scatter(nc.vector, 1, 2)
+        store(2)
+        last_product(nc.scalar, 0, 1, 0, "product_s1")
+        scatter(nc.scalar, 0, 1, 0, HALF)
+        last_product(nc.vector, 1, 3, 6, "product_v1")
+        scatter(nc.vector, 1, 3)
+        store(3)
+        last_product(nc.scalar, 1, 1, 7, "product_s0")
+        scatter(nc.scalar, 1, 1)
+        scatter(nc.vector, 0, 1, HALF, HALF)
+        store(1)

@@ -92,19 +92,18 @@ def tile_attend_ghv_cau_kernel(tc, xT, wT, vT, y, wt, xm, offs, out):
             return words.rearrange("p (c i t) -> p c t i", i=RUN, t=PACK)
 
         def stage(name, b, first=0, count=N, buffer=None):
-            staged[name, b, first] = tile([P, PACK * count], BF16, buffer or f"stage_{name}{b}_{first}")
-            return staged[name, b, first][:]
+            staged[name, b, first] = tile([P, PACK * count], BF16, buffer or f"stage_{name}{b}_{first}")[:]
+            return staged[name, b, first]
 
-        def interleave(engine, name, b, planes, first=0, buffer=None):
-            dst = stage(name, b, first, planes.shape[2], buffer)
+        def interleave(engine, dst, planes):
             if engine is nc.gpsimd:
                 move(engine, dst.rearrange("p (c t) -> p c t", t=PACK), planes.rearrange("p t c -> p c t"))
             else:
                 move(engine, interleaved_by_runs(dst), by_runs(planes))
 
-        def interleave_x(engine, b):
-            move(engine, stage("x", b).rearrange("p (t m j) -> p m j t", t=PACK, j=PACK),
-                 rows["x", b, 0][:].rearrange("p j (m t) -> p m j t", t=PACK))
+        def interleave_x(engine, b, part=slice(0, P)):
+            move(engine, staged["x", b, 0].rearrange("p (t m j) -> p m j t", t=PACK, j=PACK)[:, part],
+                 rows["x", b, 0][:].rearrange("p j (m t) -> p m j t", t=PACK)[:, part])
 
         def quantise(name, b, first=0, count=N, fmt=E4M3):
             if (name, b) not in codes:
@@ -112,7 +111,7 @@ def tile_attend_ghv_cau_kernel(tc, xT, wT, vT, y, wt, xm, offs, out):
                 scales[name, b] = tile([P, N], U8, f"scales_{name}{b}")
             columns = slice(first, first + count)
             nc.vector.quantize_mx(out=codes[name, b][:, columns].bitcast(fmt), scales=scales[name, b][:, columns],
-                                  in_=staged[name, b, first][:])
+                                  in_=staged[name, b, first])
 
         def multiply(result, b, stationary, block, moving, columns=slice(0, N), fmt=E4M3):
             held = slice(block * P, (block + 1) * P)
@@ -120,48 +119,49 @@ def tile_attend_ghv_cau_kernel(tc, xT, wT, vT, y, wt, xm, offs, out):
                                 lhsT_scale=scales[stationary, b][:, held], rhs=codes[moving, b][:, columns].bitcast(fmt),
                                 rhs_scale=scales[moving, b][:, columns], start=True, stop=True)
 
-        def factor(b, t, square_on_scalar):
+        def root(b, t):
             plane = rows["y", b, 0][:, t, :]
             bank = psum.tile([P, N], F32, name=f"bank{PACK * b + t}")
             multiply(bank[:], b, "x", t, "w")
             nc.vector.tensor_tensor(plane, bank[:], plane, ALU.subtract)
             nc.scalar.activation(plane, plane, ACT.Square)
             nc.scalar.activation(plane, plane, ACT.Abs_reciprocal_sqrt, bias=one[:])
-            if square_on_scalar:
+
+        def factor(engine, b, t):
+            plane = rows["y", b, 0][:, t, :]
+            weight = wt_sb[:, b, t:t + 1]
+            if engine is nc.vector:
+                nc.vector.scalar_tensor_tensor(factors[b][:, t, :], plane, weight, plane, ALU.mult, ALU.mult)
+            elif engine is nc.scalar:
                 nc.scalar.activation(plane, plane, ACT.Square)
-                nc.gpsimd.tensor_scalar(plane, plane, wt_sb[:, b, t:t + 1], 0.0, ALU.mult, ALU.add)
+                nc.gpsimd.tensor_scalar(factors[b][:, t, :], plane, weight, 0.0, ALU.mult, ALU.add)
             else:
-                weighted = tile([P, N], F32, f"weighted_root{t % 2}")
-                nc.gpsimd.tensor_scalar(weighted[:], plane, wt_sb[:, b, t:t + 1], 0.0, ALU.mult, ALU.add)
-                nc.gpsimd.tensor_tensor(plane, plane, weighted[:], ALU.mult)
+                nc.gpsimd.tensor_scalar(factors[b][:, t, :], plane, weight, 0.0, ALU.mult, ALU.add)
+                nc.gpsimd.tensor_tensor(factors[b][:, t, :], factors[b][:, t, :], plane, ALU.mult)
 
-        def form_g(b, first=0, count=N):
-            g = stage("g", b, first, count)
-            for c in range(first // P, (first + count) // P):
-                bank = psum.tile([P, PACK, P], F32, name=f"bank{PACK * b + c}")
-                items = slice(c * P, (c + 1) * P)
-                for t in range(PACK):
-                    multiply(bank[:, t, :], b, "x", t, "v", items)
-                words = g[:, PACK * (c * P - first):PACK * ((c + 1) * P - first)]
-                nc.vector.tensor_tensor(interleaved_by_runs(words), by_runs(bank[:]),
-                                        by_runs(rows["y", b, 0][:, :, items]), ALU.mult)
+        def form_g(b, c):
+            first = max(start for name, group, start in staged if (name, group) == ("g", b) and start <= c * P)
+            bank = psum.tile([P, PACK, P], F32, name=f"bank{PACK * b + c}")
+            items = slice(c * P, (c + 1) * P)
+            for t in range(PACK):
+                multiply(bank[:, t, :], b, "x", t, "v", items)
+            words = staged["g", b, first][:, PACK * (c * P - first):PACK * ((c + 1) * P - first)]
+            nc.vector.tensor_tensor(interleaved_by_runs(words), by_runs(bank[:]), by_runs(factors[b][:, :, items]),
+                                    ALU.mult)
 
-        def last_product(engine, b, j, bank_number, buffer, first=0, count=N):
+        def last_product(engine, b, j, bank_number, first=0, count=N):
             bank = psum.tile([P, count], F32, name=f"bank{bank_number}")
             multiply(bank[:], b, "xm", j, "g", slice(first, first + count), E5M2)
-            product = tile([P, count], F32, buffer)
-            move(engine, product[:], bank[:])
-            for start in range(first, first + count, HALF):
-                products[b, j, start] = (product, start - first)
+            move(engine, products[j][:, b * N + first:b * N + first + count], bank[:])
 
-        def scatter(engine, b, j, first=0, count=N):
-            piece = HALF if engine is nc.scalar else count
-            for start in range(first, first + count, piece):
-                product, column = products[b, j, start]
-                move(engine, windows[j][:].indirect(list_part(b * N + start, piece)), product[:, column:column + piece])
+        def scatter(engine, j, first, count):
+            move(engine, windows[j][:].indirect(list_part(first, count)), products[j][:, first:first + count])
 
         def store(j):
             nc.sync.dma_start(out[j * P:(j + 1) * P, :], windows[j][:])
+
+        def half(planes, first):
+            return planes[:, :, first:first + HALF]
 
         for t in range(PACK):
             load_plane("w", wT, t)
@@ -175,71 +175,102 @@ def tile_attend_ghv_cau_kernel(tc, xT, wT, vT, y, wt, xm, offs, out):
         for t in range(PACK):
             load_plane("v", vT, t)
 
-        for t in range(PACK):
+        for t in range(LAST):
             gather(nc.vector, "w", t, 0)
             gather(nc.scalar, "w", t, 1)
+        gather(nc.vector, "w", LAST, 0, 0, HALF)
+        gather(nc.scalar, "w", LAST, 0, HALF, HALF)
+        gather(nc.scalar, "w", LAST, 1)
         for first in (0, HALF):
             load_rows("xm", xm, 0, f"plane_w{first // HALF}", first, HALF)
         load_rows("xm", xm, 1, "plane_w2")
-        interleave(nc.vector, "w", 0, gathered["w", 0][:])
-        interleave(nc.scalar, "w", 1, gathered["w", 1][:])
-        interleave_x(nc.vector, 0)
-        interleave_x(nc.scalar, 1)
-        quantise("w", 0)
+        for first in (HALF, 0):
+            interleave(nc.vector, stage("w", 0, first, HALF), half(gathered["w", 0], first))
+        for first in (HALF, 0):
+            quantise("w", 0, first, HALF)
+        stage("x", 0)
+        interleave_x(nc.scalar, 0, slice(0, P // 2))
+        interleave_x(nc.vector, 0, slice(P // 2, P))
         quantise("x", 0)
+        interleave(nc.vector, stage("w", 1, buffer="stage_x0_0"), gathered["w", 1][:])
+        stage("x", 1)
+        interleave_x(nc.scalar, 1)
         quantise("w", 1)
         quantise("x", 1)
+        factor_tiles = [tile([P, PACK * N], F32, f"rows_x{b}") for b in range(B)]
+        factors = [factor_tile[:].rearrange("p (t n) -> p t n", t=PACK) for factor_tile in factor_tiles]
         for t in range(PACK):
-            factor(0, t, False)
+            root(0, t)
+            factor(nc.gpsimd, 0, t)
         for t in range(LAST):
             gather(nc.vector, "v", t, 0)
         gather(nc.vector, "v", LAST, 0, 0, HALF)
         gather(nc.scalar, "v", LAST, 0, HALF, HALF)
+        gather(nc.scalar, "v", 2, 1)
+        gather(nc.scalar, "v", LAST, 1, 0, HALF)
+        for t in range(2):
+            gather(nc.vector, "v", t, 1)
         for t in range(PACK):
-            gather(nc.vector if t < 2 else nc.scalar, "v", t, 1)
-        for first in (0, HALF):
-            interleave(nc.scalar, "xm", 0, rows["xm", 0, first][:], first)
-        for t in range(PACK):
-            factor(1, t, t >= 1)
+            root(1, t)
+            if t < 2:
+                factor(nc.scalar, 1, t)
+        gather(nc.scalar, "v", LAST, 1, HALF, HALF)
 
-        for first in (0, HALF):
-            interleave(nc.vector, "v", 0, gathered["v", 0][:, :, first:first + HALF], first)
-        for first in (0, HALF):
+        staged["xm", 0, 0] = factor_tiles[1][:, 2 * N:3 * N].bitcast(BF16)
+        staged["g", 0, HALF] = factor_tiles[1][:, 3 * N:].bitcast(BF16)
+        interleave(nc.scalar, staged["xm", 0, 0], rows["xm", 0, 0][:])
+        for first in (HALF, 0):
+            interleave(nc.vector, stage("v", 0, first, HALF), half(gathered["v", 0], first))
+        for first in (HALF, 0):
             quantise("v", 0, first, HALF)
-        interleave(nc.gpsimd, "v", 1, gathered["v", 1][:, :, 0:HALF], 0, f"stage_v0_{HALF}")
-        form_g(0, 0, HALF)
+        interleave(nc.gpsimd, stage("xm", 0, HALF, HALF, "stage_v0_0"), rows["xm", 0, HALF][:])
+        stage("v", 1)
+        interleave(nc.vector, staged["v", 1, 0][:, 0:PACK * HALF], half(gathered["v", 1], 0))
+        interleave(nc.scalar, staged["v", 1, 0][:, PACK * HALF:], half(gathered["v", 1], HALF))
+        stage("g", 0, 0, HALF)
+        for c in (2, 3, 0):
+            form_g(0, c)
         quantise("xm", 0, 0, HALF)
-        quantise("g", 0, 0, HALF, E5M2)
-        last_product(nc.scalar, 0, 0, 0, "product_s0", 0, HALF)
-        interleave(nc.gpsimd, "v", 1, gathered["v", 1][:, :, HALF:], HALF, "stage_g0_0")
-        form_g(0, HALF, HALF)
         quantise("g", 0, HALF, HALF, E5M2)
-        scatter(nc.scalar, 0, 0, 0, HALF)
-        last_product(nc.scalar, 0, 0, 1, "product_s1", HALF, HALF)
+        for j, buffer in ((0, "plane_v0"), (1, "plane_v1")):
+            products[j] = tile([P, B * N], F32, buffer)
+        for j in (0, 1):
+            last_product(nc.scalar, 0, j, 2 + j, HALF, HALF)
+        for j in (0, 1):
+            scatter(nc.scalar, j, HALF, HALF)
+        form_g(0, 1)
+        quantise("v", 1)
+        quantise("g", 0, 0, HALF, E5M2)
+        for j in (0, 1):
+            last_product(nc.scalar, 0, j, j, 0, HALF)
+        for j in (0, 1):
+            scatter(nc.scalar, j, 0, HALF)
+        for t in (2, LAST):
+            factor(nc.vector, 1, t)
         quantise("xm", 0, HALF, HALF)
-        for first in (0, HALF):
-            quantise("v", 1, first, HALF)
-        interleave(nc.gpsimd, "xm", 1, rows["xm", 1, 0][:], buffer="stage_g0_0")
-        form_g(1)
+        interleave(nc.gpsimd, stage("xm", 1, buffer="stage_v0_0"), rows["xm", 1, 0][:])
+        stage("g", 1)
+        for c in range(N // P):
+            form_g(1, c)
+        products[2] = tile([P, B * N], F32, "rows_x1")
+        last_product(nc.vector, 0, 2, 2)
         quantise("xm", 1)
         quantise("g", 1, fmt=E5M2)
-        scatter(nc.scalar, 0, 0, HALF, HALF)
-        last_product(nc.scalar, 0, 3, 2, "product_shared")
-        scatter(nc.scalar, 0, 3)
-        last_product(nc.vector, 0, 2, 3, "rows_y1")
-        scatter(nc.vector, 0, 2)
-        last_product(nc.scalar, 1, 0, 4, "product_s1")
-        scatter(nc.scalar, 1, 0)
-        store(0)
-        last_product(nc.vector, 1, 2, 5, "product_v1")
-        scatter(nc.vector, 1, 2)
-        store(2)
-        last_product(nc.scalar, 0, 1, 0, "product_s1")
-        scatter(nc.scalar, 0, 1, 0, HALF)
-        last_product(nc.vector, 1, 3, 6, "product_v1")
-        scatter(nc.vector, 1, 3)
-        store(3)
-        last_product(nc.scalar, 1, 1, 7, "product_s0")
-        scatter(nc.scalar, 1, 1)
-        scatter(nc.vector, 0, 1, HALF, HALF)
+        scatter(nc.vector, 2, 0, HALF)
+        products[LAST] = tile([P, B * N], F32, "stage_g1_0")
+        last_product(nc.scalar, 0, LAST, 3)
+        last_product(nc.scalar, 1, 0, 5)
+        last_product(nc.vector, 1, 1, 4)
+        scatter(nc.scalar, LAST, 0, HALF)
+        last_product(nc.vector, 1, 2, 6)
+        scatter(nc.vector, 1, N, N)
         store(1)
+        scatter(nc.scalar, 0, N, HALF)
+        last_product(nc.scalar, 1, LAST, 5)
+        scatter(nc.scalar, 0, N + HALF, HALF)
+        store(0)
+        scatter(nc.vector, 2, HALF, N + HALF)
+        store(2)
+        for first in (HALF, HALF + 3 * P):
+            scatter(nc.scalar, LAST, first, 3 * P)
+        store(LAST)

@@ -22,6 +22,7 @@ RUN = 4
 BAND = 16
 HALF = N // 2
 BLOCKS = D // P
+V_ON_GPSIMD = 192
 ALIGN = 64
 
 
@@ -68,10 +69,8 @@ def tile_attend_ghv_cau_kernel(tc, xT, wT, vT, y, wt, xm, offs, out):
             rows[name, b, first] = tile([P, PACK, count], F32, buffer)
             nc.sync.dma_start(rows[name, b, first][:], by_planes(source[b])[:, :, first:first + count])
 
-        def load_targets(b):
-            rows["y", b, 0] = tile([P, PACK, N], F32, f"rows_y{b}")
-            for planes in (slice(0, 2), slice(2, PACK)):
-                nc.sync.dma_start(rows["y", b, 0][:, planes, :], by_planes(y[b])[:, planes, :])
+        def load_targets(b, planes):
+            nc.sync.dma_start(rows["y", b, 0][:, planes, :], by_planes(y[b])[:, planes, :])
 
         def move(engine, dst, src):
             if engine is nc.scalar:
@@ -137,7 +136,10 @@ def tile_attend_ghv_cau_kernel(tc, xT, wT, vT, y, wt, xm, offs, out):
                 nc.gpsimd.tensor_scalar(factors[b][:, t, :], plane, weight, 0.0, ALU.mult, ALU.add)
             else:
                 nc.gpsimd.tensor_scalar(factors[b][:, t, :], plane, weight, 0.0, ALU.mult, ALU.add)
-                nc.gpsimd.tensor_tensor(factors[b][:, t, :], factors[b][:, t, :], plane, ALU.mult)
+                if t % 2 == 1:
+                    pair = slice(t - 1, t + 1)
+                    nc.gpsimd.tensor_tensor(factors[b][:, pair, :], factors[b][:, pair, :], rows["y", b, 0][:, pair, :],
+                                            ALU.mult)
 
         def form_g(b, c):
             first = max(start for name, group, start in staged if (name, group) == ("g", b) and start <= c * P)
@@ -171,9 +173,13 @@ def tile_attend_ghv_cau_kernel(tc, xT, wT, vT, y, wt, xm, offs, out):
         nc.scalar.dma_start(wt_sb[:], wt.rearrange("b (p t) o -> p b (t o)", t=PACK))
         load_rows("x", xT, 1, "rows_x1")
         for b in range(B):
-            load_targets(b)
+            rows["y", b, 0] = tile([P, PACK, N], F32, f"rows_y{b}")
+        load_targets(0, slice(0, 2))
+        load_targets(0, slice(2, PACK))
+        load_targets(1, slice(0, 2))
         for t in range(PACK):
             load_plane("v", vT, t)
+        load_targets(1, slice(2, PACK))
 
         for t in range(LAST):
             gather(nc.vector, "w", t, 0)
@@ -195,26 +201,26 @@ def tile_attend_ghv_cau_kernel(tc, xT, wT, vT, y, wt, xm, offs, out):
         interleave(nc.vector, stage("w", 1, buffer="stage_x0_0"), gathered["w", 1][:])
         stage("x", 1)
         interleave_x(nc.scalar, 1)
+        root(0, 0)
         quantise("w", 1)
         quantise("x", 1)
         factor_tiles = [tile([P, PACK * N], F32, f"rows_x{b}") for b in range(B)]
         factors = [factor_tile[:].rearrange("p (t n) -> p t n", t=PACK) for factor_tile in factor_tiles]
         for t in range(PACK):
-            root(0, t)
+            if t > 0:
+                root(0, t)
             factor(nc.gpsimd, 0, t)
         for t in range(LAST):
             gather(nc.vector, "v", t, 0)
         gather(nc.vector, "v", LAST, 0, 0, HALF)
         gather(nc.scalar, "v", LAST, 0, HALF, HALF)
         gather(nc.scalar, "v", 2, 1)
-        gather(nc.scalar, "v", LAST, 1, 0, HALF)
+        gather(nc.scalar, "v", LAST, 1)
         for t in range(2):
             gather(nc.vector, "v", t, 1)
-        for t in range(PACK):
+        for t in range(2):
             root(1, t)
-            if t < 2:
-                factor(nc.scalar, 1, t)
-        gather(nc.scalar, "v", LAST, 1, HALF, HALF)
+            factor(nc.scalar, 1, t)
 
         staged["xm", 0, 0] = factor_tiles[1][:, 2 * N:3 * N].bitcast(BF16)
         staged["g", 0, HALF] = factor_tiles[1][:, 3 * N:].bitcast(BF16)
@@ -223,10 +229,12 @@ def tile_attend_ghv_cau_kernel(tc, xT, wT, vT, y, wt, xm, offs, out):
             interleave(nc.vector, stage("v", 0, first, HALF), half(gathered["v", 0], first))
         for first in (HALF, 0):
             quantise("v", 0, first, HALF)
-        interleave(nc.gpsimd, stage("xm", 0, HALF, HALF, "stage_v0_0"), rows["xm", 0, HALF][:])
-        stage("v", 1)
-        interleave(nc.vector, staged["v", 1, 0][:, 0:PACK * HALF], half(gathered["v", 1], 0))
-        interleave(nc.scalar, staged["v", 1, 0][:, PACK * HALF:], half(gathered["v", 1], HALF))
+        for t in (2, LAST):
+            root(1, t)
+        stage("v", 1, buffer="stage_v0_0")
+        interleave(nc.gpsimd, staged["v", 1, 0][:, 0:PACK * V_ON_GPSIMD], gathered["v", 1][:, :, 0:V_ON_GPSIMD])
+        interleave(nc.scalar, staged["v", 1, 0][:, PACK * V_ON_GPSIMD:], gathered["v", 1][:, :, V_ON_GPSIMD:])
+        interleave(nc.gpsimd, stage("xm", 0, HALF, HALF, f"stage_v0_{HALF}"), rows["xm", 0, HALF][:])
         stage("g", 0, 0, HALF)
         for c in (2, 3, 0):
             form_g(0, c)
@@ -248,7 +256,7 @@ def tile_attend_ghv_cau_kernel(tc, xT, wT, vT, y, wt, xm, offs, out):
         for t in (2, LAST):
             factor(nc.vector, 1, t)
         quantise("xm", 0, HALF, HALF)
-        interleave(nc.gpsimd, stage("xm", 1, buffer="stage_v0_0"), rows["xm", 1, 0][:])
+        interleave(nc.gpsimd, stage("xm", 1, buffer=f"stage_v0_{HALF}"), rows["xm", 1, 0][:])
         stage("g", 1)
         for c in range(N // P):
             form_g(1, c)

@@ -57,6 +57,7 @@ def tile_attend_ghv_cau_kernel(tc, xT, wT, vT, y, wt, xm, offs, out):
         codes = {}
         scales = {}
         products = {}
+        av = {}
 
         def by_planes(source):
             return source.rearrange("(p t) c -> p t c", t=PACK)
@@ -104,9 +105,9 @@ def tile_attend_ghv_cau_kernel(tc, xT, wT, vT, y, wt, xm, offs, out):
             move(engine, staged["x", b, 0].rearrange("p (t m j) -> p m j t", t=PACK, j=PACK)[:, part],
                  rows["x", b, 0][:].rearrange("p j (m t) -> p m j t", t=PACK)[:, part])
 
-        def quantise(name, b, first=0, count=N, fmt=E4M3):
+        def quantise(name, b, first=0, count=N, fmt=E4M3, buffer=None):
             if (name, b) not in codes:
-                codes[name, b] = tile([P, N], U32, f"codes_{name}{b}")
+                codes[name, b] = tile([P, N], U32, buffer or f"codes_{name}{b}")
                 scales[name, b] = tile([P, N], U8, f"scales_{name}{b}")
             columns = slice(first, first + count)
             nc.vector.quantize_mx(out=codes[name, b][:, columns].bitcast(fmt), scales=scales[name, b][:, columns],
@@ -141,12 +142,15 @@ def tile_attend_ghv_cau_kernel(tc, xT, wT, vT, y, wt, xm, offs, out):
                     nc.gpsimd.tensor_tensor(factors[b][:, pair, :], factors[b][:, pair, :], rows["y", b, 0][:, pair, :],
                                             ALU.mult)
 
+        def multiply_v(b, c):
+            av[b, c] = psum.tile([P, PACK, P], F32, name=f"bank{PACK * b + c}")
+            for t in range(PACK):
+                multiply(av[b, c][:, t, :], b, "x", t, "v", slice(c * P, (c + 1) * P))
+
         def form_g(b, c):
             first = max(start for name, group, start in staged if (name, group) == ("g", b) and start <= c * P)
-            bank = psum.tile([P, PACK, P], F32, name=f"bank{PACK * b + c}")
+            bank = av[b, c]
             items = slice(c * P, (c + 1) * P)
-            for t in range(PACK):
-                multiply(bank[:, t, :], b, "x", t, "v", items)
             words = staged["g", b, first][:, PACK * (c * P - first):PACK * ((c + 1) * P - first)]
             nc.vector.tensor_tensor(interleaved_by_runs(words), by_runs(bank[:]), by_runs(factors[b][:, :, items]),
                                     ALU.mult)
@@ -222,8 +226,10 @@ def tile_attend_ghv_cau_kernel(tc, xT, wT, vT, y, wt, xm, offs, out):
             root(1, t)
             factor(nc.scalar, 1, t)
 
-        staged["xm", 0, 0] = factor_tiles[1][:, 2 * N:3 * N].bitcast(BF16)
+        stage("xm", 0, 0, HALF)
+        staged["g", 0, 0] = factor_tiles[1][:, 2 * N:3 * N].bitcast(BF16)
         staged["g", 0, HALF] = factor_tiles[1][:, 3 * N:].bitcast(BF16)
+        interleave(nc.scalar, stage("v", 1, 0, HALF), half(gathered["v", 1], 0))
         interleave(nc.scalar, staged["xm", 0, 0], rows["xm", 0, 0][:])
         for first in (HALF, 0):
             interleave(nc.vector, stage("v", 0, first, HALF), half(gathered["v", 0], first))
@@ -231,15 +237,17 @@ def tile_attend_ghv_cau_kernel(tc, xT, wT, vT, y, wt, xm, offs, out):
             quantise("v", 0, first, HALF)
         for t in (2, LAST):
             root(1, t)
-        stage("v", 1, buffer="stage_v0_0")
-        interleave(nc.gpsimd, staged["v", 1, 0][:, 0:PACK * V_ON_GPSIMD], gathered["v", 1][:, :, 0:V_ON_GPSIMD])
-        interleave(nc.scalar, staged["v", 1, 0][:, PACK * V_ON_GPSIMD:], gathered["v", 1][:, :, V_ON_GPSIMD:])
+        stage("v", 1, HALF, HALF, "stage_v0_0")
+        interleave(nc.gpsimd, staged["v", 1, HALF][:, 0:PACK * V_ON_GPSIMD],
+                   gathered["v", 1][:, :, HALF:HALF + V_ON_GPSIMD])
+        interleave(nc.scalar, staged["v", 1, HALF][:, PACK * V_ON_GPSIMD:], gathered["v", 1][:, :, HALF + V_ON_GPSIMD:])
         interleave(nc.gpsimd, stage("xm", 0, HALF, HALF, f"stage_v0_{HALF}"), rows["xm", 0, HALF][:])
-        stage("g", 0, 0, HALF)
+        for c in (2, 3, 0, 1):
+            multiply_v(0, c)
         for c in (2, 3, 0):
             form_g(0, c)
-        quantise("xm", 0, 0, HALF)
-        quantise("g", 0, HALF, HALF, E5M2)
+        quantise("xm", 0, 0, HALF, buffer="codes_v0")
+        quantise("g", 0, HALF, HALF, E5M2, "codes_x0")
         for j, buffer in ((0, "plane_v0"), (1, "plane_v1")):
             products[j] = tile([P, B * N], F32, buffer)
         for j in (0, 1):
@@ -247,7 +255,8 @@ def tile_attend_ghv_cau_kernel(tc, xT, wT, vT, y, wt, xm, offs, out):
         for j in (0, 1):
             scatter(nc.scalar, j, HALF, HALF)
         form_g(0, 1)
-        quantise("v", 1)
+        for first in (0, HALF):
+            quantise("v", 1, first, HALF, buffer="stage_xm0_0")
         quantise("g", 0, 0, HALF, E5M2)
         for j in (0, 1):
             last_product(nc.scalar, 0, j, j, 0, HALF)
@@ -256,9 +265,10 @@ def tile_attend_ghv_cau_kernel(tc, xT, wT, vT, y, wt, xm, offs, out):
         for t in (2, LAST):
             factor(nc.vector, 1, t)
         quantise("xm", 0, HALF, HALF)
-        interleave(nc.gpsimd, stage("xm", 1, buffer=f"stage_v0_{HALF}"), rows["xm", 1, 0][:])
+        interleave(nc.gpsimd, stage("xm", 1, buffer="rows_y1"), rows["xm", 1, 0][:])
         stage("g", 1)
         for c in range(N // P):
+            multiply_v(1, c)
             form_g(1, c)
         products[2] = tile([P, B * N], F32, "rows_x1")
         last_product(nc.vector, 0, 2, 2)

@@ -22,7 +22,6 @@ RUN = 4
 BAND = 16
 HALF = N // 2
 BLOCKS = D // P
-V_ON_GPSIMD = 192
 ALIGN = 64
 
 
@@ -108,6 +107,7 @@ def tile_attend_ghv_cau_kernel(tc, xT, wT, vT, y, wt, xm, offs, out):
         def quantise(name, b, first=0, count=N, fmt=E4M3, buffer=None):
             if (name, b) not in codes:
                 codes[name, b] = tile([P, N], U32, buffer or f"codes_{name}{b}")
+            if (name, b) not in scales:
                 scales[name, b] = tile([P, N], U8, f"scales_{name}{b}")
             columns = slice(first, first + count)
             nc.vector.quantize_mx(out=codes[name, b][:, columns].bitcast(fmt), scales=scales[name, b][:, columns],
@@ -183,7 +183,6 @@ def tile_attend_ghv_cau_kernel(tc, xT, wT, vT, y, wt, xm, offs, out):
         load_targets(1, slice(0, 2))
         for t in range(PACK):
             load_plane("v", vT, t)
-        load_targets(1, slice(2, PACK))
 
         for t in range(LAST):
             gather(nc.vector, "w", t, 0)
@@ -191,8 +190,9 @@ def tile_attend_ghv_cau_kernel(tc, xT, wT, vT, y, wt, xm, offs, out):
         gather(nc.vector, "w", LAST, 0, 0, HALF)
         gather(nc.scalar, "w", LAST, 0, HALF, HALF)
         gather(nc.scalar, "w", LAST, 1)
-        for first in (0, HALF):
-            load_rows("xm", xm, 0, f"plane_w{first // HALF}", first, HALF)
+        load_targets(1, slice(2, PACK))
+        load_rows("xm", xm, 0, "plane_w0", 0, HALF)
+        load_rows("xm", xm, 0, "plane_w1", HALF, HALF)
         load_rows("xm", xm, 1, "plane_w2")
         for first in (HALF, 0):
             interleave(nc.vector, stage("w", 0, first, HALF), half(gathered["w", 0], first))
@@ -216,12 +216,11 @@ def tile_attend_ghv_cau_kernel(tc, xT, wT, vT, y, wt, xm, offs, out):
             factor(nc.gpsimd, 0, t)
         for t in range(LAST):
             gather(nc.vector, "v", t, 0)
-        gather(nc.vector, "v", LAST, 0, 0, HALF)
-        gather(nc.scalar, "v", LAST, 0, HALF, HALF)
-        gather(nc.scalar, "v", 2, 1)
-        gather(nc.scalar, "v", LAST, 1)
-        for t in range(2):
-            gather(nc.vector, "v", t, 1)
+        for first in (HALF, 0):
+            gather(nc.vector, "v", LAST, 0, first, HALF)
+        gather(nc.vector, "v", 0, 1)
+        for t in range(1, PACK):
+            gather(nc.scalar, "v", t, 1)
         for t in range(2):
             root(1, t)
             factor(nc.scalar, 1, t)
@@ -229,7 +228,7 @@ def tile_attend_ghv_cau_kernel(tc, xT, wT, vT, y, wt, xm, offs, out):
         stage("xm", 0, 0, HALF)
         staged["g", 0, 0] = factor_tiles[1][:, 2 * N:3 * N].bitcast(BF16)
         staged["g", 0, HALF] = factor_tiles[1][:, 3 * N:].bitcast(BF16)
-        interleave(nc.scalar, stage("v", 1, 0, HALF), half(gathered["v", 1], 0))
+        interleave(nc.scalar, stage("v", 1, 0, P), gathered["v", 1][:, :, 0:P])
         interleave(nc.scalar, staged["xm", 0, 0], rows["xm", 0, 0][:])
         for first in (HALF, 0):
             interleave(nc.vector, stage("v", 0, first, HALF), half(gathered["v", 0], first))
@@ -237,17 +236,14 @@ def tile_attend_ghv_cau_kernel(tc, xT, wT, vT, y, wt, xm, offs, out):
             quantise("v", 0, first, HALF)
         for t in (2, LAST):
             root(1, t)
-        stage("v", 1, HALF, HALF, "stage_v0_0")
-        interleave(nc.gpsimd, staged["v", 1, HALF][:, 0:PACK * V_ON_GPSIMD],
-                   gathered["v", 1][:, :, HALF:HALF + V_ON_GPSIMD])
-        interleave(nc.scalar, staged["v", 1, HALF][:, PACK * V_ON_GPSIMD:], gathered["v", 1][:, :, HALF + V_ON_GPSIMD:])
-        interleave(nc.gpsimd, stage("xm", 0, HALF, HALF, f"stage_v0_{HALF}"), rows["xm", 0, HALF][:])
+        interleave(nc.gpsimd, stage("v", 1, P, N - P, "stage_v0_0"), gathered["v", 1][:, :, P:])
         for c in (2, 3, 0, 1):
             multiply_v(0, c)
         for c in (2, 3, 0):
             form_g(0, c)
         quantise("xm", 0, 0, HALF, buffer="codes_v0")
         quantise("g", 0, HALF, HALF, E5M2, "codes_x0")
+        interleave(nc.scalar, stage("xm", 0, HALF, HALF, "stage_xm0_0"), rows["xm", 0, HALF][:])
         for j, buffer in ((0, "plane_v0"), (1, "plane_v1")):
             products[j] = tile([P, B * N], F32, buffer)
         for j in (0, 1):
@@ -255,8 +251,9 @@ def tile_attend_ghv_cau_kernel(tc, xT, wT, vT, y, wt, xm, offs, out):
         for j in (0, 1):
             scatter(nc.scalar, j, HALF, HALF)
         form_g(0, 1)
-        for first in (0, HALF):
-            quantise("v", 1, first, HALF, buffer="stage_xm0_0")
+        scales["v", 1] = tile([P, N], U8, "scales_v0")
+        quantise("v", 1, P, N - P)
+        quantise("v", 1, 0, P)
         quantise("g", 0, 0, HALF, E5M2)
         for j in (0, 1):
             last_product(nc.scalar, 0, j, j, 0, HALF)

@@ -180,7 +180,7 @@ def tile_attend_ghv_cau_kernel(tc, xT, wT, vT, y, wt, xm, offs, out):
             rows["y", b, 0] = tile([P, PACK, N], F32, f"rows_y{b}")
         load_targets(0, slice(0, 2))
         load_targets(0, slice(2, PACK))
-        load_targets(1, slice(0, 2))
+        load_targets(1, slice(0, LAST))
         for t in range(PACK):
             load_plane("v", vT, t)
 
@@ -190,7 +190,7 @@ def tile_attend_ghv_cau_kernel(tc, xT, wT, vT, y, wt, xm, offs, out):
         gather(nc.vector, "w", LAST, 0, 0, HALF)
         gather(nc.scalar, "w", LAST, 0, HALF, HALF)
         gather(nc.scalar, "w", LAST, 1)
-        load_targets(1, slice(2, PACK))
+        load_targets(1, slice(LAST, PACK))
         load_rows("xm", xm, 0, "plane_w0", 0, HALF)
         load_rows("xm", xm, 0, "plane_w1", HALF, HALF)
         load_rows("xm", xm, 1, "plane_w2")
@@ -218,32 +218,32 @@ def tile_attend_ghv_cau_kernel(tc, xT, wT, vT, y, wt, xm, offs, out):
             gather(nc.vector, "v", t, 0)
         for first in (HALF, 0):
             gather(nc.vector, "v", LAST, 0, first, HALF)
-        gather(nc.vector, "v", 0, 1)
-        for t in range(1, PACK):
-            gather(nc.scalar, "v", t, 1)
         for t in range(2):
             root(1, t)
             factor(nc.scalar, 1, t)
+            gather(nc.vector, "v", t, 1)
+        for t in (2, LAST):
+            gather(nc.scalar, "v", t, 1)
+        root(1, 2)
 
         stage("xm", 0, 0, HALF)
         staged["g", 0, 0] = factor_tiles[1][:, 2 * N:3 * N].bitcast(BF16)
         staged["g", 0, HALF] = factor_tiles[1][:, 3 * N:].bitcast(BF16)
-        interleave(nc.scalar, stage("v", 1, 0, P), gathered["v", 1][:, :, 0:P])
+        interleave(nc.scalar, stage("v", 1, 0, HALF), half(gathered["v", 1], 0))
         interleave(nc.scalar, staged["xm", 0, 0], rows["xm", 0, 0][:])
         for first in (HALF, 0):
             interleave(nc.vector, stage("v", 0, first, HALF), half(gathered["v", 0], first))
         for first in (HALF, 0):
             quantise("v", 0, first, HALF)
-        for t in (2, LAST):
-            root(1, t)
-        interleave(nc.gpsimd, stage("v", 1, P, N - P, "stage_v0_0"), gathered["v", 1][:, :, P:])
+        root(1, LAST)
+        interleave(nc.gpsimd, stage("v", 1, HALF, HALF, "stage_v0_0"), half(gathered["v", 1], HALF))
+        interleave(nc.scalar, stage("xm", 0, HALF, HALF), rows["xm", 0, HALF][:])
         for c in (2, 3, 0, 1):
             multiply_v(0, c)
         for c in (2, 3, 0):
             form_g(0, c)
         quantise("xm", 0, 0, HALF, buffer="codes_v0")
         quantise("g", 0, HALF, HALF, E5M2, "codes_x0")
-        interleave(nc.scalar, stage("xm", 0, HALF, HALF, "stage_xm0_0"), rows["xm", 0, HALF][:])
         for j, buffer in ((0, "plane_v0"), (1, "plane_v1")):
             products[j] = tile([P, B * N], F32, buffer)
         for j in (0, 1):
@@ -252,8 +252,8 @@ def tile_attend_ghv_cau_kernel(tc, xT, wT, vT, y, wt, xm, offs, out):
             scatter(nc.scalar, j, HALF, HALF)
         form_g(0, 1)
         scales["v", 1] = tile([P, N], U8, "scales_v0")
-        quantise("v", 1, P, N - P)
-        quantise("v", 1, 0, P)
+        for first in (0, HALF):
+            quantise("v", 1, first, HALF)
         quantise("g", 0, 0, HALF, E5M2)
         for j in (0, 1):
             last_product(nc.scalar, 0, j, j, 0, HALF)

@@ -22,6 +22,8 @@ RUN = 4
 BAND = 16
 HALF = N // 2
 BLOCKS = D // P
+V_ON_SCALAR = 192
+XM_ON_SCALAR = 64
 ALIGN = 64
 
 
@@ -57,6 +59,7 @@ def tile_attend_ghv_cau_kernel(tc, xT, wT, vT, y, wt, xm, offs, out):
         scales = {}
         products = {}
         av = {}
+        target_tiles = {}
 
         def by_planes(source):
             return source.rearrange("(p t) c -> p t c", t=PACK)
@@ -107,7 +110,6 @@ def tile_attend_ghv_cau_kernel(tc, xT, wT, vT, y, wt, xm, offs, out):
         def quantise(name, b, first=0, count=N, fmt=E4M3, buffer=None):
             if (name, b) not in codes:
                 codes[name, b] = tile([P, N], U32, buffer or f"codes_{name}{b}")
-            if (name, b) not in scales:
                 scales[name, b] = tile([P, N], U8, f"scales_{name}{b}")
             columns = slice(first, first + count)
             nc.vector.quantize_mx(out=codes[name, b][:, columns].bitcast(fmt), scales=scales[name, b][:, columns],
@@ -177,7 +179,8 @@ def tile_attend_ghv_cau_kernel(tc, xT, wT, vT, y, wt, xm, offs, out):
         nc.scalar.dma_start(wt_sb[:], wt.rearrange("b (p t) o -> p b (t o)", t=PACK))
         load_rows("x", xT, 1, "rows_x1")
         for b in range(B):
-            rows["y", b, 0] = tile([P, PACK, N], F32, f"rows_y{b}")
+            target_tiles[b] = tile([P, PACK * N], F32, f"rows_y{b}")
+            rows["y", b, 0] = target_tiles[b][:].rearrange("p (t n) -> p t n", t=PACK)
         load_targets(0, slice(0, 2))
         load_targets(0, slice(2, PACK))
         load_targets(1, slice(0, LAST))
@@ -229,14 +232,17 @@ def tile_attend_ghv_cau_kernel(tc, xT, wT, vT, y, wt, xm, offs, out):
         stage("xm", 0, 0, HALF)
         staged["g", 0, 0] = factor_tiles[1][:, 2 * N:3 * N].bitcast(BF16)
         staged["g", 0, HALF] = factor_tiles[1][:, 3 * N:].bitcast(BF16)
-        interleave(nc.scalar, stage("v", 1, 0, HALF), half(gathered["v", 1], 0))
+        stage("v", 1)
+        interleave(nc.scalar, staged["v", 1, 0][:, 0:PACK * V_ON_SCALAR], gathered["v", 1][:, :, 0:V_ON_SCALAR])
+        stage("v", 0, HALF, HALF)
+        staged["v", 0, 0] = staged["v", 1, 0][:, PACK * HALF:]
         interleave(nc.scalar, staged["xm", 0, 0], rows["xm", 0, 0][:])
         for first in (HALF, 0):
-            interleave(nc.vector, stage("v", 0, first, HALF), half(gathered["v", 0], first))
+            interleave(nc.vector, staged["v", 0, first], half(gathered["v", 0], first))
         for first in (HALF, 0):
             quantise("v", 0, first, HALF)
         root(1, LAST)
-        interleave(nc.gpsimd, stage("v", 1, HALF, HALF, "stage_v0_0"), half(gathered["v", 1], HALF))
+        interleave(nc.gpsimd, staged["v", 1, 0][:, PACK * V_ON_SCALAR:], gathered["v", 1][:, :, V_ON_SCALAR:])
         interleave(nc.scalar, stage("xm", 0, HALF, HALF), rows["xm", 0, HALF][:])
         for c in (2, 3, 0, 1):
             multiply_v(0, c)
@@ -244,6 +250,8 @@ def tile_attend_ghv_cau_kernel(tc, xT, wT, vT, y, wt, xm, offs, out):
             form_g(0, c)
         quantise("xm", 0, 0, HALF, buffer="codes_v0")
         quantise("g", 0, HALF, HALF, E5M2, "codes_x0")
+        staged["xm", 1, 0] = target_tiles[1][:, 2 * N - 2 * XM_ON_SCALAR:PACK * N - 2 * XM_ON_SCALAR].bitcast(BF16)
+        interleave(nc.scalar, staged["xm", 1, 0][:, 0:PACK * XM_ON_SCALAR], rows["xm", 1, 0][:, :, 0:XM_ON_SCALAR])
         for j, buffer in ((0, "plane_v0"), (1, "plane_v1")):
             products[j] = tile([P, B * N], F32, buffer)
         for j in (0, 1):
@@ -251,9 +259,7 @@ def tile_attend_ghv_cau_kernel(tc, xT, wT, vT, y, wt, xm, offs, out):
         for j in (0, 1):
             scatter(nc.scalar, j, HALF, HALF)
         form_g(0, 1)
-        scales["v", 1] = tile([P, N], U8, "scales_v0")
-        for first in (0, HALF):
-            quantise("v", 1, first, HALF)
+        quantise("v", 1)
         quantise("g", 0, 0, HALF, E5M2)
         for j in (0, 1):
             last_product(nc.scalar, 0, j, j, 0, HALF)
@@ -262,13 +268,13 @@ def tile_attend_ghv_cau_kernel(tc, xT, wT, vT, y, wt, xm, offs, out):
         for t in (2, LAST):
             factor(nc.vector, 1, t)
         quantise("xm", 0, HALF, HALF)
-        interleave(nc.gpsimd, stage("xm", 1, buffer="rows_y1"), rows["xm", 1, 0][:])
+        interleave(nc.gpsimd, staged["xm", 1, 0][:, PACK * XM_ON_SCALAR:], rows["xm", 1, 0][:, :, XM_ON_SCALAR:])
         stage("g", 1)
         for c in range(N // P):
             multiply_v(1, c)
             form_g(1, c)
-        products[2] = tile([P, B * N], F32, "rows_x1")
-        last_product(nc.vector, 0, 2, 2)
+        products[2] = tile([P, B * N], F32, "plane_v2")
+        last_product(nc.vector, 0, 2, 5)
         quantise("xm", 1)
         quantise("g", 1, fmt=E5M2)
         scatter(nc.vector, 2, 0, HALF)

@@ -22,9 +22,11 @@ RUN = 4
 BAND = 16
 HALF = N // 2
 BLOCKS = D // P
-V_ON_SCALAR = 192
-XM_ON_SCALAR = 64
 ALIGN = 64
+LONG = 3 * P
+X_ON_SCALAR = 96
+V_ON_SCALAR = 192
+XM_ON_SCALAR = 128
 
 
 def tile_attend_ghv_cau_kernel(tc, xT, wT, vT, y, wt, xm, offs, out):
@@ -54,15 +56,21 @@ def tile_attend_ghv_cau_kernel(tc, xT, wT, vT, y, wt, xm, offs, out):
         rows = {}
         gathered = {(name, b): tile([P, PACK, N], F32, f"gathered_{name}{b}") for name in "wv" for b in range(B)}
         wt_sb = tile([P, B, PACK], F32, "wt_sb")
+        y_tiles = {}
         staged = {}
         codes = {}
         scales = {}
-        products = {}
         av = {}
-        target_tiles = {}
+        products = {}
 
         def by_planes(source):
             return source.rearrange("(p t) c -> p t c", t=PACK)
+
+        def as_planes(flat):
+            return flat[:].rearrange("p (t n) -> p t n", t=PACK)
+
+        def half(planes, first):
+            return planes[:, :, first:first + HALF]
 
         def load_plane(name, table, t):
             table_planes[name, t] = tile([P, T], F32, f"plane_{name}{t}")
@@ -72,8 +80,8 @@ def tile_attend_ghv_cau_kernel(tc, xT, wT, vT, y, wt, xm, offs, out):
             rows[name, b, first] = tile([P, PACK, count], F32, buffer)
             nc.sync.dma_start(rows[name, b, first][:], by_planes(source[b])[:, :, first:first + count])
 
-        def load_targets(b, planes):
-            nc.sync.dma_start(rows["y", b, 0][:, planes, :], by_planes(y[b])[:, planes, :])
+        def load_y(b, planes):
+            nc.sync.dma_start(as_planes(y_tiles[b])[:, planes, :], by_planes(y[b])[:, planes, :])
 
         def move(engine, dst, src):
             if engine is nc.scalar:
@@ -103,7 +111,7 @@ def tile_attend_ghv_cau_kernel(tc, xT, wT, vT, y, wt, xm, offs, out):
             else:
                 move(engine, interleaved_by_runs(dst), by_runs(planes))
 
-        def interleave_x(engine, b, part=slice(0, P)):
+        def interleave_x(engine, b, part):
             move(engine, staged["x", b, 0].rearrange("p (t m j) -> p m j t", t=PACK, j=PACK)[:, part],
                  rows["x", b, 0][:].rearrange("p j (m t) -> p m j t", t=PACK)[:, part])
 
@@ -122,7 +130,7 @@ def tile_attend_ghv_cau_kernel(tc, xT, wT, vT, y, wt, xm, offs, out):
                                 rhs_scale=scales[moving, b][:, columns], start=True, stop=True)
 
         def root(b, t):
-            plane = rows["y", b, 0][:, t, :]
+            plane = as_planes(y_tiles[b])[:, t, :]
             bank = psum.tile([P, N], F32, name=f"bank{PACK * b + t}")
             multiply(bank[:], b, "x", t, "w")
             nc.vector.tensor_tensor(plane, bank[:], plane, ALU.subtract)
@@ -130,32 +138,28 @@ def tile_attend_ghv_cau_kernel(tc, xT, wT, vT, y, wt, xm, offs, out):
             nc.scalar.activation(plane, plane, ACT.Abs_reciprocal_sqrt, bias=one[:])
 
         def factor(engine, b, t):
-            plane = rows["y", b, 0][:, t, :]
+            roots, result = as_planes(y_tiles[b]), as_planes(factors[b])
             weight = wt_sb[:, b, t:t + 1]
             if engine is nc.vector:
-                nc.vector.scalar_tensor_tensor(factors[b][:, t, :], plane, weight, plane, ALU.mult, ALU.mult)
+                nc.vector.scalar_tensor_tensor(result[:, t, :], roots[:, t, :], weight, roots[:, t, :], ALU.mult, ALU.mult)
             elif engine is nc.scalar:
-                nc.scalar.activation(plane, plane, ACT.Square)
-                nc.gpsimd.tensor_scalar(factors[b][:, t, :], plane, weight, 0.0, ALU.mult, ALU.add)
+                nc.scalar.activation(roots[:, t, :], roots[:, t, :], ACT.Square)
+                nc.gpsimd.tensor_scalar(result[:, t, :], roots[:, t, :], weight, 0.0, ALU.mult, ALU.add)
             else:
-                nc.gpsimd.tensor_scalar(factors[b][:, t, :], plane, weight, 0.0, ALU.mult, ALU.add)
+                nc.gpsimd.tensor_scalar(result[:, t, :], roots[:, t, :], weight, 0.0, ALU.mult, ALU.add)
                 if t % 2 == 1:
                     pair = slice(t - 1, t + 1)
-                    nc.gpsimd.tensor_tensor(factors[b][:, pair, :], factors[b][:, pair, :], rows["y", b, 0][:, pair, :],
-                                            ALU.mult)
+                    nc.gpsimd.tensor_tensor(result[:, pair, :], result[:, pair, :], roots[:, pair, :], ALU.mult)
 
         def multiply_v(b, c):
             av[b, c] = psum.tile([P, PACK, P], F32, name=f"bank{PACK * b + c}")
             for t in range(PACK):
                 multiply(av[b, c][:, t, :], b, "x", t, "v", slice(c * P, (c + 1) * P))
 
-        def form_g(b, c):
-            first = max(start for name, group, start in staged if (name, group) == ("g", b) and start <= c * P)
-            bank = av[b, c]
-            items = slice(c * P, (c + 1) * P)
+        def form_g(b, c, first):
             words = staged["g", b, first][:, PACK * (c * P - first):PACK * ((c + 1) * P - first)]
-            nc.vector.tensor_tensor(interleaved_by_runs(words), by_runs(bank[:]), by_runs(factors[b][:, :, items]),
-                                    ALU.mult)
+            nc.vector.tensor_tensor(interleaved_by_runs(words), by_runs(av[b, c][:]),
+                                    by_runs(as_planes(factors[b])[:, :, c * P:(c + 1) * P]), ALU.mult)
 
         def last_product(engine, b, j, bank_number, first=0, count=N):
             bank = psum.tile([P, count], F32, name=f"bank{bank_number}")
@@ -168,9 +172,6 @@ def tile_attend_ghv_cau_kernel(tc, xT, wT, vT, y, wt, xm, offs, out):
         def store(j):
             nc.sync.dma_start(out[j * P:(j + 1) * P, :], windows[j][:])
 
-        def half(planes, first):
-            return planes[:, :, first:first + HALF]
-
         for t in range(PACK):
             load_plane("w", wT, t)
             if t == 0:
@@ -179,11 +180,10 @@ def tile_attend_ghv_cau_kernel(tc, xT, wT, vT, y, wt, xm, offs, out):
         nc.scalar.dma_start(wt_sb[:], wt.rearrange("b (p t) o -> p b (t o)", t=PACK))
         load_rows("x", xT, 1, "rows_x1")
         for b in range(B):
-            target_tiles[b] = tile([P, PACK * N], F32, f"rows_y{b}")
-            rows["y", b, 0] = target_tiles[b][:].rearrange("p (t n) -> p t n", t=PACK)
-        load_targets(0, slice(0, 2))
-        load_targets(0, slice(2, PACK))
-        load_targets(1, slice(0, LAST))
+            y_tiles[b] = tile([P, PACK * N], F32, f"rows_y{b}")
+        load_y(0, slice(0, 2))
+        load_y(0, slice(2, PACK))
+        load_y(1, slice(0, LAST))
         for t in range(PACK):
             load_plane("v", vT, t)
 
@@ -193,10 +193,13 @@ def tile_attend_ghv_cau_kernel(tc, xT, wT, vT, y, wt, xm, offs, out):
         gather(nc.vector, "w", LAST, 0, 0, HALF)
         gather(nc.scalar, "w", LAST, 0, HALF, HALF)
         gather(nc.scalar, "w", LAST, 1)
-        load_targets(1, slice(LAST, PACK))
+
+        load_y(1, slice(LAST, PACK))
         load_rows("xm", xm, 0, "plane_w0", 0, HALF)
+        load_rows("xm", xm, 1, "plane_w3", 0, XM_ON_SCALAR)
         load_rows("xm", xm, 0, "plane_w1", HALF, HALF)
-        load_rows("xm", xm, 1, "plane_w2")
+        load_rows("xm", xm, 1, "plane_w2", XM_ON_SCALAR, D - XM_ON_SCALAR)
+
         for first in (HALF, 0):
             interleave(nc.vector, stage("w", 0, first, HALF), half(gathered["w", 0], first))
         for first in (HALF, 0):
@@ -207,12 +210,13 @@ def tile_attend_ghv_cau_kernel(tc, xT, wT, vT, y, wt, xm, offs, out):
         quantise("x", 0)
         interleave(nc.vector, stage("w", 1, buffer="stage_x0_0"), gathered["w", 1][:])
         stage("x", 1)
-        interleave_x(nc.scalar, 1)
+        interleave_x(nc.scalar, 1, slice(0, X_ON_SCALAR))
         root(0, 0)
+        interleave_x(nc.vector, 1, slice(X_ON_SCALAR, P))
         quantise("w", 1)
         quantise("x", 1)
-        factor_tiles = [tile([P, PACK * N], F32, f"rows_x{b}") for b in range(B)]
-        factors = [factor_tile[:].rearrange("p (t n) -> p t n", t=PACK) for factor_tile in factor_tiles]
+
+        factors = [tile([P, PACK * N], F32, f"rows_x{b}") for b in range(B)]
         for t in range(PACK):
             if t > 0:
                 root(0, t)
@@ -230,8 +234,8 @@ def tile_attend_ghv_cau_kernel(tc, xT, wT, vT, y, wt, xm, offs, out):
         root(1, 2)
 
         stage("xm", 0, 0, HALF)
-        staged["g", 0, 0] = factor_tiles[1][:, 2 * N:3 * N].bitcast(BF16)
-        staged["g", 0, HALF] = factor_tiles[1][:, 3 * N:].bitcast(BF16)
+        staged["g", 0, 0] = factors[1][:, 2 * N:LAST * N].bitcast(BF16)
+        staged["g", 0, HALF] = factors[1][:, LAST * N:].bitcast(BF16)
         stage("v", 1)
         interleave(nc.scalar, staged["v", 1, 0][:, 0:PACK * V_ON_SCALAR], gathered["v", 1][:, :, 0:V_ON_SCALAR])
         stage("v", 0, HALF, HALF)
@@ -246,19 +250,22 @@ def tile_attend_ghv_cau_kernel(tc, xT, wT, vT, y, wt, xm, offs, out):
         interleave(nc.scalar, stage("xm", 0, HALF, HALF), rows["xm", 0, HALF][:])
         for c in (2, 3, 0, 1):
             multiply_v(0, c)
-        for c in (2, 3, 0):
-            form_g(0, c)
+        for c in (2, 3):
+            form_g(0, c, HALF)
+        form_g(0, 0, 0)
         quantise("xm", 0, 0, HALF, buffer="codes_v0")
         quantise("g", 0, HALF, HALF, E5M2, "codes_x0")
-        staged["xm", 1, 0] = target_tiles[1][:, 2 * N - 2 * XM_ON_SCALAR:PACK * N - 2 * XM_ON_SCALAR].bitcast(BF16)
-        interleave(nc.scalar, staged["xm", 1, 0][:, 0:PACK * XM_ON_SCALAR], rows["xm", 1, 0][:, :, 0:XM_ON_SCALAR])
-        for j, buffer in ((0, "plane_v0"), (1, "plane_v1")):
-            products[j] = tile([P, B * N], F32, buffer)
+        start = 2 * N - 2 * XM_ON_SCALAR
+        staged["xm", 1, 0] = y_tiles[1][:, start:start + 2 * D].bitcast(BF16)
+        interleave(nc.scalar, staged["xm", 1, 0][:, 0:PACK * XM_ON_SCALAR], rows["xm", 1, 0][:])
+
+        for j in (0, 1):
+            products[j] = tile([P, B * N], F32, f"plane_v{j}")
         for j in (0, 1):
             last_product(nc.scalar, 0, j, 2 + j, HALF, HALF)
         for j in (0, 1):
             scatter(nc.scalar, j, HALF, HALF)
-        form_g(0, 1)
+        form_g(0, 1, 0)
         quantise("v", 1)
         quantise("g", 0, 0, HALF, E5M2)
         for j in (0, 1):
@@ -268,30 +275,31 @@ def tile_attend_ghv_cau_kernel(tc, xT, wT, vT, y, wt, xm, offs, out):
         for t in (2, LAST):
             factor(nc.vector, 1, t)
         quantise("xm", 0, HALF, HALF)
-        interleave(nc.gpsimd, staged["xm", 1, 0][:, PACK * XM_ON_SCALAR:], rows["xm", 1, 0][:, :, XM_ON_SCALAR:])
+        interleave(nc.gpsimd, staged["xm", 1, 0][:, PACK * XM_ON_SCALAR:], rows["xm", 1, XM_ON_SCALAR][:])
         stage("g", 1)
         for c in range(N // P):
             multiply_v(1, c)
-            form_g(1, c)
+            form_g(1, c, 0)
         products[2] = tile([P, B * N], F32, "plane_v2")
         last_product(nc.vector, 0, 2, 5)
         quantise("xm", 1)
         quantise("g", 1, fmt=E5M2)
+
         scatter(nc.vector, 2, 0, HALF)
-        products[LAST] = tile([P, B * N], F32, "stage_g1_0")
-        last_product(nc.scalar, 0, LAST, 3)
+        products[3] = tile([P, B * N], F32, "stage_g1_0")
+        last_product(nc.scalar, 0, 3, 3)
         last_product(nc.scalar, 1, 0, 5)
         last_product(nc.vector, 1, 1, 4)
-        scatter(nc.scalar, LAST, 0, HALF)
+        scatter(nc.scalar, 3, 0, HALF)
         last_product(nc.vector, 1, 2, 6)
         scatter(nc.vector, 1, N, N)
         store(1)
         scatter(nc.scalar, 0, N, HALF)
-        last_product(nc.scalar, 1, LAST, 5)
+        last_product(nc.scalar, 1, 3, 5)
         scatter(nc.scalar, 0, N + HALF, HALF)
         store(0)
         scatter(nc.vector, 2, HALF, N + HALF)
         store(2)
-        for first in (HALF, HALF + 3 * P):
-            scatter(nc.scalar, LAST, first, 3 * P)
-        store(LAST)
+        for first in (HALF, HALF + LONG):
+            scatter(nc.scalar, 3, first, LONG)
+        store(3)

@@ -24,6 +24,7 @@ HALF = N // 2
 BLOCKS = D // P
 ALIGN = 64
 LONG = 3 * P
+W_ON_SCALAR = 128
 X_ON_SCALAR = 96
 V_ON_SCALAR = 192
 XM_ON_SCALAR = 128
@@ -208,7 +209,9 @@ def tile_attend_ghv_cau_kernel(tc, xT, wT, vT, y, wt, xm, offs, out):
         interleave_x(nc.scalar, 0, slice(0, P // 2))
         interleave_x(nc.vector, 0, slice(P // 2, P))
         quantise("x", 0)
-        interleave(nc.vector, stage("w", 1, buffer="stage_x0_0"), gathered["w", 1][:])
+        staged["w", 1, 0] = rows["x", 0, 0][:].rearrange("p t c -> p (t c)")[:, 0:2 * N].bitcast(BF16)
+        interleave(nc.scalar, staged["w", 1, 0][:, 0:PACK * W_ON_SCALAR], gathered["w", 1][:, :, 0:W_ON_SCALAR])
+        interleave(nc.vector, staged["w", 1, 0][:, PACK * W_ON_SCALAR:], gathered["w", 1][:, :, W_ON_SCALAR:])
         stage("x", 1)
         interleave_x(nc.scalar, 1, slice(0, X_ON_SCALAR))
         root(0, 0)

from contextlib import ExitStack

import concourse.mybir as mybir

B, N, T, D, R = 2, 512, 2048, 512, 512
FLOPS = 3 * 2 * B * N * D * R

F32 = mybir.dt.float32
BF16 = mybir.dt.bfloat16
U32 = mybir.dt.uint32
U16 = mybir.dt.uint16
U8 = mybir.dt.uint8
E4M3 = mybir.dt.float8_e4m3fn_x4
E5M2 = mybir.dt.float8_e5m2_x4
ACT = mybir.ActivationFunctionType
ALU = mybir.AluOpType

P = 128
PACK = 4
LAST = PACK - 1
RUN = 4
BAND = 16
HALF = N // 2
BLOCKS = D // P
ALIGN = 64
LONG = 3 * P
W_ON_SCALAR = 128
X_ON_SCALAR = 96
V_ON_SCALAR = 192
XM_ON_SCALAR = 128


def tile_attend_ghv_cau_kernel(tc, xT, wT, vT, y, wt, xm, offs, out):
    nc = tc.nc
    with ExitStack() as ctx:
        lists = ctx.enter_context(tc.tile_pool(name="lists", bufs=1))
        sbuf = ctx.enter_context(tc.tile_pool(name="sbuf", bufs=1))
        psum = ctx.enter_context(tc.psum_pool(name="psum", bufs=1))

        offsets = lists.tile([P, B * N // BAND], U16, name="offsets")

        def list_part(first, count):
            return offsets[:, first // BAND:(first + count) // BAND]

        def tile(shape, dtype, name):
            return sbuf.tile(shape, dtype, name=name, align_bytes=ALIGN)

        one = tile([P, 1], F32, "one")
        nc.vector.memset(one[:], 1.0)
        nc.scalar.activation(one[:], one[:], ACT.Abs_reciprocal_sqrt)

        windows = [tile([P, T], F32, f"window{j}") for j in range(BLOCKS)]
        for window in windows:
            nc.gpsimd.memset(window[:], 0.0)

        table_planes = {}
        rows = {}
        gathered = {(name, b): tile([P, PACK, N], F32, f"gathered_{name}{b}") for name in "wv" for b in range(B)}
        wt_sb = tile([P, B, PACK], F32, "wt_sb")
        y_tiles = {}
        staged = {}
        codes = {}
        scales = {}
        av = {}
        products = {}

        def by_planes(source):
            return source.rearrange("(p t) c -> p t c", t=PACK)

        def as_planes(flat):
            return flat[:].rearrange("p (t n) -> p t n", t=PACK)

        def half(planes, first):
            return planes[:, :, first:first + HALF]

        def load_plane(name, table, t):
            table_planes[name, t] = tile([P, T], F32, f"plane_{name}{t}")
            nc.sync.dma_start(table_planes[name, t][:], by_planes(table)[:, t, :])

        def load_rows(name, source, b, buffer, first=0, count=N):
            rows[name, b, first] = tile([P, PACK, count], F32, buffer)
            nc.sync.dma_start(rows[name, b, first][:], by_planes(source[b])[:, :, first:first + count])

        def load_y(b, planes):
            nc.sync.dma_start(as_planes(y_tiles[b])[:, planes, :], by_planes(y[b])[:, planes, :])

        def move(engine, dst, src):
            if engine is nc.scalar:
                nc.scalar.activation(dst, src, ACT.Copy)
            elif engine is nc.gpsimd:
                nc.gpsimd.tensor_scalar(dst, src, 1.0, 0.0, ALU.mult, ALU.add)
            else:
                nc.vector.tensor_copy(dst, src)

        def gather(engine, name, t, b, first=0, count=N):
            move(engine, gathered[name, b][:, t, first:first + count],
                 table_planes[name, t][:].indirect(list_part(b * N + first, count)))

        def by_runs(planes):
            return planes.rearrange("p t (c i) -> p c t i", i=RUN)

        def interleaved_by_runs(words):
            return words.rearrange("p (c i t) -> p c t i", i=RUN, t=PACK)

        def stage(name, b, first=0, count=N, buffer=None):
            staged[name, b, first] = tile([P, PACK * count], BF16, buffer or f"stage_{name}{b}_{first}")[:]
            return staged[name, b, first]

        def interleave(engine, dst, planes):
            if engine is nc.gpsimd:
                move(engine, dst.rearrange("p (c t) -> p c t", t=PACK), planes.rearrange("p t c -> p c t"))
            else:
                move(engine, interleaved_by_runs(dst), by_runs(planes))

        def interleave_x(engine, b, part):
            move(engine, staged["x", b, 0].rearrange("p (t m j) -> p m j t", t=PACK, j=PACK)[:, part],
                 rows["x", b, 0][:].rearrange("p j (m t) -> p m j t", t=PACK)[:, part])

        def quantise(name, b, first=0, count=N, fmt=E4M3, buffer=None):
            if (name, b) not in codes:
                codes[name, b] = tile([P, N], U32, buffer or f"codes_{name}{b}")
                scales[name, b] = tile([P, N], U8, f"scales_{name}{b}")
            columns = slice(first, first + count)
            nc.vector.quantize_mx(out=codes[name, b][:, columns].bitcast(fmt), scales=scales[name, b][:, columns],
                                  in_=staged[name, b, first])

        def multiply(result, b, stationary, block, moving, columns=slice(0, N), fmt=E4M3):
            held = slice(block * P, (block + 1) * P)
            nc.tensor.matmul_mx(out=result, lhsT=codes[stationary, b][:, held].bitcast(E4M3),
                                lhsT_scale=scales[stationary, b][:, held], rhs=codes[moving, b][:, columns].bitcast(fmt),
                                rhs_scale=scales[moving, b][:, columns], start=True, stop=True)

        def root(b, t):
            plane = as_planes(y_tiles[b])[:, t, :]
            bank = psum.tile([P, N], F32, name=f"bank{PACK * b + t}")
            multiply(bank[:], b, "x", t, "w")
            nc.vector.tensor_tensor(plane, bank[:], plane, ALU.subtract)
            nc.scalar.activation(plane, plane, ACT.Square)
            nc.scalar.activation(plane, plane, ACT.Abs_reciprocal_sqrt, bias=one[:])

        def factor(engine, b, t):
            roots, result = as_planes(y_tiles[b]), as_planes(factors[b])
            weight = wt_sb[:, b, t:t + 1]
            if engine is nc.vector:
                nc.vector.scalar_tensor_tensor(result[:, t, :], roots[:, t, :], weight, roots[:, t, :], ALU.mult, ALU.mult)
            elif engine is nc.scalar:
                nc.scalar.activation(roots[:, t, :], roots[:, t, :], ACT.Square)
                nc.gpsimd.tensor_scalar(result[:, t, :], roots[:, t, :], weight, 0.0, ALU.mult, ALU.add)
            else:
                nc.gpsimd.tensor_scalar(result[:, t, :], roots[:, t, :], weight, 0.0, ALU.mult, ALU.add)
                if t % 2 == 1:
                    pair = slice(t - 1, t + 1)
                    nc.gpsimd.tensor_tensor(result[:, pair, :], result[:, pair, :], roots[:, pair, :], ALU.mult)

        def multiply_v(b, c):
            av[b, c] = psum.tile([P, PACK, P], F32, name=f"bank{PACK * b + c}")
            for t in range(PACK):
                multiply(av[b, c][:, t, :], b, "x", t, "v", slice(c * P, (c + 1) * P))

        def form_g(b, c, first):
            words = staged["g", b, first][:, PACK * (c * P - first):PACK * ((c + 1) * P - first)]
            nc.vector.tensor_tensor(interleaved_by_runs(words), by_runs(av[b, c][:]),
                                    by_runs(as_planes(factors[b])[:, :, c * P:(c + 1) * P]), ALU.mult)

        def last_product(engine, b, j, bank_number, first=0, count=N):
            bank = psum.tile([P, count], F32, name=f"bank{bank_number}")
            multiply(bank[:], b, "xm", j, "g", slice(first, first + count), E5M2)
            move(engine, products[j][:, b * N + first:b * N + first + count], bank[:])

        def scatter(engine, j, first, count):
            move(engine, windows[j][:].indirect(list_part(first, count)), products[j][:, first:first + count])

        def store(j):
            nc.sync.dma_start(out[j * P:(j + 1) * P, :], windows[j][:])

        for t in range(PACK):
            load_plane("w", wT, t)
            if t == 0:
                nc.sync.dma_start(offsets[:], offs)
        load_rows("x", xT, 0, "rows_x0")
        nc.scalar.dma_start(wt_sb[:], wt.rearrange("b (p t) o -> p b (t o)", t=PACK))
        load_rows("x", xT, 1, "rows_x1")
        for b in range(B):
            y_tiles[b] = tile([P, PACK * N], F32, f"rows_y{b}")
        load_y(0, slice(0, 2))
        load_y(0, slice(2, PACK))
        load_y(1, slice(0, LAST))
        for t in range(PACK):
            load_plane("v", vT, t)

        for t in range(LAST):
            gather(nc.vector, "w", t, 0)
            gather(nc.scalar, "w", t, 1)
        gather(nc.vector, "w", LAST, 0, 0, HALF)
        gather(nc.scalar, "w", LAST, 0, HALF, HALF)
        gather(nc.scalar, "w", LAST, 1)

        load_y(1, slice(LAST, PACK))
        load_rows("xm", xm, 0, "plane_w0", 0, HALF)
        load_rows("xm", xm, 1, "plane_w3", 0, XM_ON_SCALAR)
        load_rows("xm", xm, 0, "plane_w1", HALF, HALF)
        load_rows("xm", xm, 1, "plane_w2", XM_ON_SCALAR, D - XM_ON_SCALAR)

        for first in (HALF, 0):
            interleave(nc.vector, stage("w", 0, first, HALF), half(gathered["w", 0], first))
        for first in (HALF, 0):
            quantise("w", 0, first, HALF)
        stage("x", 0)
        interleave_x(nc.scalar, 0, slice(0, P // 2))
        interleave_x(nc.vector, 0, slice(P // 2, P))
        quantise("x", 0)
        staged["w", 1, 0] = rows["x", 0, 0][:].rearrange("p t c -> p (t c)")[:, 0:2 * N].bitcast(BF16)
        interleave(nc.scalar, staged["w", 1, 0][:, 0:PACK * W_ON_SCALAR], gathered["w", 1][:, :, 0:W_ON_SCALAR])
        interleave(nc.vector, staged["w", 1, 0][:, PACK * W_ON_SCALAR:], gathered["w", 1][:, :, W_ON_SCALAR:])
        stage("x", 1)
        interleave_x(nc.scalar, 1, slice(0, X_ON_SCALAR))
        root(0, 0)
        interleave_x(nc.vector, 1, slice(X_ON_SCALAR, P))
        quantise("w", 1)
        quantise("x", 1)

        factors = [tile([P, PACK * N], F32, f"rows_x{b}") for b in range(B)]
        for t in range(PACK):
            if t > 0:
                root(0, t)
            factor(nc.gpsimd, 0, t)
        for t in range(LAST):
            gather(nc.vector, "v", t, 0)
        for first in (HALF, 0):
            gather(nc.vector, "v", LAST, 0, first, HALF)
        for t in range(2):
            root(1, t)
            factor(nc.scalar, 1, t)
            gather(nc.vector, "v", t, 1)
        for t in (2, LAST):
            gather(nc.scalar, "v", t, 1)
        root(1, 2)

        stage("xm", 0, 0, HALF)
        staged["g", 0, 0] = factors[1][:, 2 * N:LAST * N].bitcast(BF16)
        staged["g", 0, HALF] = factors[1][:, LAST * N:].bitcast(BF16)
        stage("v", 1)
        interleave(nc.scalar, staged["v", 1, 0][:, 0:PACK * V_ON_SCALAR], gathered["v", 1][:, :, 0:V_ON_SCALAR])
        stage("v", 0, HALF, HALF)
        staged["v", 0, 0] = staged["v", 1, 0][:, PACK * HALF:]
        interleave(nc.scalar, staged["xm", 0, 0], rows["xm", 0, 0][:])
        for first in (HALF, 0):
            interleave(nc.vector, staged["v", 0, first], half(gathered["v", 0], first))
        for first in (HALF, 0):
            quantise("v", 0, first, HALF)
        root(1, LAST)
        interleave(nc.gpsimd, staged["v", 1, 0][:, PACK * V_ON_SCALAR:], gathered["v", 1][:, :, V_ON_SCALAR:])
        interleave(nc.scalar, stage("xm", 0, HALF, HALF), rows["xm", 0, HALF][:])
        for c in (2, 3, 0, 1):
            multiply_v(0, c)
        for c in (2, 3):
            form_g(0, c, HALF)
        form_g(0, 0, 0)
        quantise("xm", 0, 0, HALF, buffer="codes_v0")
        quantise("g", 0, HALF, HALF, E5M2, "codes_x0")
        start = 2 * N - 2 * XM_ON_SCALAR
        staged["xm", 1, 0] = y_tiles[1][:, start:start + 2 * D].bitcast(BF16)
        interleave(nc.scalar, staged["xm", 1, 0][:, 0:PACK * XM_ON_SCALAR], rows["xm", 1, 0][:])

        for j in (0, 1):
            products[j] = tile([P, B * N], F32, f"plane_v{j}")
        for j in (0, 1):
            last_product(nc.scalar, 0, j, 2 + j, HALF, HALF)
        for j in (0, 1):
            scatter(nc.scalar, j, HALF, HALF)
        form_g(0, 1, 0)
        quantise("v", 1)
        quantise("g", 0, 0, HALF, E5M2)
        for j in (0, 1):
            last_product(nc.scalar, 0, j, j, 0, HALF)
        for j in (0, 1):
            scatter(nc.scalar, j, 0, HALF)
        for t in (2, LAST):
            factor(nc.vector, 1, t)
        quantise("xm", 0, HALF, HALF)
        interleave(nc.gpsimd, staged["xm", 1, 0][:, PACK * XM_ON_SCALAR:], rows["xm", 1, XM_ON_SCALAR][:])
        stage("g", 1)
        for c in range(N // P):
            multiply_v(1, c)
            form_g(1, c, 0)
        products[2] = tile([P, B * N], F32, "plane_v2")
        last_product(nc.vector, 0, 2, 5)
        quantise("xm", 1)
        quantise("g", 1, fmt=E5M2)

        scatter(nc.vector, 2, 0, HALF)
        products[3] = tile([P, B * N], F32, "stage_g1_0")
        last_product(nc.scalar, 0, 3, 3)
        last_product(nc.scalar, 1, 0, 5)
        last_product(nc.vector, 1, 1, 4)
        scatter(nc.scalar, 3, 0, HALF)
        last_product(nc.vector, 1, 2, 6)
        scatter(nc.vector, 1, N, N)
        store(1)
        scatter(nc.scalar, 0, N, HALF)
        last_product(nc.scalar, 1, 3, 5)
        scatter(nc.scalar, 0, N + HALF, HALF)
        store(0)
        scatter(nc.vector, 2, HALF, N + HALF)
        store(2)
        for first in (HALF, HALF + LONG):
            scatter(nc.scalar, 3, first, LONG)
        store(3)
